import numpy as np
import ml_dtypes


def mxq(x, axis, fmt="e4m3"):
    dtype, down = {"e4m3": (ml_dtypes.float8_e4m3fn, 7), "e5m2": (ml_dtypes.float8_e5m2, 14)}[fmt]
    v = np.moveaxis(np.asarray(x, np.float32).astype(ml_dtypes.bfloat16).astype(np.float64), axis, -1)
    blocks = v.reshape(v.shape[:-1] + (-1, 32))
    amax = np.abs(blocks).max(-1, keepdims=True)
    byte = np.maximum(np.where(amax > 0, np.frexp(amax)[1] - 1 + 127, 0) - down, 1)
    scale = np.exp2(byte - 127.0)
    codes = (blocks / scale).astype(np.float32).astype(dtype).astype(np.float64)
    return np.moveaxis((codes * scale).reshape(v.shape), -1, axis)


WIDE = False


def mx_kscale(k):
    if not WIDE:
        return np.ones(k)
    levels = np.array([10, -10, 5, -5, 0])
    if k % 512:
        return np.exp2(np.random.permutation(np.resize(levels, k // 32))).repeat(32)
    a = np.empty((k // 512, 16))
    for p in range(k // 512):
        a[p, :8] = np.random.permutation(np.resize(levels, 8))
        for g in range(8):
            far = levels[np.abs(levels - a[p, g]) >= 10]
            a[p, g + 8] = far[np.random.randint(len(far))]
    return np.exp2(a.ravel()).repeat(32)


def f64(x):
    return np.asarray(x).astype(np.float64)


def striped(idx):
    return np.tile(idx.reshape(-1, 16).T, (8, 1)).astype(np.uint16)


def unstriped(offs):
    return offs[:16].T.reshape(-1).astype(np.int64)


E2M1 = np.array([0.0, 0.5, 1.0, 1.5, 2.0, 3.0, 4.0, 6.0, -0.0, -0.5, -1.0, -1.5, -2.0, -3.0, -4.0, -6.0])


def pack_weight(w, fmt):
    k, n = w.shape
    w = f64(np.asarray(w, np.float32).astype(ml_dtypes.bfloat16)).reshape(k // 32, 32, n)
    amax = np.abs(w).max(1)
    if fmt == "e4m3":
        byte = np.frexp(amax)[1] - 1 + 127 - 7
    else:
        mant, ex = np.frexp(amax / 6.0)
        byte = np.where(mant > 0.5, ex, ex - 1) + 127
    byte = np.clip(np.where(amax > 0, byte, 1), 1, 254)
    scaled = (w * np.exp2(127.0 - byte)[:, None, :]).reshape(k, n).astype(np.float32)
    by_word = np.ascontiguousarray(scaled.reshape(k // 512, 128, 4, n).transpose(0, 1, 3, 2))
    if fmt == "e4m3":
        words = by_word.astype(ml_dtypes.float8_e4m3fn).view(np.uint8)
    else:
        c = by_word.astype(ml_dtypes.float4_e2m1fn).view(np.uint8) & 0xF
        words = (c[..., 0::2] | (c[..., 1::2] << 4)).reshape(k // 512, 128, 2 * n)
    return np.ascontiguousarray(words), np.ascontiguousarray(byte.astype(np.uint8).reshape(k // 512, 16, n))


def unpack_weight(words, scales, fmt):
    g, _, n = scales.shape
    words = np.ascontiguousarray(words).reshape(g, 128, n, -1)
    if fmt == "e4m3":
        vals = words.view(ml_dtypes.float8_e4m3fn).astype(np.float64)
    else:
        nib = np.empty((g, 128, n, 4), np.uint8)
        nib[..., 0::2] = words & 0xF
        nib[..., 1::2] = words >> 4
        vals = E2M1[nib]
    vals = vals * np.repeat(np.exp2(scales.astype(np.float64) - 127.0), 8, axis=1)[..., None]
    return vals.transpose(0, 1, 3, 2).reshape(g * 512, n)


def gelu(v):
    return 0.5 * v * (1.0 + np.tanh(np.sqrt(2.0 / np.pi) * (v + 0.044715 * v**3)))


def striped8(idx):
    return np.concatenate([v.reshape(-1, 16).T for v in idx]).astype(np.uint16)


def unstriped8(offs):
    return np.stack([offs[16 * g:16 * g + 16].T.reshape(-1) for g in range(8)]).astype(np.int64)


def heads(xT, wgt, idx8):
    k = np.arange(xT.shape[0])
    return wgt[k // 4 % 128] * xT[k[:, None], idx8[k % 512 // 64]]


K, C, H, N, T, D, S, G, L = 512, 1024, 1024, 256, 2048, 2048, 1024, 8, 16

def setup_inputs():
    n = np.random.standard_normal
    s = mx_kscale(K)[:, None]
    sx = mx_kscale(C)[:, None]
    u = mx_kscale(H)[:, None]
    tab_words, tab_scales = pack_weight(n((K, T)) * s, "e4m3")
    wk_words, wk_scales = pack_weight(0.8 * n((K, H)) / np.sqrt(K) / s, "e2m1")
    return {
        "tab_words": tab_words, "tab_scales": tab_scales,
        "offs": striped(np.random.permutation(T)[:S]),
        "xT": (n((C, D)) * sx).astype(np.float32),
        "wgt": np.repeat(np.random.uniform(0.5, 2.0, (G, S)), L, axis=0).astype(np.float32),
        "offs2": striped8(np.stack([np.random.permutation(D)[:S] for _ in range(G)])),
        "wx": (0.6 * n((C, H)) / np.sqrt(C) / sx).astype(np.float32),
        "wk_words": wk_words, "wk_scales": wk_scales,
        "sel": (np.exp(0.3 * n(H)) * u[:, 0]).astype(np.float32),
        "wo": (n((H, N)) / np.sqrt(H) / u).astype(np.float32),
        "bo": (0.5 * n(N)).astype(np.float32),
    }

def reference(tab_words, tab_scales, offs, xT, wgt, offs2, wx, wk_words, wk_scales, sel, wo, bo):
    v = unpack_weight(tab_words, tab_scales, "e4m3")[:, unstriped(offs)]
    xg = heads(f64(xT), f64(wgt), unstriped8(offs2))
    xq = mxq(xg, 0, "e4m3")
    wxq = mxq(f64(wx), 0, "e4m3")
    wk = unpack_weight(wk_words, wk_scales, "e2m1")
    a = wxq.T @ xq + wk.T @ v
    e = np.exp(a)
    h = f64(sel)[:, None] * np.log(1.0 + e)
    hq = mxq(h, 0, "e4m3")
    woq = mxq(f64(wo), 0, "e4m3")
    y = woq.T @ hq
    return y + f64(bo)[:, None]

@@ -1,0 +1,301 @@
+from contextlib import ExitStack
+
+import concourse.mybir as mybir
+
+K, C, H, N, T, D, S = 512, 1024, 1024, 256, 2048, 2048, 1024
+FLOPS = 2 * S * (C * H + K * H + H * N)
+
+F32 = mybir.dt.float32
+BF16 = mybir.dt.bfloat16
+I32 = mybir.dt.int32
+U32 = mybir.dt.uint32
+U16 = mybir.dt.uint16
+U8 = mybir.dt.uint8
+E4M3 = mybir.dt.float8_e4m3fn_x4
+E2M1 = mybir.dt.float4_e2m1fn_x4
+MULT = mybir.AluOpType.mult
+ACT = mybir.ActivationFunctionType
+
+P = 128
+PACK = 4
+KP = P * PACK
+HALF = S // 2
+QUART = S // 4
+
+
+def tile_list_predicate_join_cardinality_kernel(
+    tc, tab_words, tab_scales, offs, xT, wgt, offs2, wx, wk_words, wk_scales, sel, wo, bo, out
+):
+    nc = tc.nc
+    with ExitStack() as ctx:
+        keep = ctx.enter_context(tc.tile_pool(name="keep", bufs=1))
+        big = ctx.enter_context(tc.tile_pool(name="big", bufs=8))
+        late = ctx.enter_context(tc.tile_pool(name="late", bufs=3))
+        ring = ctx.enter_context(tc.tile_pool(name="ring", bufs=2))
+        psum = ctx.enter_context(tc.psum_pool(name="psum", bufs=8))
+
+        def held(shape, dtype, name):
+            return keep.tile(shape, dtype, name=name, align_bytes=64)
+
+        offs2_t = keep.tile([P, S // 16], U16, name="offs2_t")
+        offs_t = keep.tile([P, S // 16], U16, name="offs_t")
+        wk_raw = held([P, 2 * H], U8, "wk_raw")
+        wks_raw = held([P, H], U8, "wks_raw")
+        tabs = held([P, T], U8, "tabs")
+        tabw = held([P, T], U32, "tabw")
+        wgt_t = [held([P, HALF], F32, "wgt%d" % h) for h in range(2)]
+        sel_t = held([P, 2, PACK], F32, "sel_t")
+        bo_t = held([P, 2], F32, "bo_t")
+
+        nc.gpsimd.memset(wks_raw[:].bitcast(I32), 0)
+        for q in range(4):
+            nc.gpsimd.dma_start(out=wks_raw[32 * q : 32 * q + 4, :].bitcast(I32), in_=wk_scales[0, 4 * q : 4 * q + 4, :].bitcast(I32))
+        nc.gpsimd.memset(tabs[:].bitcast(I32), 0)
+        for q in range(4):
+            nc.gpsimd.dma_start(out=tabs[32 * q : 32 * q + 4, :].bitcast(I32), in_=tab_scales[0, 4 * q : 4 * q + 4, :].bitcast(I32))
+        nc.gpsimd.dma_start(out=sel_t[:], in_=sel.rearrange("(g p t) -> p g t", g=2, t=PACK))
+        nc.gpsimd.dma_start(out=bo_t[:], in_=bo.rearrange("(p h) -> p h", h=2))
+
+        x_rows = xT.rearrange("(a p i) d -> a i p d", a=2, i=PACK)
+        wx_rows = wx.rearrange("(a p j) (g r) -> g a p j r", a=2, j=PACK, g=2)
+        planes = {}
+        wx_raw = {}
+
+        def load_plane(a, i):
+            planes[a, i] = big.tile([P, D], F32, name="plane", tag="big", align_bytes=64)
+            nc.sync.dma_start(out=planes[a, i][:], in_=x_rows[a, i])
+
+        def load_wx(g, a):
+            wx_raw[g, a] = held([P, PACK, KP], F32, "wx_raw%d%d" % (g, a))
+            nc.sync.dma_start(out=wx_raw[g, a][:], in_=wx_rows[g, a])
+
+        def load_tab():
+            nc.sync.dma_start(out=tabw[:].bitcast(I32), in_=tab_words[0].rearrange("p t i -> p (t i)").bitcast(I32))
+
+        nc.sync.dma_start(offs2_t[:], offs2)
+        nc.sync.dma_start(out=wk_raw[:].bitcast(I32), in_=wk_words[0].bitcast(I32))
+        nc.sync.dma_start(out=wgt_t[0][:], in_=wgt[:, :HALF])
+        load_plane(0, 0)
+        nc.sync.dma_start(out=wgt_t[1][:], in_=wgt[:, HALF:])
+        for n in range(1, 8):
+            load_plane(n // PACK, n % PACK)
+        nc.sync.dma_start(offs_t[:], offs)
+        load_wx(0, 0)
+        load_wx(0, 1)
+        load_tab()
+        load_wx(1, 0)
+        load_wx(1, 1)
+        wo_raw = held([P, 2, PACK * N], F32, "wo_raw")
+        nc.sync.dma_start(out=wo_raw[:], in_=wo.rearrange("(g p j) n -> p g (j n)", g=2, j=PACK))
+
+        wk_q = held([P, 2 * H], U8, "wk_q")
+        wk_s = held([P, H], U8, "wk_s")
+        nc.vector.tensor_copy(
+            out=wk_q[:].bitcast(U16).rearrange("p (g t m) -> p g m t", g=2, t=PACK),
+            in_=wk_raw[:].bitcast(U16).rearrange("p (g m t) -> p g m t", g=2, t=PACK),
+        )
+        nc.vector.tensor_copy(
+            out=wk_s[:].rearrange("p (g t m) -> p g m t", g=2, t=PACK),
+            in_=wks_raw[:].rearrange("p (g m t) -> p g m t", g=2, t=PACK),
+        )
+
+        def copy_on(engine, dst, src):
+            if engine == "vector":
+                nc.vector.tensor_copy(out=dst, in_=src)
+            else:
+                nc.scalar.copy(out=dst, in_=src)
+
+        picked = {}
+        x_bf, x_q, x_s = {}, {}, {}
+
+        def gather_x(a, i, h):
+            if i == 0:
+                picked[a, h] = held([P, PACK, HALF], F32, "picked%d%d" % (a, h))
+            cols = slice(h * HALF // 16, (h + 1) * HALF // 16)
+            nc.vector.tensor_tensor(picked[a, h][:, i, :], planes[a, i][:].indirect(offs2_t[:, cols]), wgt_t[h][:], MULT)
+
+        def weave_x(a, h, engine):
+            x_bf[a, h] = ring.tile([P, HALF * PACK], BF16, name="x_bf", align_bytes=64)
+            copy_on(
+                engine,
+                x_bf[a, h][:].rearrange("p (c i t) -> p c t i", i=4, t=PACK),
+                picked[a, h][:].rearrange("p t (c i) -> p c t i", i=4),
+            )
+
+        def quant_x(a, h):
+            if (a, h) == (1, 1):
+                x_q[a, h] = late.tile([P, HALF], U32, name="x_q_late", tag="late", align_bytes=64)
+            else:
+                x_q[a, h] = held([P, HALF], U32, "x_q%d%d" % (a, h))
+            x_s[a, h] = held([P, HALF], U8, "x_s%d%d" % (a, h))
+            nc.vector.quantize_mx(out=x_q[a, h][:].bitcast(E4M3), scales=x_s[a, h][:], in_=x_bf[a, h][:])
+
+        w_bf, w_q, w_s = {}, {}, {}
+
+        def weave_wx(g, a, engine):
+            w_bf[g, a] = ring.tile([P, KP * PACK], BF16, name="w_bf", align_bytes=64)
+            copy_on(
+                engine,
+                w_bf[g, a][:].rearrange("p (t m j) -> p m j t", t=PACK, j=PACK),
+                wx_raw[g, a][:].rearrange("p j (m t) -> p m j t", t=PACK),
+            )
+
+        def quant_wx(g, a):
+            if g == 1:
+                w_q[g, a] = late.tile([P, KP], U32, name="w_q_late", tag="late", align_bytes=64)
+            else:
+                w_q[g, a] = held([P, KP], U32, "w_q%d%d" % (g, a))
+            w_s[g, a] = held([P, KP], U8, "w_s%d%d" % (g, a))
+            nc.vector.quantize_mx(out=w_q[g, a][:].bitcast(E4M3), scales=w_s[g, a][:], in_=w_bf[g, a][:])
+
+        t_q, t_s = {}, {}
+
+        def gather_tab(q):
+            t_q[q] = held([P, QUART], U32, "t_q%d" % q)
+            t_s[q] = held([P, QUART], U8, "t_s%d" % q)
+            cols = slice(q * QUART // 16, (q + 1) * QUART // 16)
+            nc.vector.tensor_copy(t_q[q][:], tabw[:].indirect(offs_t[:, cols]))
+            nc.vector.tensor_copy(t_s[q][:], tabs[:].indirect(offs_t[:, cols]))
+
+        banks, expd = {}, {}
+
+        def mm_x(g, q, u, a, first, last):
+            if first:
+                banks[g, q, u] = psum.tile([P, 2, QUART], F32, name="bank", tag="bank")
+            h = q // 2
+            cols = slice((q % 2) * QUART, (q % 2 + 1) * QUART)
+            for e in range(2):
+                t = 2 * u + e
+                m = slice(t * P, (t + 1) * P)
+                nc.tensor.matmul_mx(
+                    out=banks[g, q, u][:, e, :],
+                    lhsT=w_q[g, a][:, m].bitcast(E4M3),
+                    lhsT_scale=w_s[g, a][:, m],
+                    rhs=x_q[a, h][:, cols].bitcast(E4M3),
+                    rhs_scale=x_s[a, h][:, cols],
+                    start=first and e == 0,
+                    stop=last and e == 1,
+                )
+
+        def mm_tab(g, q, u, last):
+            for e in range(2):
+                c0 = g * KP + (2 * u + e) * P
+                for s in range(2):
+                    cols = slice(s * P, (s + 1) * P)
+                    nc.tensor.matmul_mx(
+                        out=banks[g, q, u][:, e, cols],
+                        lhsT=wk_q[:, 2 * c0 : 2 * (c0 + P)].bitcast(E2M1),
+                        lhsT_scale=wk_s[:, c0 : c0 + P],
+                        rhs=t_q[q][:, cols].bitcast(E4M3),
+                        rhs_scale=t_s[q][:, cols],
+                        start=False,
+                        stop=last and e == 1 and s == 1,
+                    )
+
+        def exp_bank(g, q, u):
+            if u == 0:
+                expd[g, q] = big.tile([P, 2, QUART, 2], F32, name="expd", tag="big", align_bytes=64)
+            nc.scalar.activation(expd[g, q][:, u], banks[g, q, u][:].rearrange("p e j -> p j e"), ACT.Exp)
+
+        for a in range(2):
+            for i in range(PACK):
+                for h in range(2):
+                    gather_x(a, i, h)
+            for h in range(2):
+                weave_x(a, h, "scalar")
+            if a == 0:
+                for h in range(2):
+                    quant_x(a, h)
+        for a in range(2):
+            weave_wx(0, a, "vector")
+            quant_x(1, a)
+            quant_wx(0, a)
+        for q in range(4):
+            for u in range(2):
+                mm_x(0, q, u, 0, True, False)
+        for q in range(4):
+            for u in range(2):
+                mm_x(0, q, u, 1, False, False)
+        for q in range(4):
+            gather_tab(q)
+            for u in range(2):
+                mm_tab(0, q, u, True)
+                exp_bank(0, q, u)
+        for a in range(2):
+            weave_wx(1, a, "vector")
+        for a in range(2):
+            quant_wx(1, a)
+        for q in range(4):
+            for u in range(2):
+                mm_x(1, q, u, 0, True, False)
+                mm_tab(1, q, u, False)
+                mm_x(1, q, u, 1, False, True)
+                exp_bank(1, q, u)
+
+        wo_q = held([P, 2 * N], U32, "wo_q")
+        wo_s = held([P, 2 * N], U8, "wo_s")
+        wo_bf = held([P, 2, N * PACK], BF16, "wo_bf")
+        for g in range(2):
+            nc.vector.tensor_copy(
+                out=wo_bf[:, g, :].rearrange("p (h m j) -> p m j h", h=2, j=PACK),
+                in_=wo_raw[:, g, :].rearrange("p (j m h) -> p m j h", j=PACK, h=2),
+            )
+        nc.vector.quantize_mx(out=wo_q[:].bitcast(E4M3), scales=wo_s[:], in_=wo_bf[:].rearrange("p g c -> p (g c)"))
+
+        out_rows = out.rearrange("(p h) j -> p h j", h=2)
+        logs, h_bf, h_q, h_s, acc = {}, {}, {}, {}, {}
+
+        def log_unit(g, q):
+            logs[g, q] = late.tile([P, QUART, PACK], F32, name="logs", tag="late", align_bytes=64)
+            nc.scalar.activation(
+                logs[g, q][:].rearrange("p j (u e) -> p j u e", u=2),
+                expd[g, q][:].rearrange("p u j e -> p j u e"),
+                ACT.Ln,
+                bias=1.0,
+            )
+
+        def scale_unit(g, q):
+            h_bf[g, q] = ring.tile([P, QUART, PACK], BF16, name="h_bf", align_bytes=64, bufs=3)
+            nc.vector.tensor_tensor(
+                h_bf[g, q][:], logs[g, q][:], sel_t[:, g, :].unsqueeze(1).to_broadcast([P, QUART, PACK]), MULT
+            )
+
+        def quant_unit(g, q):
+            h_q[g, q] = ring.tile([P, QUART], U32, name="h_q", align_bytes=64, bufs=4)
+            h_s[g, q] = ring.tile([P, QUART], U8, name="h_s", align_bytes=64, bufs=4)
+            nc.vector.quantize_mx(
+                out=h_q[g, q][:].bitcast(E4M3), scales=h_s[g, q][:], in_=h_bf[g, q][:].rearrange("p j t -> p (j t)")
+            )
+
+        def mm_out(g, q):
+            if g == 0:
+                acc[q] = psum.tile([P, 2, QUART], F32, name="acc", tag="bank")
+            for h in range(2):
+                m = slice(g * N + h * P, g * N + (h + 1) * P)
+                nc.tensor.matmul_mx(
+                    out=acc[q][:, h, :],
+                    lhsT=wo_q[:, m].bitcast(E4M3),
+                    lhsT_scale=wo_s[:, m],
+                    rhs=h_q[g, q][:].bitcast(E4M3),
+                    rhs_scale=h_s[g, q][:],
+                    start=g == 0 and h == 0,
+                    stop=g == 1 and h == 1,
+                )
+
+        def store(q):
+            res = ring.tile([P, 2, QUART], F32, name="res", align_bytes=64, bufs=4)
+            for h in range(2):
+                nc.scalar.activation(res[:, h, :], acc[q][:, h, :], ACT.Identity, bias=bo_t[:, h : h + 1])
+            nc.sync.dma_start(out=out_rows[:, :, q * QUART : (q + 1) * QUART], in_=res[:])
+
+        units = [(g, q) for q in range(4) for g in range(2)]
+        for n in range(len(units) + 3):
+            if n < len(units):
+                log_unit(*units[n])
+            if 0 <= n - 1 < len(units):
+                scale_unit(*units[n - 1])
+            if 0 <= n - 2 < len(units):
+                quant_unit(*units[n - 2])
+                mm_out(*units[n - 2])
+            if 0 <= n - 3 < len(units) and units[n - 3][0] == 1:
+                store(units[n - 3][1])

@@ -47,14 +47,12 @@ def tile_list_predicate_join_cardinality_kernel(
         sel_t = held([P, 2, PACK], F32, "sel_t")
         bo_t = held([P, 2], F32, "bo_t")
 
-        nc.gpsimd.memset(wks_raw[:].bitcast(I32), 0)
-        for q in range(4):
-            nc.gpsimd.dma_start(out=wks_raw[32 * q : 32 * q + 4, :].bitcast(I32), in_=wk_scales[0, 4 * q : 4 * q + 4, :].bitcast(I32))
-        nc.gpsimd.memset(tabs[:].bitcast(I32), 0)
-        for q in range(4):
-            nc.gpsimd.dma_start(out=tabs[32 * q : 32 * q + 4, :].bitcast(I32), in_=tab_scales[0, 4 * q : 4 * q + 4, :].bitcast(I32))
-        nc.gpsimd.dma_start(out=sel_t[:], in_=sel.rearrange("(g p t) -> p g t", g=2, t=PACK))
-        nc.gpsimd.dma_start(out=bo_t[:], in_=bo.rearrange("(p h) -> p h", h=2))
+        nc.vector.memset(wks_raw[:].bitcast(I32), 0)
+        nc.vector.memset(tabs[:].bitcast(I32), 0)
+
+        def load_scales(engine, tile, rows):
+            for q in range(4):
+                engine.dma_start(out=tile[32 * q : 32 * q + 4, :].bitcast(I32), in_=rows[0, 4 * q : 4 * q + 4, :].bitcast(I32))
 
         x_rows = xT.rearrange("(a p i) d -> a i p d", a=2, i=PACK)
         wx_rows = wx.rearrange("(a p j) (g r) -> g a p j r", a=2, j=PACK, g=2)
@@ -74,17 +72,23 @@ def tile_list_predicate_join_cardinality_kernel(
 
         nc.sync.dma_start(offs2_t[:], offs2)
         nc.sync.dma_start(out=wk_raw[:].bitcast(I32), in_=wk_words[0].bitcast(I32))
+        load_scales(nc.scalar, wks_raw, wk_scales)
         nc.sync.dma_start(out=wgt_t[0][:], in_=wgt[:, :HALF])
         load_plane(0, 0)
         nc.sync.dma_start(out=wgt_t[1][:], in_=wgt[:, HALF:])
-        for n in range(1, 8):
+        for n in range(1, 6):
+            load_plane(n // PACK, n % PACK)
+        load_wx(0, 0)
+        for n in range(6, 8):
             load_plane(n // PACK, n % PACK)
         nc.sync.dma_start(offs_t[:], offs)
-        load_wx(0, 0)
         load_wx(0, 1)
+        load_scales(nc.sync, tabs, tab_scales)
         load_tab()
         load_wx(1, 0)
         load_wx(1, 1)
+        nc.sync.dma_start(out=sel_t[:], in_=sel.rearrange("(g p t) -> p g t", g=2, t=PACK))
+        nc.sync.dma_start(out=bo_t[:], in_=bo.rearrange("(p h) -> p h", h=2))
         wo_raw = held([P, 2, PACK * N], F32, "wo_raw")
         nc.sync.dma_start(out=wo_raw[:], in_=wo.rearrange("(g p j) n -> p g (j n)", g=2, j=PACK))
 
@@ -115,7 +119,7 @@ def tile_list_predicate_join_cardinality_kernel(
             nc.vector.tensor_tensor(picked[a, h][:, i, :], planes[a, i][:].indirect(offs2_t[:, cols]), wgt_t[h][:], MULT)
 
         def weave_x(a, h, engine):
-            x_bf[a, h] = ring.tile([P, HALF * PACK], BF16, name="x_bf", align_bytes=64)
+            x_bf[a, h] = ring.tile([P, HALF * PACK], BF16, name="x_bf", tag="bf", align_bytes=64, bufs=4)
             copy_on(
                 engine,
                 x_bf[a, h][:].rearrange("p (c i t) -> p c t i", i=4, t=PACK),
@@ -133,7 +137,7 @@ def tile_list_predicate_join_cardinality_kernel(
         w_bf, w_q, w_s = {}, {}, {}
 
         def weave_wx(g, a, engine):
-            w_bf[g, a] = ring.tile([P, KP * PACK], BF16, name="w_bf", align_bytes=64)
+            w_bf[g, a] = ring.tile([P, KP * PACK], BF16, name="w_bf", tag="wbf", align_bytes=64, bufs=3)
             copy_on(
                 engine,
                 w_bf[g, a][:].rearrange("p (t m j) -> p m j t", t=PACK, j=PACK),
@@ -197,32 +201,37 @@ def tile_list_predicate_join_cardinality_kernel(
                 expd[g, q] = big.tile([P, 2, QUART, 2], F32, name="expd", tag="big", align_bytes=64)
             nc.scalar.activation(expd[g, q][:, u], banks[g, q, u][:].rearrange("p e j -> p j e"), ACT.Exp)
 
-        for a in range(2):
-            for i in range(PACK):
-                for h in range(2):
-                    gather_x(a, i, h)
+        for i in range(PACK):
             for h in range(2):
-                weave_x(a, h, "scalar")
-            if a == 0:
-                for h in range(2):
-                    quant_x(a, h)
-        for a in range(2):
-            weave_wx(0, a, "vector")
-            quant_x(1, a)
-            quant_wx(0, a)
+                gather_x(0, i, h)
+        for h in range(2):
+            weave_x(0, h, "scalar")
+        weave_wx(0, 0, "scalar")
+        for i in range(PACK):
+            for h in range(2):
+                gather_x(1, i, h)
+        for h in range(2):
+            weave_x(1, h, "scalar")
+        for h in range(2):
+            quant_x(0, h)
+        quant_wx(0, 0)
+        weave_wx(0, 1, "vector")
+        quant_x(1, 0)
+        quant_wx(0, 1)
+        quant_x(1, 1)
         for q in range(4):
             for u in range(2):
                 mm_x(0, q, u, 0, True, False)
         for q in range(4):
             for u in range(2):
                 mm_x(0, q, u, 1, False, False)
+        weave_wx(1, 0, "scalar")
         for q in range(4):
             gather_tab(q)
             for u in range(2):
                 mm_tab(0, q, u, True)
                 exp_bank(0, q, u)
-        for a in range(2):
-            weave_wx(1, a, "vector")
+        weave_wx(1, 1, "vector")
         for a in range(2):
             quant_wx(1, a)
         for q in range(4):
@@ -255,7 +264,7 @@ def tile_list_predicate_join_cardinality_kernel(
             )
 
         def scale_unit(g, q):
-            h_bf[g, q] = ring.tile([P, QUART, PACK], BF16, name="h_bf", align_bytes=64, bufs=3)
+            h_bf[g, q] = ring.tile([P, QUART, PACK], BF16, name="h_bf", tag="bf", align_bytes=64, bufs=4)
             nc.vector.tensor_tensor(
                 h_bf[g, q][:], logs[g, q][:], sel_t[:, g, :].unsqueeze(1).to_broadcast([P, QUART, PACK]), MULT
             )
@@ -283,7 +292,7 @@ def tile_list_predicate_join_cardinality_kernel(
                 )
 
         def store(q):
-            res = ring.tile([P, 2, QUART], F32, name="res", align_bytes=64, bufs=4)
+            res = ring.tile([P, 2, QUART], F32, name="res", tag="wbf", align_bytes=64, bufs=3)
             for h in range(2):
                 nc.scalar.activation(res[:, h, :], acc[q][:, h, :], ACT.Identity, bias=bo_t[:, h : h + 1])
             nc.sync.dma_start(out=out_rows[:, :, q * QUART : (q + 1) * QUART], in_=res[:])

@@ -44,14 +44,14 @@ def tile_list_predicate_join_cardinality_kernel(
         tabs = held([P, T], U8, "tabs")
         tabw = held([P, T], U32, "tabw")
         wgt_t = [held([P, HALF], F32, "wgt%d" % h) for h in range(2)]
-        sel_t = held([P, 2, PACK], F32, "sel_t")
+        sel_t = held([P, 2, 8], F32, "sel_t")
         bo_t = held([P, 2], F32, "bo_t")
 
         nc.vector.memset(wks_raw[:].bitcast(I32), 0)
         nc.vector.memset(tabs[:].bitcast(I32), 0)
 
-        def load_scales(engine, tile, rows):
-            for q in range(4):
+        def load_scales(engine, tile, rows, quadrants):
+            for q in quadrants:
                 engine.dma_start(out=tile[32 * q : 32 * q + 4, :].bitcast(I32), in_=rows[0, 4 * q : 4 * q + 4, :].bitcast(I32))
 
         x_rows = xT.rearrange("(a p i) d -> a i p d", a=2, i=PACK)
@@ -64,44 +64,51 @@ def tile_list_predicate_join_cardinality_kernel(
             nc.sync.dma_start(out=planes[a, i][:], in_=x_rows[a, i])
 
         def load_wx(g, a):
-            wx_raw[g, a] = held([P, PACK, KP], F32, "wx_raw%d%d" % (g, a))
+            wx_raw[g, a] = keep.tile([P, PACK, KP], F32, name="wx_raw", tag="wx%d%d" % (g, a), align_bytes=64)
             nc.sync.dma_start(out=wx_raw[g, a][:], in_=wx_rows[g, a])
 
         def load_tab():
             nc.sync.dma_start(out=tabw[:].bitcast(I32), in_=tab_words[0].rearrange("p t i -> p (t i)").bitcast(I32))
 
         nc.sync.dma_start(offs2_t[:], offs2)
-        nc.sync.dma_start(out=wk_raw[:].bitcast(I32), in_=wk_words[0].bitcast(I32))
-        load_scales(nc.scalar, wks_raw, wk_scales)
         nc.sync.dma_start(out=wgt_t[0][:], in_=wgt[:, :HALF])
         load_plane(0, 0)
         nc.sync.dma_start(out=wgt_t[1][:], in_=wgt[:, HALF:])
         for n in range(1, 6):
             load_plane(n // PACK, n % PACK)
         load_wx(0, 0)
-        for n in range(6, 8):
-            load_plane(n // PACK, n % PACK)
-        nc.sync.dma_start(offs_t[:], offs)
+        load_plane(1, 2)
+        load_plane(1, 3)
         load_wx(0, 1)
-        load_scales(nc.sync, tabs, tab_scales)
-        load_tab()
+        nc.sync.dma_start(out=wk_raw[:].bitcast(I32), in_=wk_words[0].bitcast(I32))
+        load_scales(nc.sync, wks_raw, wk_scales, range(4))
         load_wx(1, 0)
+        nc.sync.dma_start(offs_t[:], offs)
+        load_scales(nc.sync, tabs, tab_scales, range(4))
+        load_tab()
         load_wx(1, 1)
-        nc.sync.dma_start(out=sel_t[:], in_=sel.rearrange("(g p t) -> p g t", g=2, t=PACK))
-        nc.sync.dma_start(out=bo_t[:], in_=bo.rearrange("(p h) -> p h", h=2))
-        wo_raw = held([P, 2, PACK * N], F32, "wo_raw")
-        nc.sync.dma_start(out=wo_raw[:], in_=wo.rearrange("(g p j) n -> p g (j n)", g=2, j=PACK))
+        wo_raw = [held([P, PACK, N], F32, "wo_raw%d" % g) for g in range(2)]
+        wo_rows = wo.rearrange("(g m t e) n -> g e m t n", g=2, t=PACK, e=2)
+        for g in range(2):
+            for e in range(2):
+                nc.sync.dma_start(out=wo_raw[g][e::2, :, :], in_=wo_rows[g, e])
+        sel_runs = sel.rearrange("(g m k) -> m g k", g=2, k=8)
+        for e in range(2):
+            nc.sync.dma_start(out=sel_t[e::2, :, 0:7], in_=sel_runs[:, :, e : e + 7])
+        nc.sync.dma_start(out=bo_t[:], in_=bo.rearrange("(h p) -> p h", h=2))
 
         wk_q = held([P, 2 * H], U8, "wk_q")
         wk_s = held([P, H], U8, "wk_s")
-        nc.vector.tensor_copy(
-            out=wk_q[:].bitcast(U16).rearrange("p (g t m) -> p g m t", g=2, t=PACK),
-            in_=wk_raw[:].bitcast(U16).rearrange("p (g m t) -> p g m t", g=2, t=PACK),
-        )
-        nc.vector.tensor_copy(
-            out=wk_s[:].rearrange("p (g t m) -> p g m t", g=2, t=PACK),
-            in_=wks_raw[:].rearrange("p (g m t) -> p g m t", g=2, t=PACK),
-        )
+
+        def order_wk():
+            nc.vector.tensor_copy(
+                out=wk_q[:].bitcast(I32).rearrange("p (g t c m) -> p g c t m", g=2, t=PACK, m=4),
+                in_=wk_raw[:].bitcast(I32).rearrange("p (g c m t) -> p g c t m", g=2, t=PACK, m=4),
+            )
+            nc.vector.tensor_copy(
+                out=wk_s[:].bitcast(U16).rearrange("p (g t c m) -> p g c t m", g=2, t=PACK, m=8),
+                in_=wks_raw[:].bitcast(U16).rearrange("p (g c m t) -> p g c t m", g=2, t=PACK, m=8),
+            )
 
         def copy_on(engine, dst, src):
             if engine == "vector":
@@ -119,11 +126,11 @@ def tile_list_predicate_join_cardinality_kernel(
             nc.vector.tensor_tensor(picked[a, h][:, i, :], planes[a, i][:].indirect(offs2_t[:, cols]), wgt_t[h][:], MULT)
 
         def weave_x(a, h, engine):
-            x_bf[a, h] = ring.tile([P, HALF * PACK], BF16, name="x_bf", tag="bf", align_bytes=64, bufs=4)
+            x_bf[a, h] = ring.tile([P, HALF * PACK], BF16, name="x_bf", tag="bf", align_bytes=64, bufs=3)
             copy_on(
                 engine,
-                x_bf[a, h][:].rearrange("p (c i t) -> p c t i", i=4, t=PACK),
-                picked[a, h][:].rearrange("p t (c i) -> p c t i", i=4),
+                x_bf[a, h][:].rearrange("p (c i t) -> p c t i", i=2, t=PACK),
+                picked[a, h][:].rearrange("p t (c i) -> p c t i", i=2),
             )
 
         def quant_x(a, h):
@@ -137,29 +144,46 @@ def tile_list_predicate_join_cardinality_kernel(
         w_bf, w_q, w_s = {}, {}, {}
 
         def weave_wx(g, a, engine):
-            w_bf[g, a] = ring.tile([P, KP * PACK], BF16, name="w_bf", tag="wbf", align_bytes=64, bufs=3)
+            if g == 0:
+                w_bf[g, a] = ring.tile([P, KP * PACK], BF16, name="w_bf", tag="wbf", align_bytes=64, bufs=3)
+            else:
+                w_bf[g, a] = keep.tile([P, KP * PACK], BF16, name="w_bf1", tag="wbf1%d" % a, align_bytes=64)
             copy_on(
                 engine,
-                w_bf[g, a][:].rearrange("p (t m j) -> p m j t", t=PACK, j=PACK),
-                wx_raw[g, a][:].rearrange("p j (m t) -> p m j t", t=PACK),
+                w_bf[g, a][:].rearrange("p (t m e j) -> p m t j e", t=PACK, e=2, j=PACK),
+                wx_raw[g, a][:].rearrange("p j (m t e) -> p m t j e", t=PACK, e=2),
             )
 
         def quant_wx(g, a):
-            if g == 1:
+            if (g, a) == (1, 1):
                 w_q[g, a] = late.tile([P, KP], U32, name="w_q_late", tag="late", align_bytes=64)
+                w_s[g, a] = late.tile([P, KP], U8, name="w_s_late", tag="late", align_bytes=64)
             else:
                 w_q[g, a] = held([P, KP], U32, "w_q%d%d" % (g, a))
-            w_s[g, a] = held([P, KP], U8, "w_s%d%d" % (g, a))
+                w_s[g, a] = held([P, KP], U8, "w_s%d%d" % (g, a))
             nc.vector.quantize_mx(out=w_q[g, a][:].bitcast(E4M3), scales=w_s[g, a][:], in_=w_bf[g, a][:])
 
         t_q, t_s = {}, {}
 
-        def gather_tab(q):
-            t_q[q] = held([P, QUART], U32, "t_q%d" % q)
-            t_s[q] = held([P, QUART], U8, "t_s%d" % q)
+        def gather_words(q):
+            if q == 0:
+                t_q[q] = held([P, QUART], U32, "t_q0")[:]
+            if q == 1:
+                t_q[q] = keep.tile([P, QUART], U32, name="t_q1", tag="wbf10", align_bytes=64)[:]
+            if q == 2:
+                pair = keep.tile([P, HALF], U32, name="t_q23", tag="wbf11", align_bytes=64)
+                t_q[2], t_q[3] = pair[:, :QUART], pair[:, QUART:]
             cols = slice(q * QUART // 16, (q + 1) * QUART // 16)
-            nc.vector.tensor_copy(t_q[q][:], tabw[:].indirect(offs_t[:, cols]))
-            nc.vector.tensor_copy(t_s[q][:], tabs[:].indirect(offs_t[:, cols]))
+            nc.vector.tensor_copy(t_q[q], tabw[:].indirect(offs_t[:, cols]))
+
+        def gather_scales(h):
+            if h == 0:
+                pair = held([P, HALF], U8, "t_s01")
+            else:
+                pair = keep.tile([P, HALF], U8, name="t_s23", tag="wx10", align_bytes=64)
+            t_s[2 * h], t_s[2 * h + 1] = pair[:, :QUART], pair[:, QUART:]
+            cols = slice(h * HALF // 16, (h + 1) * HALF // 16)
+            nc.vector.tensor_copy(pair[:], tabs[:].indirect(offs_t[:, cols]))
 
         banks, expd = {}, {}
 
@@ -181,7 +205,9 @@ def tile_list_predicate_join_cardinality_kernel(
                     stop=last and e == 1,
                 )
 
-        def mm_tab(g, q, u, last):
+        def mm_tab(g, q, u, first, last):
+            if first:
+                banks[g, q, u] = psum.tile([P, 2, QUART], F32, name="bank", tag="bank")
             for e in range(2):
                 c0 = g * KP + (2 * u + e) * P
                 for s in range(2):
@@ -192,24 +218,30 @@ def tile_list_predicate_join_cardinality_kernel(
                         lhsT_scale=wk_s[:, c0 : c0 + P],
                         rhs=t_q[q][:, cols].bitcast(E4M3),
                         rhs_scale=t_s[q][:, cols],
-                        start=False,
+                        start=first and e == 0 and s == 0,
                         stop=last and e == 1 and s == 1,
                     )
 
         def exp_bank(g, q, u):
-            if u == 0:
-                expd[g, q] = big.tile([P, 2, QUART, 2], F32, name="expd", tag="big", align_bytes=64)
-            nc.scalar.activation(expd[g, q][:, u], banks[g, q, u][:].rearrange("p e j -> p j e"), ACT.Exp)
+            if g == 0 and q == 0 and u == 0:
+                first_half = keep.tile([P, 4, 2, QUART, 2], F32, name="first_half", tag="wx11", align_bytes=64)
+                for n in range(4):
+                    expd[0, n] = first_half[:, n]
+            if g == 1 and u == 0:
+                expd[g, q] = big.tile([P, 2, QUART, 2], F32, name="expd", tag="big", align_bytes=64)[:]
+            nc.scalar.activation(
+                expd[g, q][:, u].rearrange("p (c i) e -> p c e i", i=2),
+                banks[g, q, u][:].rearrange("p e (c i) -> p c e i", i=2),
+                ACT.Exp,
+            )
 
-        for i in range(PACK):
-            for h in range(2):
-                gather_x(0, i, h)
+        for a in range(2):
+            for i in range(PACK):
+                for h in range(2):
+                    gather_x(a, i, h)
         for h in range(2):
             weave_x(0, h, "scalar")
         weave_wx(0, 0, "scalar")
-        for i in range(PACK):
-            for h in range(2):
-                gather_x(1, i, h)
         for h in range(2):
             weave_x(1, h, "scalar")
         for h in range(2):
@@ -218,86 +250,102 @@ def tile_list_predicate_join_cardinality_kernel(
         weave_wx(0, 1, "vector")
         quant_x(1, 0)
         quant_wx(0, 1)
-        quant_x(1, 1)
-        for q in range(4):
-            for u in range(2):
-                mm_x(0, q, u, 0, True, False)
-        for q in range(4):
-            for u in range(2):
-                mm_x(0, q, u, 1, False, False)
-        weave_wx(1, 0, "scalar")
-        for q in range(4):
-            gather_tab(q)
-            for u in range(2):
-                mm_tab(0, q, u, True)
-                exp_bank(0, q, u)
-        weave_wx(1, 1, "vector")
         for a in range(2):
-            quant_wx(1, a)
-        for q in range(4):
+            weave_wx(1, a, "scalar")
+        order_wk()
+        quant_x(1, 1)
+        for a in range(2):
+            for q in range(4):
+                for u in range(2):
+                    mm_x(0, q, u, a, a == 0, False)
+
+        def close_first(q):
+            gather_words(q)
             for u in range(2):
-                mm_x(1, q, u, 0, True, False)
-                mm_tab(1, q, u, False)
+                mm_tab(0, q, u, False, True)
+                exp_bank(0, q, u)
+
+        def whole_second(q):
+            for u in range(2):
+                mm_tab(1, q, u, True, False)
+                mm_x(1, q, u, 0, False, False)
                 mm_x(1, q, u, 1, False, True)
                 exp_bank(1, q, u)
+
+        gather_scales(0)
+        close_first(0)
+        quant_wx(1, 0)
+        close_first(1)
+        gather_scales(1)
+        quant_wx(1, 1)
+        whole_second(0)
+        close_first(2)
+        whole_second(1)
+        close_first(3)
+        whole_second(2)
+        whole_second(3)
 
         wo_q = held([P, 2 * N], U32, "wo_q")
         wo_s = held([P, 2 * N], U8, "wo_s")
         wo_bf = held([P, 2, N * PACK], BF16, "wo_bf")
         for g in range(2):
-            nc.vector.tensor_copy(
-                out=wo_bf[:, g, :].rearrange("p (h m j) -> p m j h", h=2, j=PACK),
-                in_=wo_raw[:, g, :].rearrange("p (j m h) -> p m j h", j=PACK, h=2),
+            copy_on(
+                "vector",
+                wo_bf[:, g, :].rearrange("p (c i j) -> p c j i", i=2, j=PACK),
+                wo_raw[g][:].rearrange("p j (c i) -> p c j i", i=2),
             )
         nc.vector.quantize_mx(out=wo_q[:].bitcast(E4M3), scales=wo_s[:], in_=wo_bf[:].rearrange("p g c -> p (g c)"))
 
-        out_rows = out.rearrange("(p h) j -> p h j", h=2)
+        out_rows = out.rearrange("(h p) j -> p h j", h=2)
         logs, h_bf, h_q, h_s, acc = {}, {}, {}, {}, {}
 
-        def log_unit(g, q):
-            logs[g, q] = late.tile([P, QUART, PACK], F32, name="logs", tag="late", align_bytes=64)
+        def log_unit(g, j0, width):
+            q, lo = divmod(j0, QUART)
+            logs[g, j0] = late.tile([P, width, PACK], F32, name="logs", tag="late", align_bytes=64)
             nc.scalar.activation(
-                logs[g, q][:].rearrange("p j (u e) -> p j u e", u=2),
-                expd[g, q][:].rearrange("p u j e -> p j u e"),
+                logs[g, j0][:].rearrange("p j (u e) -> p j u e", u=2),
+                expd[g, q][:, :, lo : lo + width, :].rearrange("p u j e -> p j u e"),
                 ACT.Ln,
                 bias=1.0,
             )
 
-        def scale_unit(g, q):
-            h_bf[g, q] = ring.tile([P, QUART, PACK], BF16, name="h_bf", tag="bf", align_bytes=64, bufs=4)
+        def scale_unit(g, j0, width):
+            h_bf[g, j0] = ring.tile([P, width, PACK], BF16, name="h_bf", tag="bf", align_bytes=64, bufs=3)
             nc.vector.tensor_tensor(
-                h_bf[g, q][:], logs[g, q][:], sel_t[:, g, :].unsqueeze(1).to_broadcast([P, QUART, PACK]), MULT
+                h_bf[g, j0][:], logs[g, j0][:], sel_t[:, g, 0:7:2].unsqueeze(1).to_broadcast([P, width, PACK]), MULT
             )
 
-        def quant_unit(g, q):
-            h_q[g, q] = ring.tile([P, QUART], U32, name="h_q", align_bytes=64, bufs=4)
-            h_s[g, q] = ring.tile([P, QUART], U8, name="h_s", align_bytes=64, bufs=4)
+        def quant_unit(g, j0, width):
+            h_q[g, j0] = ring.tile([P, width], U32, name="h_q", align_bytes=64, bufs=4)
+            h_s[g, j0] = ring.tile([P, width], U8, name="h_s", align_bytes=64, bufs=4)
             nc.vector.quantize_mx(
-                out=h_q[g, q][:].bitcast(E4M3), scales=h_s[g, q][:], in_=h_bf[g, q][:].rearrange("p j t -> p (j t)")
+                out=h_q[g, j0][:].bitcast(E4M3), scales=h_s[g, j0][:], in_=h_bf[g, j0][:].rearrange("p j t -> p (j t)")
             )
 
-        def mm_out(g, q):
+        def mm_out(g, j0, width):
             if g == 0:
-                acc[q] = psum.tile([P, 2, QUART], F32, name="acc", tag="bank")
+                acc[j0] = psum.tile([P, 2, width], F32, name="acc", tag="bank")
             for h in range(2):
                 m = slice(g * N + h * P, g * N + (h + 1) * P)
                 nc.tensor.matmul_mx(
-                    out=acc[q][:, h, :],
+                    out=acc[j0][:, h, :],
                     lhsT=wo_q[:, m].bitcast(E4M3),
                     lhsT_scale=wo_s[:, m],
-                    rhs=h_q[g, q][:].bitcast(E4M3),
-                    rhs_scale=h_s[g, q][:],
+                    rhs=h_q[g, j0][:].bitcast(E4M3),
+                    rhs_scale=h_s[g, j0][:],
                     start=g == 0 and h == 0,
                     stop=g == 1 and h == 1,
                 )
 
-        def store(q):
-            res = ring.tile([P, 2, QUART], F32, name="res", tag="wbf", align_bytes=64, bufs=3)
+        def store(j0, width):
+            res = ring.tile([P, 2, width], F32, name="res", tag="wbf", align_bytes=64, bufs=3)
             for h in range(2):
-                nc.scalar.activation(res[:, h, :], acc[q][:, h, :], ACT.Identity, bias=bo_t[:, h : h + 1])
-            nc.sync.dma_start(out=out_rows[:, :, q * QUART : (q + 1) * QUART], in_=res[:])
+                nc.scalar.activation(res[:, h, :], acc[j0][:, h, :], ACT.Identity, bias=bo_t[:, h : h + 1])
+            nc.sync.dma_start(out=out_rows[:, :, j0 : j0 + width], in_=res[:])
 
-        units = [(g, q) for q in range(4) for g in range(2)]
+        widths = [128, 128, 256, 256, 128, 128]
+        starts = [sum(widths[:n]) for n in range(len(widths))]
+        units = [(g, j0, width) for j0, width in zip(starts, widths) for g in range(2)]
         for n in range(len(units) + 3):
             if n < len(units):
                 log_unit(*units[n])
@@ -307,4 +355,4 @@ def tile_list_predicate_join_cardinality_kernel(
                 quant_unit(*units[n - 2])
                 mm_out(*units[n - 2])
             if 0 <= n - 3 < len(units) and units[n - 3][0] == 1:
-                store(units[n - 3][1])
+                store(*units[n - 3][1:])

@@ -32,7 +32,7 @@ def tile_list_predicate_join_cardinality_kernel(
         big = ctx.enter_context(tc.tile_pool(name="big", bufs=8))
         late = ctx.enter_context(tc.tile_pool(name="late", bufs=3))
         ring = ctx.enter_context(tc.tile_pool(name="ring", bufs=2))
-        psum = ctx.enter_context(tc.psum_pool(name="psum", bufs=8))
+        psum = ctx.enter_context(tc.psum_pool(name="psum", bufs=1))
 
         def held(shape, dtype, name):
             return keep.tile(shape, dtype, name=name, align_bytes=64)
@@ -42,7 +42,7 @@ def tile_list_predicate_join_cardinality_kernel(
         wk_raw = held([P, 2 * H], U8, "wk_raw")
         wks_raw = held([P, H], U8, "wks_raw")
         tabs = held([P, T], U8, "tabs")
-        tabw = held([P, T], U32, "tabw")
+        tabw = keep.tile([P, T], U32, name="tabw", tag="tabw", align_bytes=64)
         wgt_t = [held([P, HALF], F32, "wgt%d" % h) for h in range(2)]
         sel_t = held([P, 2, 8], F32, "sel_t")
         bo_t = held([P, 2], F32, "bo_t")
@@ -176,20 +176,21 @@ def tile_list_predicate_join_cardinality_kernel(
             cols = slice(q * QUART // 16, (q + 1) * QUART // 16)
             nc.vector.tensor_copy(t_q[q], tabw[:].indirect(offs_t[:, cols]))
 
-        def gather_scales(h):
-            if h == 0:
-                pair = held([P, HALF], U8, "t_s01")
+        def gather_scales(q0, q1):
+            width = (q1 - q0) * QUART
+            if q0 < 2:
+                run = held([P, width], U8, "t_s%d" % q0)
             else:
-                pair = keep.tile([P, HALF], U8, name="t_s23", tag="wx10", align_bytes=64)
-            t_s[2 * h], t_s[2 * h + 1] = pair[:, :QUART], pair[:, QUART:]
-            cols = slice(h * HALF // 16, (h + 1) * HALF // 16)
-            nc.vector.tensor_copy(pair[:], tabs[:].indirect(offs_t[:, cols]))
+                run = keep.tile([P, width], U8, name="t_s23", tag="wx11", align_bytes=64)
+            for q in range(q0, q1):
+                t_s[q] = run[:, (q - q0) * QUART : (q - q0 + 1) * QUART]
+            nc.vector.tensor_copy(run[:], tabs[:].indirect(offs_t[:, q0 * QUART // 16 : q1 * QUART // 16]))
 
         banks, expd = {}, {}
 
         def mm_x(g, q, u, a, first, last):
             if first:
-                banks[g, q, u] = psum.tile([P, 2, QUART], F32, name="bank", tag="bank")
+                banks[g, q, u] = psum.tile([P, 2, QUART], F32, name="bank", tag="bank%d" % (2 * (q if g == 0 else q % 2) + u))
             h = q // 2
             cols = slice((q % 2) * QUART, (q % 2 + 1) * QUART)
             for e in range(2):
@@ -207,7 +208,7 @@ def tile_list_predicate_join_cardinality_kernel(
 
         def mm_tab(g, q, u, first, last):
             if first:
-                banks[g, q, u] = psum.tile([P, 2, QUART], F32, name="bank", tag="bank")
+                banks[g, q, u] = psum.tile([P, 2, QUART], F32, name="bank", tag="bank%d" % (2 * (q if g == 0 else q % 2) + u))
             for e in range(2):
                 c0 = g * KP + (2 * u + e) * P
                 for s in range(2):
@@ -223,11 +224,7 @@ def tile_list_predicate_join_cardinality_kernel(
                     )
 
         def exp_bank(g, q, u):
-            if g == 0 and q == 0 and u == 0:
-                first_half = keep.tile([P, 4, 2, QUART, 2], F32, name="first_half", tag="wx11", align_bytes=64)
-                for n in range(4):
-                    expd[0, n] = first_half[:, n]
-            if g == 1 and u == 0:
+            if u == 0:
                 expd[g, q] = big.tile([P, 2, QUART, 2], F32, name="expd", tag="big", align_bytes=64)[:]
             nc.scalar.activation(
                 expd[g, q][:, u].rearrange("p (c i) e -> p c e i", i=2),
@@ -250,8 +247,7 @@ def tile_list_predicate_join_cardinality_kernel(
         weave_wx(0, 1, "vector")
         quant_x(1, 0)
         quant_wx(0, 1)
-        for a in range(2):
-            weave_wx(1, a, "scalar")
+        weave_wx(1, 0, "scalar")
         order_wk()
         quant_x(1, 1)
         for a in range(2):
@@ -272,22 +268,24 @@ def tile_list_predicate_join_cardinality_kernel(
                 mm_x(1, q, u, 1, False, True)
                 exp_bank(1, q, u)
 
-        gather_scales(0)
+        gather_scales(0, 1)
         close_first(0)
         quant_wx(1, 0)
+        gather_scales(1, 2)
         close_first(1)
-        gather_scales(1)
+        weave_wx(1, 1, "vector")
         quant_wx(1, 1)
         whole_second(0)
-        close_first(2)
         whole_second(1)
+        gather_scales(2, 4)
+        close_first(2)
         close_first(3)
         whole_second(2)
         whole_second(3)
 
         wo_q = held([P, 2 * N], U32, "wo_q")
         wo_s = held([P, 2 * N], U8, "wo_s")
-        wo_bf = held([P, 2, N * PACK], BF16, "wo_bf")
+        wo_bf = keep.tile([P, 2, N * PACK], BF16, name="wo_bf", tag="tabw", align_bytes=64)
         for g in range(2):
             copy_on(
                 "vector",
@@ -296,6 +294,8 @@ def tile_list_predicate_join_cardinality_kernel(
             )
         nc.vector.quantize_mx(out=wo_q[:].bitcast(E4M3), scales=wo_s[:], in_=wo_bf[:].rearrange("p g c -> p (g c)"))
 
+        sel_c = held([P, 2, PACK], F32, "sel_c")
+        nc.vector.tensor_copy(out=sel_c[:], in_=sel_t[:, :, 0:7:2])
         out_rows = out.rearrange("(h p) j -> p h j", h=2)
         logs, h_bf, h_q, h_s, acc = {}, {}, {}, {}, {}
 
@@ -312,7 +312,7 @@ def tile_list_predicate_join_cardinality_kernel(
         def scale_unit(g, j0, width):
             h_bf[g, j0] = ring.tile([P, width, PACK], BF16, name="h_bf", tag="bf", align_bytes=64, bufs=3)
             nc.vector.tensor_tensor(
-                h_bf[g, j0][:], logs[g, j0][:], sel_t[:, g, 0:7:2].unsqueeze(1).to_broadcast([P, width, PACK]), MULT
+                h_bf[g, j0][:], logs[g, j0][:], sel_c[:, g, :].unsqueeze(1).to_broadcast([P, width, PACK]), MULT
             )
 
         def quant_unit(g, j0, width):
@@ -324,7 +324,7 @@ def tile_list_predicate_join_cardinality_kernel(
 
         def mm_out(g, j0, width):
             if g == 0:
-                acc[j0] = psum.tile([P, 2, width], F32, name="acc", tag="bank")
+                acc[j0] = psum.tile([P, 2, width], F32, name="acc", tag="bank%d" % ((4 + len(acc)) % 8))
             for h in range(2):
                 m = slice(g * N + h * P, g * N + (h + 1) * P)
                 nc.tensor.matmul_mx(

@@ -29,7 +29,7 @@ def tile_list_predicate_join_cardinality_kernel(
     nc = tc.nc
     with ExitStack() as ctx:
         keep = ctx.enter_context(tc.tile_pool(name="keep", bufs=1))
-        big = ctx.enter_context(tc.tile_pool(name="big", bufs=8))
+        big = ctx.enter_context(tc.tile_pool(name="big", bufs=7))
         late = ctx.enter_context(tc.tile_pool(name="late", bufs=3))
         ring = ctx.enter_context(tc.tile_pool(name="ring", bufs=2))
         psum = ctx.enter_context(tc.psum_pool(name="psum", bufs=1))
@@ -43,12 +43,12 @@ def tile_list_predicate_join_cardinality_kernel(
         wks_raw = held([P, H], U8, "wks_raw")
         tabs = held([P, T], U8, "tabs")
         tabw = keep.tile([P, T], U32, name="tabw", tag="tabw", align_bytes=64)
-        wgt_t = [held([P, HALF], F32, "wgt%d" % h) for h in range(2)]
+        wgt_t = [keep.tile([P, HALF], F32, name="wgt", tag="wgt%d" % h, align_bytes=64) for h in range(2)]
         sel_t = held([P, 2, 8], F32, "sel_t")
         bo_t = held([P, 2], F32, "bo_t")
 
-        nc.vector.memset(wks_raw[:].bitcast(I32), 0)
         nc.vector.memset(tabs[:].bitcast(I32), 0)
+        nc.vector.memset(wks_raw[:].bitcast(I32), 0)
 
         def load_scales(engine, tile, rows, quadrants):
             for q in quadrants:
@@ -70,22 +70,24 @@ def tile_list_predicate_join_cardinality_kernel(
         def load_tab():
             nc.sync.dma_start(out=tabw[:].bitcast(I32), in_=tab_words[0].rearrange("p t i -> p (t i)").bitcast(I32))
 
+        nc.sync.dma_start(offs_t[:], offs)
+        load_tab()
         nc.sync.dma_start(offs2_t[:], offs2)
         nc.sync.dma_start(out=wgt_t[0][:], in_=wgt[:, :HALF])
         load_plane(0, 0)
         nc.sync.dma_start(out=wgt_t[1][:], in_=wgt[:, HALF:])
-        for n in range(1, 6):
-            load_plane(n // PACK, n % PACK)
+        load_scales(nc.sync, tabs, tab_scales, range(4))
+        for i in range(1, PACK):
+            load_plane(0, i)
         load_wx(0, 0)
-        load_plane(1, 2)
-        load_plane(1, 3)
-        load_wx(0, 1)
+        load_plane(1, 0)
         nc.sync.dma_start(out=wk_raw[:].bitcast(I32), in_=wk_words[0].bitcast(I32))
         load_scales(nc.sync, wks_raw, wk_scales, range(4))
+        load_plane(1, 1)
+        load_wx(0, 1)
+        load_plane(1, 2)
+        load_plane(1, 3)
         load_wx(1, 0)
-        nc.sync.dma_start(offs_t[:], offs)
-        load_scales(nc.sync, tabs, tab_scales, range(4))
-        load_tab()
         load_wx(1, 1)
         wo_raw = [held([P, PACK, N], F32, "wo_raw%d" % g) for g in range(2)]
         wo_rows = wo.rearrange("(g m t e) n -> g e m t n", g=2, t=PACK, e=2)
@@ -119,212 +121,155 @@ def tile_list_predicate_join_cardinality_kernel(
         picked = {}
         x_bf, x_q, x_s = {}, {}, {}
 
-        def gather_x(a, i, h):
+        def gather_x(a, i, h, lo=0, hi=HALF):
             if i == 0:
-                picked[a, h] = held([P, PACK, HALF], F32, "picked%d%d" % (a, h))
-            cols = slice(h * HALF // 16, (h + 1) * HALF // 16)
-            nc.vector.tensor_tensor(picked[a, h][:, i, :], planes[a, i][:].indirect(offs2_t[:, cols]), wgt_t[h][:], MULT)
-
-        def weave_x(a, h, engine):
-            x_bf[a, h] = ring.tile([P, HALF * PACK], BF16, name="x_bf", tag="bf", align_bytes=64, bufs=3)
-            copy_on(
-                engine,
-                x_bf[a, h][:].rearrange("p (c i t) -> p c t i", i=2, t=PACK),
-                picked[a, h][:].rearrange("p t (c i) -> p c t i", i=2),
+                tag = "picked%d%d" % (a, h)
+                picked[a, h] = keep.tile([P, PACK, HALF], F32, name="picked", tag=tag, align_bytes=64)
+            cols = slice((h * HALF + lo) // 16, (h * HALF + hi) // 16)
+            nc.vector.tensor_tensor(
+                picked[a, h][:, i, lo:hi], planes[a, i][:].indirect(offs2_t[:, cols]), wgt_t[h][:, lo:hi], MULT
             )
 
-        def quant_x(a, h):
-            if (a, h) == (1, 1):
-                x_q[a, h] = late.tile([P, HALF], U32, name="x_q_late", tag="late", align_bytes=64)
+        def weave_x(a, h, u, engine):
+            if (a, h, u) == (1, 0, 0):
+                x_bf[a, h, u] = picked[1, 1][:, PACK - 1, :].bitcast(BF16)
             else:
-                x_q[a, h] = held([P, HALF], U32, "x_q%d%d" % (a, h))
-            x_s[a, h] = held([P, HALF], U8, "x_s%d%d" % (a, h))
-            nc.vector.quantize_mx(out=x_q[a, h][:].bitcast(E4M3), scales=x_s[a, h][:], in_=x_bf[a, h][:])
+                x_bf[a, h, u] = ring.tile([P, QUART * PACK], BF16, name="x_bf", tag="bf", align_bytes=64, bufs=6)[:]
+            copy_on(
+                engine,
+                x_bf[a, h, u].rearrange("p (c i t) -> p c t i", i=2, t=PACK),
+                picked[a, h][:, :, u * QUART : (u + 1) * QUART].rearrange("p t (c i) -> p c t i", i=2),
+            )
+
+        def quant_x(a, h, u):
+            if (a, h) not in x_q:
+                if (a, h) == (1, 1):
+                    x_q[a, h] = late.tile([P, HALF], U32, name="x_q_late", tag="late", align_bytes=64)
+                else:
+                    x_q[a, h] = keep.tile([P, HALF], U32, name="x_q", tag="x_q%d%d" % (a, h), align_bytes=64)
+                x_s[a, h] = keep.tile([P, HALF], U8, name="x_s", tag="x_s%d%d" % (a, h), align_bytes=64)
+            cols = slice(u * QUART, (u + 1) * QUART)
+            nc.vector.quantize_mx(out=x_q[a, h][:, cols].bitcast(E4M3), scales=x_s[a, h][:, cols], in_=x_bf[a, h, u])
 
         w_bf, w_q, w_s = {}, {}, {}
 
-        def weave_wx(g, a, engine):
-            if g == 0:
-                w_bf[g, a] = ring.tile([P, KP * PACK], BF16, name="w_bf", tag="wbf", align_bytes=64, bufs=3)
+        def weave_wx(g, a, u, engine):
+            if (g, a, u) == (1, 1, 1):
+                w_bf[g, a, u] = keep.tile([P, 2 * P * PACK], BF16, name="w_bf11", tag="wo_bf", align_bytes=64)[:]
             else:
-                w_bf[g, a] = keep.tile([P, KP * PACK], BF16, name="w_bf1", tag="wbf1%d" % a, align_bytes=64)
+                w_bf[g, a, u] = ring.tile([P, 2 * P * PACK], BF16, name="w_bf", tag="wbf", align_bytes=64, bufs=4)[:]
             copy_on(
                 engine,
-                w_bf[g, a][:].rearrange("p (t m e j) -> p m t j e", t=PACK, e=2, j=PACK),
-                wx_raw[g, a][:].rearrange("p j (m t e) -> p m t j e", t=PACK, e=2),
+                w_bf[g, a, u].rearrange("p (t m e j) -> p m t j e", t=2, e=2, j=PACK),
+                wx_raw[g, a][:].rearrange("p j (m t e) -> p m t j e", t=PACK, e=2)[:, :, 2 * u : 2 * u + 2],
             )
 
-        def quant_wx(g, a):
-            if (g, a) == (1, 1):
-                w_q[g, a] = late.tile([P, KP], U32, name="w_q_late", tag="late", align_bytes=64)
-                w_s[g, a] = late.tile([P, KP], U8, name="w_s_late", tag="late", align_bytes=64)
+        def quant_wx(g, a, u):
+            if (g, a, u) == (1, 1, 1):
+                w_q[g, a, u] = late.tile([P, 2 * P], U32, name="w_q_late", tag="late", align_bytes=64)
+                w_s[g, a, u] = late.tile([P, 2 * P], U8, name="w_s_late", tag="late", align_bytes=64)
             else:
-                w_q[g, a] = held([P, KP], U32, "w_q%d%d" % (g, a))
-                w_s[g, a] = held([P, KP], U8, "w_s%d%d" % (g, a))
-            nc.vector.quantize_mx(out=w_q[g, a][:].bitcast(E4M3), scales=w_s[g, a][:], in_=w_bf[g, a][:])
+                w_q[g, a, u] = held([P, 2 * P], U32, "w_q%d%d%d" % (g, a, u))
+                w_s[g, a, u] = held([P, 2 * P], U8, "w_s%d%d%d" % (g, a, u))
+            nc.vector.quantize_mx(out=w_q[g, a, u][:].bitcast(E4M3), scales=w_s[g, a, u][:], in_=w_bf[g, a, u])
 
         t_q, t_s = {}, {}
 
-        def gather_words(q):
-            if q == 0:
-                t_q[q] = held([P, QUART], U32, "t_q0")[:]
-            if q == 1:
-                t_q[q] = keep.tile([P, QUART], U32, name="t_q1", tag="wbf10", align_bytes=64)[:]
-            if q == 2:
-                pair = keep.tile([P, HALF], U32, name="t_q23", tag="wbf11", align_bytes=64)
-                t_q[2], t_q[3] = pair[:, :QUART], pair[:, QUART:]
-            cols = slice(q * QUART // 16, (q + 1) * QUART // 16)
-            nc.vector.tensor_copy(t_q[q], tabw[:].indirect(offs_t[:, cols]))
+        def gather_scales(h):
+            t_s[h] = keep.tile([P, HALF], U8, name="t_s", tag="t_s%d" % h, align_bytes=64)
+            nc.vector.tensor_copy(t_s[h][:], tabs[:].indirect(offs_t[:, h * HALF // 16 : (h + 1) * HALF // 16]))
 
-        def gather_scales(q0, q1):
-            width = (q1 - q0) * QUART
-            if q0 < 2:
-                run = held([P, width], U8, "t_s%d" % q0)
-            else:
-                run = keep.tile([P, width], U8, name="t_s23", tag="wx11", align_bytes=64)
-            for q in range(q0, q1):
-                t_s[q] = run[:, (q - q0) * QUART : (q - q0 + 1) * QUART]
-            nc.vector.tensor_copy(run[:], tabs[:].indirect(offs_t[:, q0 * QUART // 16 : q1 * QUART // 16]))
+        def gather_words(h):
+            t_q[h] = keep.tile([P, HALF], U32, name="t_q", tag="t_q%d" % h, align_bytes=64)
+            nc.vector.tensor_copy(t_q[h][:], tabw[:].indirect(offs_t[:, h * HALF // 16 : (h + 1) * HALF // 16]))
 
         banks, expd = {}, {}
 
-        def mm_x(g, q, u, a, first, last):
-            if first:
-                banks[g, q, u] = psum.tile([P, 2, QUART], F32, name="bank", tag="bank%d" % (2 * (q if g == 0 else q % 2) + u))
-            h = q // 2
-            cols = slice((q % 2) * QUART, (q % 2 + 1) * QUART)
-            for e in range(2):
-                t = 2 * u + e
-                m = slice(t * P, (t + 1) * P)
-                nc.tensor.matmul_mx(
-                    out=banks[g, q, u][:, e, :],
-                    lhsT=w_q[g, a][:, m].bitcast(E4M3),
-                    lhsT_scale=w_s[g, a][:, m],
-                    rhs=x_q[a, h][:, cols].bitcast(E4M3),
-                    rhs_scale=x_s[a, h][:, cols],
-                    start=first and e == 0,
-                    stop=last and e == 1,
-                )
+        def bank(g, h, t):
+            if (g, h, t) not in banks:
+                banks[g, h, t] = psum.tile([P, HALF], F32, name="bank", tag="bank%d" % (PACK * h + t))
+            return banks[g, h, t][:]
 
-        def mm_tab(g, q, u, first, last):
-            if first:
-                banks[g, q, u] = psum.tile([P, 2, QUART], F32, name="bank", tag="bank%d" % (2 * (q if g == 0 else q % 2) + u))
-            for e in range(2):
-                c0 = g * KP + (2 * u + e) * P
-                for s in range(2):
-                    cols = slice(s * P, (s + 1) * P)
-                    nc.tensor.matmul_mx(
-                        out=banks[g, q, u][:, e, cols],
-                        lhsT=wk_q[:, 2 * c0 : 2 * (c0 + P)].bitcast(E2M1),
-                        lhsT_scale=wk_s[:, c0 : c0 + P],
-                        rhs=t_q[q][:, cols].bitcast(E4M3),
-                        rhs_scale=t_s[q][:, cols],
-                        start=first and e == 0 and s == 0,
-                        stop=last and e == 1 and s == 1,
-                    )
-
-        def exp_bank(g, q, u):
-            if u == 0:
-                expd[g, q] = big.tile([P, 2, QUART, 2], F32, name="expd", tag="big", align_bytes=64)[:]
-            nc.scalar.activation(
-                expd[g, q][:, u].rearrange("p (c i) e -> p c e i", i=2),
-                banks[g, q, u][:].rearrange("p e (c i) -> p c e i", i=2),
-                ACT.Exp,
+        def mm_x(g, h, t, a, first, last):
+            u, m = t // 2, slice(t % 2 * P, (t % 2 + 1) * P)
+            nc.tensor.matmul_mx(
+                out=bank(g, h, t),
+                lhsT=w_q[g, a, u][:, m].bitcast(E4M3),
+                lhsT_scale=w_s[g, a, u][:, m],
+                rhs=x_q[a, h][:].bitcast(E4M3),
+                rhs_scale=x_s[a, h][:],
+                start=first,
+                stop=last,
             )
 
-        for a in range(2):
-            for i in range(PACK):
-                for h in range(2):
-                    gather_x(a, i, h)
-        for h in range(2):
-            weave_x(0, h, "scalar")
-        weave_wx(0, 0, "scalar")
-        for h in range(2):
-            weave_x(1, h, "scalar")
-        for h in range(2):
-            quant_x(0, h)
-        quant_wx(0, 0)
-        weave_wx(0, 1, "vector")
-        quant_x(1, 0)
-        quant_wx(0, 1)
-        weave_wx(1, 0, "scalar")
-        order_wk()
-        quant_x(1, 1)
-        for a in range(2):
-            for q in range(4):
-                for u in range(2):
-                    mm_x(0, q, u, a, a == 0, False)
+        def mm_tab(g, h, t, first, last):
+            c0 = g * KP + t * P
+            nc.tensor.matmul_mx(
+                out=bank(g, h, t),
+                lhsT=wk_q[:, 2 * c0 : 2 * (c0 + P)].bitcast(E2M1),
+                lhsT_scale=wk_s[:, c0 : c0 + P],
+                rhs=t_q[h][:].bitcast(E4M3),
+                rhs_scale=t_s[h][:],
+                start=first,
+                stop=last,
+            )
 
-        def close_first(q):
-            gather_words(q)
-            for u in range(2):
-                mm_tab(0, q, u, False, True)
-                exp_bank(0, q, u)
+        def exp_bank(g, h, t):
+            if (g, h) not in expd:
+                expd[g, h] = keep.tile([P, PACK, HALF], F32, name="expd", tag=("wx00", "wx01", "picked00", "picked01")[2 * g + h], align_bytes=64)
+            nc.scalar.activation(expd[g, h][:, t, :], bank(g, h, t), ACT.Exp)
 
-        def whole_second(q):
-            for u in range(2):
-                mm_tab(1, q, u, True, False)
-                mm_x(1, q, u, 0, False, False)
-                mm_x(1, q, u, 1, False, True)
-                exp_bank(1, q, u)
-
-        gather_scales(0, 1)
-        close_first(0)
-        quant_wx(1, 0)
-        gather_scales(1, 2)
-        close_first(1)
-        weave_wx(1, 1, "vector")
-        quant_wx(1, 1)
-        whole_second(0)
-        whole_second(1)
-        gather_scales(2, 4)
-        close_first(2)
-        close_first(3)
-        whole_second(2)
-        whole_second(3)
+        def gather_plane(n):
+            for h in range(2):
+                gather_x(n // PACK, n % PACK, h)
 
         wo_q = held([P, 2 * N], U32, "wo_q")
         wo_s = held([P, 2 * N], U8, "wo_s")
-        wo_bf = keep.tile([P, 2, N * PACK], BF16, name="wo_bf", tag="tabw", align_bytes=64)
-        for g in range(2):
-            copy_on(
-                "vector",
-                wo_bf[:, g, :].rearrange("p (c i j) -> p c j i", i=2, j=PACK),
-                wo_raw[g][:].rearrange("p j (c i) -> p c j i", i=2),
-            )
-        nc.vector.quantize_mx(out=wo_q[:].bitcast(E4M3), scales=wo_s[:], in_=wo_bf[:].rearrange("p g c -> p (g c)"))
-
         sel_c = held([P, 2, PACK], F32, "sel_c")
-        nc.vector.tensor_copy(out=sel_c[:], in_=sel_t[:, :, 0:7:2])
+
+        def quant_wo():
+            wo_bf = keep.tile([P, 2, N * PACK], BF16, name="wo_bf", tag="wo_bf", align_bytes=64)
+            for g in range(2):
+                nc.vector.tensor_copy(
+                    out=wo_bf[:, g, :].rearrange("p (c i j) -> p c j i", i=2, j=PACK),
+                    in_=wo_raw[g][:].rearrange("p j (c i) -> p c j i", i=2),
+                )
+            nc.vector.tensor_copy(out=sel_c[:], in_=sel_t[:, :, 0:7:2])
+            nc.vector.quantize_mx(out=wo_q[:].bitcast(E4M3), scales=wo_s[:], in_=wo_bf[:].rearrange("p g c -> p (g c)"))
+
         out_rows = out.rearrange("(h p) j -> p h j", h=2)
         logs, h_bf, h_q, h_s, acc = {}, {}, {}, {}, {}
 
         def log_unit(g, j0, width):
-            q, lo = divmod(j0, QUART)
-            logs[g, j0] = late.tile([P, width, PACK], F32, name="logs", tag="late", align_bytes=64)
+            h, lo = divmod(j0, HALF)
+            whole = late.tile([P, 2, width, 2], F32, name="logs", tag="late", align_bytes=64)
+            logs[g, j0] = whole[:]
             nc.scalar.activation(
-                logs[g, j0][:].rearrange("p j (u e) -> p j u e", u=2),
-                expd[g, q][:, :, lo : lo + width, :].rearrange("p u j e -> p j u e"),
+                whole[:],
+                expd[g, h][:, :, lo : lo + width].rearrange("p (u e) j -> p u j e", u=2),
                 ACT.Ln,
                 bias=1.0,
             )
 
         def scale_unit(g, j0, width):
-            h_bf[g, j0] = ring.tile([P, width, PACK], BF16, name="h_bf", tag="bf", align_bytes=64, bufs=3)
+            h_bf[g, j0] = ring.tile([P, width, PACK], BF16, name="h_bf", tag="bf", align_bytes=64, bufs=6)
             nc.vector.tensor_tensor(
-                h_bf[g, j0][:], logs[g, j0][:], sel_c[:, g, :].unsqueeze(1).to_broadcast([P, width, PACK]), MULT
+                h_bf[g, j0][:].rearrange("p j (u e) -> p j u e", u=2),
+                logs[g, j0].rearrange("p u j e -> p j u e"),
+                sel_c[:, g, :].rearrange("p (u e) -> p u e", u=2).unsqueeze(1).to_broadcast([P, width, 2, 2]),
+                MULT,
             )
 
         def quant_unit(g, j0, width):
-            h_q[g, j0] = ring.tile([P, width], U32, name="h_q", align_bytes=64, bufs=4)
-            h_s[g, j0] = ring.tile([P, width], U8, name="h_s", align_bytes=64, bufs=4)
+            h_q[g, j0] = ring.tile([P, width], U32, name="h_q", align_bytes=64, bufs=8)
+            h_s[g, j0] = ring.tile([P, width], U8, name="h_s", align_bytes=64, bufs=8)
             nc.vector.quantize_mx(
                 out=h_q[g, j0][:].bitcast(E4M3), scales=h_s[g, j0][:], in_=h_bf[g, j0][:].rearrange("p j t -> p (j t)")
             )
 
         def mm_out(g, j0, width):
             if g == 0:
-                acc[j0] = psum.tile([P, 2, width], F32, name="acc", tag="bank%d" % ((4 + len(acc)) % 8))
+                acc[j0] = psum.tile([P, 2, width], F32, name="acc", tag="bank%d" % len(acc))
             for h in range(2):
                 m = slice(g * N + h * P, g * N + (h + 1) * P)
                 nc.tensor.matmul_mx(
@@ -338,11 +283,73 @@ def tile_list_predicate_join_cardinality_kernel(
                 )
 
         def store(j0, width):
-            res = ring.tile([P, 2, width], F32, name="res", tag="wbf", align_bytes=64, bufs=3)
+            res = ring.tile([P, 2, width], F32, name="res", tag="wbf", align_bytes=64, bufs=4)
             for h in range(2):
                 nc.scalar.activation(res[:, h, :], acc[j0][:, h, :], ACT.Identity, bias=bo_t[:, h : h + 1])
             nc.sync.dma_start(out=out_rows[:, :, j0 : j0 + width], in_=res[:])
 
+        for h in range(2):
+            gather_words(h)
+        gather_plane(0)
+        for h in range(2):
+            gather_scales(h)
+        for n in range(1, 5):
+            gather_plane(n)
+        for h in range(2):
+            for u in range(2):
+                weave_x(0, h, u, "scalar")
+        for a in range(2):
+            for u in range(2):
+                weave_wx(0, a, u, "scalar")
+        for u in range(2):
+            quant_x(0, 0, u)
+        order_wk()
+        for u in range(2):
+            quant_x(0, 1, u)
+        gather_plane(5)
+        for u in range(2):
+            quant_wx(0, 0, u)
+        gather_plane(6)
+        for u in range(2):
+            quant_wx(0, 1, u)
+        for h in range(2):
+            for t in range(PACK):
+                mm_tab(0, h, t, True, False)
+        for h in range(2):
+            for t in range(PACK):
+                mm_x(0, h, t, 0, False, False)
+        gather_x(1, 3, 0)
+        weave_x(1, 0, 1, "vector")
+        weave_x(1, 0, 0, "scalar")
+        weave_wx(1, 0, 0, "scalar")
+        for u in (1, 0):
+            quant_x(1, 0, u)
+        for t in range(PACK):
+            mm_x(0, 0, t, 1, False, True)
+            exp_bank(0, 0, t)
+        gather_x(1, 3, 1)
+        for u in range(2):
+            weave_x(1, 1, u, "vector")
+        for u in range(2):
+            quant_x(1, 1, u)
+        weave_wx(1, 0, 1, "scalar")
+        for t in range(PACK):
+            mm_x(0, 1, t, 1, False, True)
+            exp_bank(0, 1, t)
+        for t in range(PACK):
+            mm_tab(1, 0, t, True, False)
+        for u in range(2):
+            weave_wx(1, 1, u, "vector")
+            for a in range(2):
+                quant_wx(1, a, u)
+            for h in range(2):
+                for t in (2 * u, 2 * u + 1):
+                    if h == 1:
+                        mm_tab(1, h, t, True, False)
+                    mm_x(1, h, t, 0, False, False)
+                    mm_x(1, h, t, 1, False, True)
+                    exp_bank(1, h, t)
+        quant_wo()
         widths = [128, 128, 256, 256, 128, 128]
         starts = [sum(widths[:n]) for n in range(len(widths))]
         units = [(g, j0, width) for j0, width in zip(starts, widths) for g in range(2)]

@@ -14,6 +14,7 @@ U8 = mybir.dt.uint8
 E4M3 = mybir.dt.float8_e4m3fn_x4
 E2M1 = mybir.dt.float4_e2m1fn_x4
 MULT = mybir.AluOpType.mult
+ADD = mybir.AluOpType.add
 ACT = mybir.ActivationFunctionType
 
 P = 128
@@ -43,7 +44,7 @@ def tile_list_predicate_join_cardinality_kernel(
         wks_raw = held([P, H], U8, "wks_raw")
         tabs = held([P, T], U8, "tabs")
         tabw = keep.tile([P, T], U32, name="tabw", tag="tabw", align_bytes=64)
-        wgt_t = [keep.tile([P, HALF], F32, name="wgt", tag="wgt%d" % h, align_bytes=64) for h in range(2)]
+        wgt_t = held([P, S], F32, "wgt_t")
         sel_t = held([P, 2, 8], F32, "sel_t")
         bo_t = held([P, 2], F32, "bo_t")
 
@@ -70,16 +71,16 @@ def tile_list_predicate_join_cardinality_kernel(
         def load_tab():
             nc.sync.dma_start(out=tabw[:].bitcast(I32), in_=tab_words[0].rearrange("p t i -> p (t i)").bitcast(I32))
 
+        load_scales(nc.scalar, tabs, tab_scales, range(4))
         nc.sync.dma_start(offs_t[:], offs)
         load_tab()
         nc.sync.dma_start(offs2_t[:], offs2)
-        nc.sync.dma_start(out=wgt_t[0][:], in_=wgt[:, :HALF])
+        nc.sync.dma_start(out=wgt_t[:], in_=wgt)
         load_plane(0, 0)
-        nc.sync.dma_start(out=wgt_t[1][:], in_=wgt[:, HALF:])
-        load_scales(nc.sync, tabs, tab_scales, range(4))
-        for i in range(1, PACK):
-            load_plane(0, i)
+        load_plane(0, 1)
+        load_plane(0, 2)
         load_wx(0, 0)
+        load_plane(0, 3)
         load_plane(1, 0)
         nc.sync.dma_start(out=wk_raw[:].bitcast(I32), in_=wk_words[0].bitcast(I32))
         load_scales(nc.sync, wks_raw, wk_scales, range(4))
@@ -118,70 +119,67 @@ def tile_list_predicate_join_cardinality_kernel(
             else:
                 nc.scalar.copy(out=dst, in_=src)
 
-        picked = {}
-        x_bf, x_q, x_s = {}, {}, {}
+        picked0 = keep.tile([P, PACK, S], F32, name="picked0", tag="picked0", align_bytes=64)
+        picked1 = [held([P, PACK, HALF], F32, "picked1%d" % h) for h in range(2)]
 
-        def gather_x(a, i, h, lo=0, hi=HALF):
-            if i == 0:
-                tag = "picked%d%d" % (a, h)
-                picked[a, h] = keep.tile([P, PACK, HALF], F32, name="picked", tag=tag, align_bytes=64)
-            cols = slice((h * HALF + lo) // 16, (h * HALF + hi) // 16)
+        def picks(a, lo, hi):
+            if a == 0:
+                return picked0[:, :, lo:hi]
+            h = lo // HALF
+            return picked1[h][:, :, lo - h * HALF : hi - h * HALF]
+
+        x_bf = {}
+        x_q = [held([P, S], U32, "x_q0"), late.tile([P, S], U32, name="x_q1", tag="late", align_bytes=64)]
+        x_s = [held([P, S], U8, "x_s%d" % a) for a in range(2)]
+
+        def gather_x(a, i, lo, hi):
             nc.vector.tensor_tensor(
-                picked[a, h][:, i, lo:hi], planes[a, i][:].indirect(offs2_t[:, cols]), wgt_t[h][:, lo:hi], MULT
+                picks(a, lo, hi)[:, i, :], planes[a, i][:].indirect(offs2_t[:, lo // 16 : hi // 16]), wgt_t[:, lo:hi], MULT
             )
 
-        def weave_x(a, h, u, engine):
-            if (a, h, u) == (1, 0, 0):
-                x_bf[a, h, u] = picked[1, 1][:, PACK - 1, :].bitcast(BF16)
+        def weave_x(a, lo, hi, engine):
+            if (a, lo) == (1, 0):
+                x_bf[a, lo] = picked1[1][:, PACK - 1, :].bitcast(BF16)
             else:
-                x_bf[a, h, u] = ring.tile([P, QUART * PACK], BF16, name="x_bf", tag="bf", align_bytes=64, bufs=6)[:]
+                x_bf[a, lo] = ring.tile([P, (hi - lo) * PACK], BF16, name="x_bf", tag="bf", align_bytes=64, bufs=4)[:]
             copy_on(
                 engine,
-                x_bf[a, h, u].rearrange("p (c i t) -> p c t i", i=2, t=PACK),
-                picked[a, h][:, :, u * QUART : (u + 1) * QUART].rearrange("p t (c i) -> p c t i", i=2),
+                x_bf[a, lo].rearrange("p (c i t) -> p c t i", i=2, t=PACK),
+                picks(a, lo, hi).rearrange("p t (c i) -> p c t i", i=2),
             )
 
-        def quant_x(a, h, u):
-            if (a, h) not in x_q:
-                if (a, h) == (1, 1):
-                    x_q[a, h] = late.tile([P, HALF], U32, name="x_q_late", tag="late", align_bytes=64)
-                else:
-                    x_q[a, h] = keep.tile([P, HALF], U32, name="x_q", tag="x_q%d%d" % (a, h), align_bytes=64)
-                x_s[a, h] = keep.tile([P, HALF], U8, name="x_s", tag="x_s%d%d" % (a, h), align_bytes=64)
-            cols = slice(u * QUART, (u + 1) * QUART)
-            nc.vector.quantize_mx(out=x_q[a, h][:, cols].bitcast(E4M3), scales=x_s[a, h][:, cols], in_=x_bf[a, h, u])
+        def quant_x(a, lo, hi):
+            nc.vector.quantize_mx(out=x_q[a][:, lo:hi].bitcast(E4M3), scales=x_s[a][:, lo:hi], in_=x_bf[a, lo])
 
         w_bf, w_q, w_s = {}, {}, {}
 
-        def weave_wx(g, a, u, engine):
-            if (g, a, u) == (1, 1, 1):
-                w_bf[g, a, u] = keep.tile([P, 2 * P * PACK], BF16, name="w_bf11", tag="wo_bf", align_bytes=64)[:]
+        def weave_wx(g, a, t0, t1, engine):
+            width = (t1 - t0) * P * PACK
+            if (g, a, t0) == (1, 1, 2):
+                w_bf[g, a, t0] = keep.tile([P, width], BF16, name="w_bf_last", tag="wo_bf", align_bytes=64)
             else:
-                w_bf[g, a, u] = ring.tile([P, 2 * P * PACK], BF16, name="w_bf", tag="wbf", align_bytes=64, bufs=4)[:]
+                w_bf[g, a, t0] = ring.tile([P, width], BF16, name="w_bf", tag="wbf", align_bytes=64, bufs=4)
             copy_on(
                 engine,
-                w_bf[g, a, u].rearrange("p (t m e j) -> p m t j e", t=2, e=2, j=PACK),
-                wx_raw[g, a][:].rearrange("p j (m t e) -> p m t j e", t=PACK, e=2)[:, :, 2 * u : 2 * u + 2],
+                w_bf[g, a, t0][:].rearrange("p (t m e j) -> p m t j e", t=t1 - t0, e=2, j=PACK),
+                wx_raw[g, a][:].rearrange("p j (m t e) -> p m t j e", t=PACK, e=2)[:, :, t0:t1],
             )
 
-        def quant_wx(g, a, u):
-            if (g, a, u) == (1, 1, 1):
-                w_q[g, a, u] = late.tile([P, 2 * P], U32, name="w_q_late", tag="late", align_bytes=64)
-                w_s[g, a, u] = late.tile([P, 2 * P], U8, name="w_s_late", tag="late", align_bytes=64)
+        def quant_wx(g, a, t0, t1):
+            width = (t1 - t0) * P
+            if (g, a, t0) == (1, 1, 2):
+                codes = late.tile([P, width], U32, name="w_q_late", tag="late", align_bytes=64)
+                scales = late.tile([P, width], U8, name="w_s_late", tag="late", align_bytes=64)
             else:
-                w_q[g, a, u] = held([P, 2 * P], U32, "w_q%d%d%d" % (g, a, u))
-                w_s[g, a, u] = held([P, 2 * P], U8, "w_s%d%d%d" % (g, a, u))
-            nc.vector.quantize_mx(out=w_q[g, a, u][:].bitcast(E4M3), scales=w_s[g, a, u][:], in_=w_bf[g, a, u])
+                codes = held([P, width], U32, "w_q%d%d%d" % (g, a, t0))
+                scales = held([P, width], U8, "w_s%d%d%d" % (g, a, t0))
+            for t in range(t0, t1):
+                w_q[g, a, t] = codes[:, (t - t0) * P : (t - t0 + 1) * P]
+                w_s[g, a, t] = scales[:, (t - t0) * P : (t - t0 + 1) * P]
+            nc.vector.quantize_mx(out=codes[:].bitcast(E4M3), scales=scales[:], in_=w_bf[g, a, t0][:])
 
-        t_q, t_s = {}, {}
-
-        def gather_scales(h):
-            t_s[h] = keep.tile([P, HALF], U8, name="t_s", tag="t_s%d" % h, align_bytes=64)
-            nc.vector.tensor_copy(t_s[h][:], tabs[:].indirect(offs_t[:, h * HALF // 16 : (h + 1) * HALF // 16]))
-
-        def gather_words(h):
-            t_q[h] = keep.tile([P, HALF], U32, name="t_q", tag="t_q%d" % h, align_bytes=64)
-            nc.vector.tensor_copy(t_q[h][:], tabw[:].indirect(offs_t[:, h * HALF // 16 : (h + 1) * HALF // 16]))
+        t_q = held([P, S], U32, "t_q")
+        t_s = held([P, S], U8, "t_s")
 
         banks, expd = {}, {}
 
@@ -191,13 +189,13 @@ def tile_list_predicate_join_cardinality_kernel(
             return banks[g, h, t][:]
 
         def mm_x(g, h, t, a, first, last):
-            u, m = t // 2, slice(t % 2 * P, (t % 2 + 1) * P)
+            cols = slice(h * HALF, (h + 1) * HALF)
             nc.tensor.matmul_mx(
                 out=bank(g, h, t),
-                lhsT=w_q[g, a, u][:, m].bitcast(E4M3),
-                lhsT_scale=w_s[g, a, u][:, m],
-                rhs=x_q[a, h][:].bitcast(E4M3),
-                rhs_scale=x_s[a, h][:],
+                lhsT=w_q[g, a, t].bitcast(E4M3),
+                lhsT_scale=w_s[g, a, t],
+                rhs=x_q[a][:, cols].bitcast(E4M3),
+                rhs_scale=x_s[a][:, cols],
                 start=first,
                 stop=last,
             )
@@ -208,20 +206,55 @@ def tile_list_predicate_join_cardinality_kernel(
                 out=bank(g, h, t),
                 lhsT=wk_q[:, 2 * c0 : 2 * (c0 + P)].bitcast(E2M1),
                 lhsT_scale=wk_s[:, c0 : c0 + P],
-                rhs=t_q[h][:].bitcast(E4M3),
-                rhs_scale=t_s[h][:],
+                rhs=t_q[:, h * HALF : (h + 1) * HALF].bitcast(E4M3),
+                rhs_scale=t_s[:, h * HALF : (h + 1) * HALF],
                 start=first,
                 stop=last,
             )
 
         def exp_bank(g, h, t):
             if (g, h) not in expd:
-                expd[g, h] = keep.tile([P, PACK, HALF], F32, name="expd", tag=("wx00", "wx01", "picked00", "picked01")[2 * g + h], align_bytes=64)
+                expd[g, h] = keep.tile([P, PACK, HALF], F32, name="expd", tag=("wx00", "wx01", "picked0", "tabw")[2 * g + h], align_bytes=64)
             nc.scalar.activation(expd[g, h][:, t, :], bank(g, h, t), ACT.Exp)
 
-        def gather_plane(n):
-            for h in range(2):
-                gather_x(n // PACK, n % PACK, h)
+        def quarter_bank(q, u):
+            if (q, u) not in banks:
+                banks[q, u] = psum.tile([P, 2, QUART], F32, name="bank", tag="bank%d" % (2 * q + u))
+            return banks[q, u]
+
+        def quarter_tab(q, u):
+            for e in range(2):
+                c0 = (2 * u + e) * P
+                for k in range(2):
+                    cols = slice(q * QUART + k * P, q * QUART + (k + 1) * P)
+                    nc.tensor.matmul_mx(
+                        out=quarter_bank(q, u)[:, e, k * P : (k + 1) * P],
+                        lhsT=wk_q[:, 2 * c0 : 2 * (c0 + P)].bitcast(E2M1),
+                        lhsT_scale=wk_s[:, c0 : c0 + P],
+                        rhs=t_q[:, cols].bitcast(E4M3),
+                        rhs_scale=t_s[:, cols],
+                        start=e == 0 and k == 0,
+                        stop=False,
+                    )
+
+        def quarter_x(q, u, a):
+            cols = slice(q * QUART, (q + 1) * QUART)
+            for e in range(2):
+                nc.tensor.matmul_mx(
+                    out=quarter_bank(q, u)[:, e, :],
+                    lhsT=w_q[0, a, 2 * u + e].bitcast(E4M3),
+                    lhsT_scale=w_s[0, a, 2 * u + e],
+                    rhs=x_q[a][:, cols].bitcast(E4M3),
+                    rhs_scale=x_s[a][:, cols],
+                    start=False,
+                    stop=a == 1 and e == 1,
+                )
+
+        def quarter_exp(q, u):
+            if (0, 1) not in expd:
+                expd[0, 1] = keep.tile([P, PACK, HALF], F32, name="expd", tag="wx01", align_bytes=64)
+            lo = q * QUART - HALF
+            nc.scalar.activation(expd[0, 1][:, 2 * u : 2 * u + 2, lo : lo + QUART], quarter_bank(q, u)[:], ACT.Exp)
 
         wo_q = held([P, 2 * N], U32, "wo_q")
         wo_s = held([P, 2 * N], U8, "wo_s")
@@ -252,19 +285,23 @@ def tile_list_predicate_join_cardinality_kernel(
             )
 
         def scale_unit(g, j0, width):
-            h_bf[g, j0] = ring.tile([P, width, PACK], BF16, name="h_bf", tag="bf", align_bytes=64, bufs=6)
+            if g == 0:
+                h_bf[j0] = ring.tile([P, 2, width, PACK], BF16, name="h_bf", tag="bf", align_bytes=64, bufs=4)
             nc.vector.tensor_tensor(
-                h_bf[g, j0][:].rearrange("p j (u e) -> p j u e", u=2),
+                h_bf[j0][:, g].rearrange("p j (u e) -> p j u e", u=2),
                 logs[g, j0].rearrange("p u j e -> p j u e"),
                 sel_c[:, g, :].rearrange("p (u e) -> p u e", u=2).unsqueeze(1).to_broadcast([P, width, 2, 2]),
                 MULT,
             )
 
-        def quant_unit(g, j0, width):
-            h_q[g, j0] = ring.tile([P, width], U32, name="h_q", align_bytes=64, bufs=8)
-            h_s[g, j0] = ring.tile([P, width], U8, name="h_s", align_bytes=64, bufs=8)
+        def quant_unit(g0, g1, j0, width):
+            if g0 == 0:
+                h_q[j0] = ring.tile([P, 2, width], U32, name="h_q", align_bytes=64, bufs=3)
+                h_s[j0] = ring.tile([P, 2, width], U8, name="h_s", align_bytes=64, bufs=3)
             nc.vector.quantize_mx(
-                out=h_q[g, j0][:].bitcast(E4M3), scales=h_s[g, j0][:], in_=h_bf[g, j0][:].rearrange("p j t -> p (j t)")
+                out=h_q[j0][:, g0:g1].rearrange("p g j -> p (g j)").bitcast(E4M3),
+                scales=h_s[j0][:, g0:g1].rearrange("p g j -> p (g j)"),
+                in_=h_bf[j0][:, g0:g1].rearrange("p g j t -> p (g j t)"),
             )
 
         def mm_out(g, j0, width):
@@ -276,74 +313,77 @@ def tile_list_predicate_join_cardinality_kernel(
                     out=acc[j0][:, h, :],
                     lhsT=wo_q[:, m].bitcast(E4M3),
                     lhsT_scale=wo_s[:, m],
-                    rhs=h_q[g, j0][:].bitcast(E4M3),
-                    rhs_scale=h_s[g, j0][:],
+                    rhs=h_q[j0][:, g].bitcast(E4M3),
+                    rhs_scale=h_s[j0][:, g],
                     start=g == 0 and h == 0,
                     stop=g == 1 and h == 1,
                 )
 
         def store(j0, width):
             res = ring.tile([P, 2, width], F32, name="res", tag="wbf", align_bytes=64, bufs=4)
-            for h in range(2):
-                nc.scalar.activation(res[:, h, :], acc[j0][:, h, :], ACT.Identity, bias=bo_t[:, h : h + 1])
+            if j0 + width == S:
+                nc.vector.tensor_tensor(res[:], acc[j0][:], bo_t[:].unsqueeze(2).to_broadcast([P, 2, width]), ADD)
+            else:
+                for h in range(2):
+                    nc.scalar.activation(res[:, h, :], acc[j0][:, h, :], ACT.Identity, bias=bo_t[:, h : h + 1])
             nc.sync.dma_start(out=out_rows[:, :, j0 : j0 + width], in_=res[:])
 
+        nc.vector.tensor_copy(t_s[:], tabs[:].indirect(offs_t[:]))
+        nc.vector.tensor_copy(t_q[:], tabw[:].indirect(offs_t[:]))
+        gather_x(0, 0, 0, S)
+        for i in range(1, PACK):
+            gather_x(0, i, 0, S)
+        gather_x(1, 0, 0, HALF)
+        gather_x(1, 0, HALF, S)
+        weave_wx(0, 0, 0, PACK, "scalar")
         for h in range(2):
-            gather_words(h)
-        gather_plane(0)
-        for h in range(2):
-            gather_scales(h)
-        for n in range(1, 5):
-            gather_plane(n)
-        for h in range(2):
-            for u in range(2):
-                weave_x(0, h, u, "scalar")
-        for a in range(2):
-            for u in range(2):
-                weave_wx(0, a, u, "scalar")
-        for u in range(2):
-            quant_x(0, 0, u)
+            weave_x(0, h * HALF, (h + 1) * HALF, "scalar")
+        weave_wx(0, 1, 0, PACK, "scalar")
+        quant_wx(0, 0, 0, PACK)
+        quant_x(0, 0, HALF)
         order_wk()
-        for u in range(2):
-            quant_x(0, 1, u)
-        gather_plane(5)
-        for u in range(2):
-            quant_wx(0, 0, u)
-        gather_plane(6)
-        for u in range(2):
-            quant_wx(0, 1, u)
-        for h in range(2):
-            for t in range(PACK):
-                mm_tab(0, h, t, True, False)
-        for h in range(2):
-            for t in range(PACK):
-                mm_x(0, h, t, 0, False, False)
-        gather_x(1, 3, 0)
-        weave_x(1, 0, 1, "vector")
-        weave_x(1, 0, 0, "scalar")
-        weave_wx(1, 0, 0, "scalar")
-        for u in (1, 0):
-            quant_x(1, 0, u)
+        quant_x(0, HALF, S)
+        gather_x(1, 1, 0, HALF)
+        gather_x(1, 1, HALF, S)
+        gather_x(1, 2, 0, HALF)
+        gather_x(1, 2, HALF, S)
+        quant_wx(0, 1, 0, PACK)
+        for t in range(PACK):
+            mm_tab(0, 0, t, True, False)
+        for q in (2, 3):
+            for u in range(2):
+                quarter_tab(q, u)
+        for t in range(PACK):
+            mm_x(0, 0, t, 0, False, False)
+        for q in (2, 3):
+            for u in range(2):
+                quarter_x(q, u, 0)
+        gather_x(1, 3, 0, HALF)
+        weave_x(1, QUART, HALF, "vector")
+        weave_x(1, 0, QUART, "scalar")
+        weave_wx(1, 0, 0, 2, "scalar")
+        quant_x(1, QUART, HALF)
+        quant_x(1, 0, QUART)
         for t in range(PACK):
             mm_x(0, 0, t, 1, False, True)
             exp_bank(0, 0, t)
-        gather_x(1, 3, 1)
-        for u in range(2):
-            weave_x(1, 1, u, "vector")
-        for u in range(2):
-            quant_x(1, 1, u)
-        weave_wx(1, 0, 1, "scalar")
-        for t in range(PACK):
-            mm_x(0, 1, t, 1, False, True)
-            exp_bank(0, 1, t)
+        for q in (2, 3):
+            gather_x(1, 3, q * QUART, (q + 1) * QUART)
+            weave_x(1, q * QUART, (q + 1) * QUART, "vector")
+            quant_x(1, q * QUART, (q + 1) * QUART)
+            for u in range(2):
+                quarter_x(q, u, 1)
+                quarter_exp(q, u)
         for t in range(PACK):
             mm_tab(1, 0, t, True, False)
-        for u in range(2):
-            weave_wx(1, 1, u, "vector")
+        for t0 in (0, 2):
+            if t0 == 2:
+                weave_wx(1, 0, t0, t0 + 2, "vector")
+            weave_wx(1, 1, t0, t0 + 2, "vector")
             for a in range(2):
-                quant_wx(1, a, u)
+                quant_wx(1, a, t0, t0 + 2)
             for h in range(2):
-                for t in (2 * u, 2 * u + 1):
+                for t in (t0, t0 + 1):
                     if h == 1:
                         mm_tab(1, h, t, True, False)
                     mm_x(1, h, t, 0, False, False)
@@ -351,15 +391,25 @@ def tile_list_predicate_join_cardinality_kernel(
                     exp_bank(1, h, t)
         quant_wo()
         widths = [128, 128, 256, 256, 128, 128]
-        starts = [sum(widths[:n]) for n in range(len(widths))]
-        units = [(g, j0, width) for j0, width in zip(starts, widths) for g in range(2)]
-        for n in range(len(units) + 3):
-            if n < len(units):
-                log_unit(*units[n])
-            if 0 <= n - 1 < len(units):
-                scale_unit(*units[n - 1])
-            if 0 <= n - 2 < len(units):
-                quant_unit(*units[n - 2])
-                mm_out(*units[n - 2])
-            if 0 <= n - 3 < len(units) and units[n - 3][0] == 1:
-                store(*units[n - 3][1:])
+        steps = [(sum(widths[:n]), width) for n, width in enumerate(widths)]
+
+        def finish(g0, g1, j0, width):
+            quant_unit(g0, g1, j0, width)
+            for g in range(g0, g1):
+                mm_out(g, j0, width)
+            if g1 == 2:
+                store(j0, width)
+
+        for g in range(2):
+            log_unit(g, *steps[0])
+        for n, step in enumerate(steps):
+            if n + 1 < len(steps):
+                log_unit(0, *steps[n + 1])
+            scale_unit(0, *step)
+            if n > 0:
+                finish(0, 2, *steps[n - 1])
+            if n + 1 < len(steps):
+                log_unit(1, *steps[n + 1])
+            scale_unit(1, *step)
+        finish(0, 1, *steps[-1])
+        finish(1, 2, *steps[-1])

@@ -14,7 +14,6 @@ U8 = mybir.dt.uint8
 E4M3 = mybir.dt.float8_e4m3fn_x4
 E2M1 = mybir.dt.float4_e2m1fn_x4
 MULT = mybir.AluOpType.mult
-ADD = mybir.AluOpType.add
 ACT = mybir.ActivationFunctionType
 
 P = 128
@@ -31,7 +30,7 @@ def tile_list_predicate_join_cardinality_kernel(
     with ExitStack() as ctx:
         keep = ctx.enter_context(tc.tile_pool(name="keep", bufs=1))
         big = ctx.enter_context(tc.tile_pool(name="big", bufs=7))
-        late = ctx.enter_context(tc.tile_pool(name="late", bufs=3))
+        late = ctx.enter_context(tc.tile_pool(name="late", bufs=4))
         ring = ctx.enter_context(tc.tile_pool(name="ring", bufs=2))
         psum = ctx.enter_context(tc.psum_pool(name="psum", bufs=1))
 
@@ -130,7 +129,7 @@ def tile_list_predicate_join_cardinality_kernel(
 
         x_bf = {}
         x_q = [held([P, S], U32, "x_q0"), late.tile([P, S], U32, name="x_q1", tag="late", align_bytes=64)]
-        x_s = [held([P, S], U8, "x_s%d" % a) for a in range(2)]
+        x_s = [held([P, S], U8, "x_s0"), late.tile([P, S], U8, name="x_s1", tag="late", align_bytes=64)]
 
         def gather_x(a, i, lo, hi):
             nc.vector.tensor_tensor(
@@ -155,7 +154,7 @@ def tile_list_predicate_join_cardinality_kernel(
 
         def weave_wx(g, a, t0, t1, engine):
             width = (t1 - t0) * P * PACK
-            if (g, a, t0) == (1, 1, 2):
+            if (g, a, t1) == (1, 1, PACK):
                 w_bf[g, a, t0] = keep.tile([P, width], BF16, name="w_bf_last", tag="wo_bf", align_bytes=64)
             else:
                 w_bf[g, a, t0] = ring.tile([P, width], BF16, name="w_bf", tag="wbf", align_bytes=64, bufs=4)
@@ -167,7 +166,7 @@ def tile_list_predicate_join_cardinality_kernel(
 
         def quant_wx(g, a, t0, t1):
             width = (t1 - t0) * P
-            if (g, a, t0) == (1, 1, 2):
+            if (g, a, t1) == (1, 1, PACK):
                 codes = late.tile([P, width], U32, name="w_q_late", tag="late", align_bytes=64)
                 scales = late.tile([P, width], U8, name="w_s_late", tag="late", align_bytes=64)
             else:
@@ -251,10 +250,10 @@ def tile_list_predicate_join_cardinality_kernel(
                 )
 
         def quarter_exp(q, u):
-            if (0, 1) not in expd:
-                expd[0, 1] = keep.tile([P, PACK, HALF], F32, name="expd", tag="wx01", align_bytes=64)
-            lo = q * QUART - HALF
-            nc.scalar.activation(expd[0, 1][:, 2 * u : 2 * u + 2, lo : lo + QUART], quarter_bank(q, u)[:], ACT.Exp)
+            h, lo = divmod(q * QUART, HALF)
+            if (0, h) not in expd:
+                expd[0, h] = keep.tile([P, PACK, HALF], F32, name="expd", tag="wx0%d" % h, align_bytes=64)
+            nc.scalar.activation(expd[0, h][:, 2 * u : 2 * u + 2, lo : lo + QUART], quarter_bank(q, u)[:], ACT.Exp)
 
         wo_q = held([P, 2 * N], U32, "wo_q")
         wo_s = held([P, 2 * N], U8, "wo_s")
@@ -284,13 +283,13 @@ def tile_list_predicate_join_cardinality_kernel(
                 bias=1.0,
             )
 
-        def scale_unit(g, j0, width):
-            if g == 0:
+        def scale_unit(g, j0, width, lo, hi):
+            if g == 0 and lo == 0:
                 h_bf[j0] = ring.tile([P, 2, width, PACK], BF16, name="h_bf", tag="bf", align_bytes=64, bufs=4)
             nc.vector.tensor_tensor(
-                h_bf[j0][:, g].rearrange("p j (u e) -> p j u e", u=2),
-                logs[g, j0].rearrange("p u j e -> p j u e"),
-                sel_c[:, g, :].rearrange("p (u e) -> p u e", u=2).unsqueeze(1).to_broadcast([P, width, 2, 2]),
+                h_bf[j0][:, g, lo:hi].rearrange("p j (u e) -> p j u e", u=2),
+                logs[g, j0 + lo].rearrange("p u j e -> p j u e"),
+                sel_c[:, g, :].rearrange("p (u e) -> p u e", u=2).unsqueeze(1).to_broadcast([P, hi - lo, 2, 2]),
                 MULT,
             )
 
@@ -305,27 +304,32 @@ def tile_list_predicate_join_cardinality_kernel(
             )
 
         def mm_out(g, j0, width):
+            apart = j0 + width == S
             if g == 0:
-                acc[j0] = psum.tile([P, 2, width], F32, name="acc", tag="bank%d" % len(acc))
+                if apart:
+                    acc[j0] = [psum.tile([P, width], F32, name="acc", tag="bank%d" % (6 + h))[:] for h in range(2)]
+                else:
+                    both = psum.tile([P, 2, width], F32, name="acc", tag="bank%d" % len(acc))
+                    acc[j0] = [both[:, h, :] for h in range(2)]
             for h in range(2):
                 m = slice(g * N + h * P, g * N + (h + 1) * P)
                 nc.tensor.matmul_mx(
-                    out=acc[j0][:, h, :],
+                    out=acc[j0][h],
                     lhsT=wo_q[:, m].bitcast(E4M3),
                     lhsT_scale=wo_s[:, m],
                     rhs=h_q[j0][:, g].bitcast(E4M3),
                     rhs_scale=h_s[j0][:, g],
-                    start=g == 0 and h == 0,
-                    stop=g == 1 and h == 1,
+                    start=g == 0 and (h == 0 or apart),
+                    stop=g == 1 and (h == 1 or apart),
                 )
 
         def store(j0, width):
             res = ring.tile([P, 2, width], F32, name="res", tag="wbf", align_bytes=64, bufs=4)
-            if j0 + width == S:
-                nc.vector.tensor_tensor(res[:], acc[j0][:], bo_t[:].unsqueeze(2).to_broadcast([P, 2, width]), ADD)
-            else:
-                for h in range(2):
-                    nc.scalar.activation(res[:, h, :], acc[j0][:, h, :], ACT.Identity, bias=bo_t[:, h : h + 1])
+            for h in range(2):
+                if j0 + width == S and h == 1:
+                    nc.vector.tensor_scalar_add(res[:, h, :], acc[j0][h], bo_t[:, h : h + 1])
+                else:
+                    nc.scalar.activation(res[:, h, :], acc[j0][h], ACT.Identity, bias=bo_t[:, h : h + 1])
             nc.sync.dma_start(out=out_rows[:, :, j0 : j0 + width], in_=res[:])
 
         nc.vector.tensor_copy(t_s[:], tabs[:].indirect(offs_t[:]))
@@ -348,25 +352,21 @@ def tile_list_predicate_join_cardinality_kernel(
         gather_x(1, 2, 0, HALF)
         gather_x(1, 2, HALF, S)
         quant_wx(0, 1, 0, PACK)
-        for t in range(PACK):
-            mm_tab(0, 0, t, True, False)
-        for q in (2, 3):
+        for q in range(4):
             for u in range(2):
                 quarter_tab(q, u)
-        for t in range(PACK):
-            mm_x(0, 0, t, 0, False, False)
-        for q in (2, 3):
+        for q in range(4):
             for u in range(2):
                 quarter_x(q, u, 0)
-        gather_x(1, 3, 0, HALF)
-        weave_x(1, QUART, HALF, "vector")
-        weave_x(1, 0, QUART, "scalar")
+        for q, engine in enumerate(("scalar", "vector")):
+            gather_x(1, 3, q * QUART, (q + 1) * QUART)
+            weave_x(1, q * QUART, (q + 1) * QUART, engine)
         weave_wx(1, 0, 0, 2, "scalar")
-        quant_x(1, QUART, HALF)
-        quant_x(1, 0, QUART)
-        for t in range(PACK):
-            mm_x(0, 0, t, 1, False, True)
-            exp_bank(0, 0, t)
+        for q in range(2):
+            quant_x(1, q * QUART, (q + 1) * QUART)
+            for u in range(2):
+                quarter_x(q, u, 1)
+                quarter_exp(q, u)
         for q in (2, 3):
             gather_x(1, 3, q * QUART, (q + 1) * QUART)
             weave_x(1, q * QUART, (q + 1) * QUART, "vector")
@@ -376,14 +376,14 @@ def tile_list_predicate_join_cardinality_kernel(
                 quarter_exp(q, u)
         for t in range(PACK):
             mm_tab(1, 0, t, True, False)
-        for t0 in (0, 2):
-            if t0 == 2:
-                weave_wx(1, 0, t0, t0 + 2, "vector")
-            weave_wx(1, 1, t0, t0 + 2, "vector")
+        for t0, t1 in ((0, 2), (2, 3), (3, 4)):
+            if t0 > 0:
+                weave_wx(1, 0, t0, t1, "vector")
+            weave_wx(1, 1, t0, t1, "vector")
             for a in range(2):
-                quant_wx(1, a, t0, t0 + 2)
+                quant_wx(1, a, t0, t1)
             for h in range(2):
-                for t in (t0, t0 + 1):
+                for t in range(t0, t1):
                     if h == 1:
                         mm_tab(1, h, t, True, False)
                     mm_x(1, h, t, 0, False, False)
@@ -397,19 +397,23 @@ def tile_list_predicate_join_cardinality_kernel(
             quant_unit(g0, g1, j0, width)
             for g in range(g0, g1):
                 mm_out(g, j0, width)
-            if g1 == 2:
-                store(j0, width)
 
-        for g in range(2):
-            log_unit(g, *steps[0])
+        lead = widths[0] // 2
+        log_unit(0, 0, lead)
+        log_unit(0, lead, lead)
+        log_unit(1, *steps[0])
         for n, step in enumerate(steps):
+            if n == 0:
+                scale_unit(0, *step, 0, lead)
             if n + 1 < len(steps):
                 log_unit(0, *steps[n + 1])
-            scale_unit(0, *step)
+            scale_unit(0, *step, lead if n == 0 else 0, step[1])
             if n > 0:
                 finish(0, 2, *steps[n - 1])
             if n + 1 < len(steps):
                 log_unit(1, *steps[n + 1])
-            scale_unit(1, *step)
+            scale_unit(1, *step, 0, step[1])
         finish(0, 1, *steps[-1])
         finish(1, 2, *steps[-1])
+        for step in steps:
+            store(*step)

@@ -21,6 +21,15 @@ PACK = 4
 KP = P * PACK
 HALF = S // 2
 QUART = S // 4
+PER_COLUMN = 16
+
+PLANE_BUFS = 7
+LOG_BUFS = 4
+WOVEN_BUFS = 4
+CODE_BUFS = 3
+STEP_WIDTHS = [128, 128, 256, 256, 128, 128]
+LEAD = STEP_WIDTHS[0] // 2
+LATE_RUNS = ((0, 2), (2, 3), (3, 4))
 
 
 def tile_list_predicate_join_cardinality_kernel(
@@ -29,16 +38,16 @@ def tile_list_predicate_join_cardinality_kernel(
     nc = tc.nc
     with ExitStack() as ctx:
         keep = ctx.enter_context(tc.tile_pool(name="keep", bufs=1))
-        big = ctx.enter_context(tc.tile_pool(name="big", bufs=7))
-        late = ctx.enter_context(tc.tile_pool(name="late", bufs=4))
+        plane_pool = ctx.enter_context(tc.tile_pool(name="planes", bufs=PLANE_BUFS))
+        late = ctx.enter_context(tc.tile_pool(name="late", bufs=LOG_BUFS))
         ring = ctx.enter_context(tc.tile_pool(name="ring", bufs=2))
         psum = ctx.enter_context(tc.psum_pool(name="psum", bufs=1))
 
         def held(shape, dtype, name):
             return keep.tile(shape, dtype, name=name, align_bytes=64)
 
-        offs2_t = keep.tile([P, S // 16], U16, name="offs2_t")
-        offs_t = keep.tile([P, S // 16], U16, name="offs_t")
+        offs2_t = keep.tile([P, S // PER_COLUMN], U16, name="offs2_t")
+        offs_t = keep.tile([P, S // PER_COLUMN], U16, name="offs_t")
         wk_raw = held([P, 2 * H], U8, "wk_raw")
         wks_raw = held([P, H], U8, "wks_raw")
         tabs = held([P, T], U8, "tabs")
@@ -50,9 +59,12 @@ def tile_list_predicate_join_cardinality_kernel(
         nc.vector.memset(tabs[:].bitcast(I32), 0)
         nc.vector.memset(wks_raw[:].bitcast(I32), 0)
 
-        def load_scales(engine, tile, rows, quadrants):
-            for q in quadrants:
-                engine.dma_start(out=tile[32 * q : 32 * q + 4, :].bitcast(I32), in_=rows[0, 4 * q : 4 * q + 4, :].bitcast(I32))
+        def load_scales(engine, tile, rows):
+            for quad in range(4):
+                engine.dma_start(
+                    out=tile[32 * quad : 32 * quad + 4, :].bitcast(I32),
+                    in_=rows[0, 4 * quad : 4 * quad + 4, :].bitcast(I32),
+                )
 
         x_rows = xT.rearrange("(a p i) d -> a i p d", a=2, i=PACK)
         wx_rows = wx.rearrange("(a p j) (g r) -> g a p j r", a=2, j=PACK, g=2)
@@ -60,29 +72,24 @@ def tile_list_predicate_join_cardinality_kernel(
         wx_raw = {}
 
         def load_plane(a, i):
-            planes[a, i] = big.tile([P, D], F32, name="plane", tag="big", align_bytes=64)
+            planes[a, i] = plane_pool.tile([P, D], F32, name="plane", tag="plane", align_bytes=64)
             nc.sync.dma_start(out=planes[a, i][:], in_=x_rows[a, i])
 
         def load_wx(g, a):
             wx_raw[g, a] = keep.tile([P, PACK, KP], F32, name="wx_raw", tag="wx%d%d" % (g, a), align_bytes=64)
             nc.sync.dma_start(out=wx_raw[g, a][:], in_=wx_rows[g, a])
 
-        def load_tab():
-            nc.sync.dma_start(out=tabw[:].bitcast(I32), in_=tab_words[0].rearrange("p t i -> p (t i)").bitcast(I32))
-
-        load_scales(nc.scalar, tabs, tab_scales, range(4))
+        load_scales(nc.scalar, tabs, tab_scales)
         nc.sync.dma_start(offs_t[:], offs)
-        load_tab()
+        nc.sync.dma_start(out=tabw[:].bitcast(I32), in_=tab_words[0].rearrange("p t i -> p (t i)").bitcast(I32))
         nc.sync.dma_start(offs2_t[:], offs2)
         nc.sync.dma_start(out=wgt_t[:], in_=wgt)
-        load_plane(0, 0)
-        load_plane(0, 1)
-        load_plane(0, 2)
+        for i in range(PACK):
+            load_plane(0, i)
         load_wx(0, 0)
-        load_plane(0, 3)
-        load_plane(1, 0)
         nc.sync.dma_start(out=wk_raw[:].bitcast(I32), in_=wk_words[0].bitcast(I32))
-        load_scales(nc.sync, wks_raw, wk_scales, range(4))
+        load_scales(nc.sync, wks_raw, wk_scales)
+        load_plane(1, 0)
         load_plane(1, 1)
         load_wx(0, 1)
         load_plane(1, 2)
@@ -97,19 +104,19 @@ def tile_list_predicate_join_cardinality_kernel(
         sel_runs = sel.rearrange("(g m k) -> m g k", g=2, k=8)
         for e in range(2):
             nc.sync.dma_start(out=sel_t[e::2, :, 0:7], in_=sel_runs[:, :, e : e + 7])
-        nc.sync.dma_start(out=bo_t[:], in_=bo.rearrange("(h p) -> p h", h=2))
+        nc.sync.dma_start(out=bo_t[:], in_=bo.rearrange("(y p) -> p y", y=2))
 
         wk_q = held([P, 2 * H], U8, "wk_q")
         wk_s = held([P, H], U8, "wk_s")
 
         def order_wk():
             nc.vector.tensor_copy(
-                out=wk_q[:].bitcast(I32).rearrange("p (g t c m) -> p g c t m", g=2, t=PACK, m=4),
-                in_=wk_raw[:].bitcast(I32).rearrange("p (g c m t) -> p g c t m", g=2, t=PACK, m=4),
+                out=wk_q[:].bitcast(I32).rearrange("p (g t w m) -> p g w t m", g=2, t=PACK, m=4),
+                in_=wk_raw[:].bitcast(I32).rearrange("p (g w m t) -> p g w t m", g=2, t=PACK, m=4),
             )
             nc.vector.tensor_copy(
-                out=wk_s[:].bitcast(U16).rearrange("p (g t c m) -> p g c t m", g=2, t=PACK, m=8),
-                in_=wks_raw[:].bitcast(U16).rearrange("p (g c m t) -> p g c t m", g=2, t=PACK, m=8),
+                out=wk_s[:].bitcast(U16).rearrange("p (g t w m) -> p g w t m", g=2, t=PACK, m=8),
+                in_=wks_raw[:].bitcast(U16).rearrange("p (g w m t) -> p g w t m", g=2, t=PACK, m=8),
             )
 
         def copy_on(engine, dst, src):
@@ -119,32 +126,37 @@ def tile_list_predicate_join_cardinality_kernel(
                 nc.scalar.copy(out=dst, in_=src)
 
         picked0 = keep.tile([P, PACK, S], F32, name="picked0", tag="picked0", align_bytes=64)
-        picked1 = [held([P, PACK, HALF], F32, "picked1%d" % h) for h in range(2)]
+        picked1 = [held([P, PACK, HALF], F32, "picked1%d" % half) for half in range(2)]
 
         def picks(a, lo, hi):
             if a == 0:
                 return picked0[:, :, lo:hi]
-            h = lo // HALF
-            return picked1[h][:, :, lo - h * HALF : hi - h * HALF]
+            half = lo // HALF
+            return picked1[half][:, :, lo - half * HALF : hi - half * HALF]
 
-        x_bf = {}
+        x_bf, x_bf_pass0 = {}, []
         x_q = [held([P, S], U32, "x_q0"), late.tile([P, S], U32, name="x_q1", tag="late", align_bytes=64)]
         x_s = [held([P, S], U8, "x_s0"), late.tile([P, S], U8, name="x_s1", tag="late", align_bytes=64)]
 
         def gather_x(a, i, lo, hi):
-            nc.vector.tensor_tensor(
-                picks(a, lo, hi)[:, i, :], planes[a, i][:].indirect(offs2_t[:, lo // 16 : hi // 16]), wgt_t[:, lo:hi], MULT
-            )
+            window = planes[a, i][:].indirect(offs2_t[:, lo // PER_COLUMN : hi // PER_COLUMN])
+            nc.vector.tensor_tensor(picks(a, lo, hi)[:, i, :], window, wgt_t[:, lo:hi], MULT)
 
         def weave_x(a, lo, hi, engine):
             if (a, lo) == (1, 0):
                 x_bf[a, lo] = picked1[1][:, PACK - 1, :].bitcast(BF16)
+            elif a == 0:
+                if lo == 0:
+                    x_bf_pass0.append(keep.tile([P, S * PACK], BF16, name="x_bf0", tag="wx00", align_bytes=64))
+                x_bf[a, lo] = x_bf_pass0[0][:, lo * PACK : hi * PACK]
             else:
-                x_bf[a, lo] = ring.tile([P, (hi - lo) * PACK], BF16, name="x_bf", tag="bf", align_bytes=64, bufs=4)[:]
+                x_bf[a, lo] = ring.tile(
+                    [P, (hi - lo) * PACK], BF16, name="x_bf", tag="bf", align_bytes=64, bufs=WOVEN_BUFS
+                )[:]
             copy_on(
                 engine,
-                x_bf[a, lo].rearrange("p (c i t) -> p c t i", i=2, t=PACK),
-                picks(a, lo, hi).rearrange("p t (c i) -> p c t i", i=2),
+                x_bf[a, lo].rearrange("p (w z i) -> p w i z", z=2, i=PACK),
+                picks(a, lo, hi).rearrange("p i (w z) -> p w i z", z=2),
             )
 
         def quant_x(a, lo, hi):
@@ -157,11 +169,11 @@ def tile_list_predicate_join_cardinality_kernel(
             if (g, a, t1) == (1, 1, PACK):
                 w_bf[g, a, t0] = keep.tile([P, width], BF16, name="w_bf_last", tag="wo_bf", align_bytes=64)
             else:
-                w_bf[g, a, t0] = ring.tile([P, width], BF16, name="w_bf", tag="wbf", align_bytes=64, bufs=4)
+                w_bf[g, a, t0] = ring.tile([P, width], BF16, name="w_bf", tag="wbf", align_bytes=64, bufs=WOVEN_BUFS)
             copy_on(
                 engine,
-                w_bf[g, a, t0][:].rearrange("p (t m e j) -> p m t j e", t=t1 - t0, e=2, j=PACK),
-                wx_raw[g, a][:].rearrange("p j (m t e) -> p m t j e", t=PACK, e=2)[:, :, t0:t1],
+                w_bf[g, a, t0][:].rearrange("p (t m e i) -> p m t i e", t=t1 - t0, e=2, i=PACK),
+                wx_raw[g, a][:].rearrange("p i (m t e) -> p m t i e", t=PACK, e=2)[:, :, t0:t1],
             )
 
         def quant_wx(g, a, t0, t1):
@@ -182,78 +194,81 @@ def tile_list_predicate_join_cardinality_kernel(
 
         banks, expd = {}, {}
 
-        def bank(g, h, t):
-            if (g, h, t) not in banks:
-                banks[g, h, t] = psum.tile([P, HALF], F32, name="bank", tag="bank%d" % (PACK * h + t))
-            return banks[g, h, t][:]
-
-        def mm_x(g, h, t, a, first, last):
-            cols = slice(h * HALF, (h + 1) * HALF)
-            nc.tensor.matmul_mx(
-                out=bank(g, h, t),
-                lhsT=w_q[g, a, t].bitcast(E4M3),
-                lhsT_scale=w_s[g, a, t],
-                rhs=x_q[a][:, cols].bitcast(E4M3),
-                rhs_scale=x_s[a][:, cols],
-                start=first,
-                stop=last,
-            )
-
-        def mm_tab(g, h, t, first, last):
-            c0 = g * KP + t * P
-            nc.tensor.matmul_mx(
-                out=bank(g, h, t),
-                lhsT=wk_q[:, 2 * c0 : 2 * (c0 + P)].bitcast(E2M1),
-                lhsT_scale=wk_s[:, c0 : c0 + P],
-                rhs=t_q[:, h * HALF : (h + 1) * HALF].bitcast(E4M3),
-                rhs_scale=t_s[:, h * HALF : (h + 1) * HALF],
-                start=first,
-                stop=last,
-            )
-
-        def exp_bank(g, h, t):
-            if (g, h) not in expd:
-                expd[g, h] = keep.tile([P, PACK, HALF], F32, name="expd", tag=("wx00", "wx01", "picked0", "tabw")[2 * g + h], align_bytes=64)
-            nc.scalar.activation(expd[g, h][:, t, :], bank(g, h, t), ACT.Exp)
+        def exp_tile(g, half):
+            if (g, half) not in expd:
+                tag = (("wx00", "wx01"), ("picked0", "tabw"))[g][half]
+                expd[g, half] = keep.tile([P, PACK, HALF], F32, name="expd", tag=tag, align_bytes=64)
+            return expd[g, half]
 
         def quarter_bank(q, u):
-            if (q, u) not in banks:
-                banks[q, u] = psum.tile([P, 2, QUART], F32, name="bank", tag="bank%d" % (2 * q + u))
-            return banks[q, u]
+            if ("quarter", q, u) not in banks:
+                banks["quarter", q, u] = psum.tile([P, 2, QUART], F32, name="bank", tag="bank%d" % (2 * q + u))
+            return banks["quarter", q, u]
 
         def quarter_tab(q, u):
-            for e in range(2):
-                c0 = (2 * u + e) * P
-                for k in range(2):
-                    cols = slice(q * QUART + k * P, q * QUART + (k + 1) * P)
+            for s in range(2):
+                c0 = (2 * u + s) * P
+                for part in range(QUART // P):
+                    cols = slice(q * QUART + part * P, q * QUART + (part + 1) * P)
                     nc.tensor.matmul_mx(
-                        out=quarter_bank(q, u)[:, e, k * P : (k + 1) * P],
+                        out=quarter_bank(q, u)[:, s, part * P : (part + 1) * P],
                         lhsT=wk_q[:, 2 * c0 : 2 * (c0 + P)].bitcast(E2M1),
                         lhsT_scale=wk_s[:, c0 : c0 + P],
                         rhs=t_q[:, cols].bitcast(E4M3),
                         rhs_scale=t_s[:, cols],
-                        start=e == 0 and k == 0,
+                        start=s == 0 and part == 0,
                         stop=False,
                     )
 
         def quarter_x(q, u, a):
             cols = slice(q * QUART, (q + 1) * QUART)
-            for e in range(2):
+            for s in range(2):
                 nc.tensor.matmul_mx(
-                    out=quarter_bank(q, u)[:, e, :],
-                    lhsT=w_q[0, a, 2 * u + e].bitcast(E4M3),
-                    lhsT_scale=w_s[0, a, 2 * u + e],
+                    out=quarter_bank(q, u)[:, s, :],
+                    lhsT=w_q[0, a, 2 * u + s].bitcast(E4M3),
+                    lhsT_scale=w_s[0, a, 2 * u + s],
                     rhs=x_q[a][:, cols].bitcast(E4M3),
                     rhs_scale=x_s[a][:, cols],
                     start=False,
-                    stop=a == 1 and e == 1,
+                    stop=a == 1 and s == 1,
                 )
 
         def quarter_exp(q, u):
-            h, lo = divmod(q * QUART, HALF)
-            if (0, h) not in expd:
-                expd[0, h] = keep.tile([P, PACK, HALF], F32, name="expd", tag="wx0%d" % h, align_bytes=64)
-            nc.scalar.activation(expd[0, h][:, 2 * u : 2 * u + 2, lo : lo + QUART], quarter_bank(q, u)[:], ACT.Exp)
+            half, lo = divmod(q * QUART, HALF)
+            nc.scalar.activation(exp_tile(0, half)[:, 2 * u : 2 * u + 2, lo : lo + QUART], quarter_bank(q, u)[:], ACT.Exp)
+
+        def half_bank(half, t):
+            if ("half", half, t) not in banks:
+                banks["half", half, t] = psum.tile([P, HALF], F32, name="bank", tag="bank%d" % (PACK * half + t))
+            return banks["half", half, t][:]
+
+        def half_tab(half, t):
+            c0 = KP + t * P
+            cols = slice(half * HALF, (half + 1) * HALF)
+            nc.tensor.matmul_mx(
+                out=half_bank(half, t),
+                lhsT=wk_q[:, 2 * c0 : 2 * (c0 + P)].bitcast(E2M1),
+                lhsT_scale=wk_s[:, c0 : c0 + P],
+                rhs=t_q[:, cols].bitcast(E4M3),
+                rhs_scale=t_s[:, cols],
+                start=True,
+                stop=False,
+            )
+
+        def half_x(half, t, a):
+            cols = slice(half * HALF, (half + 1) * HALF)
+            nc.tensor.matmul_mx(
+                out=half_bank(half, t),
+                lhsT=w_q[1, a, t].bitcast(E4M3),
+                lhsT_scale=w_s[1, a, t],
+                rhs=x_q[a][:, cols].bitcast(E4M3),
+                rhs_scale=x_s[a][:, cols],
+                start=False,
+                stop=a == 1,
+            )
+
+        def half_exp(half, t):
+            nc.scalar.activation(exp_tile(1, half)[:, t, :], half_bank(half, t), ACT.Exp)
 
         wo_q = held([P, 2 * N], U32, "wo_q")
         wo_s = held([P, 2 * N], U8, "wo_s")
@@ -263,94 +278,93 @@ def tile_list_predicate_join_cardinality_kernel(
             wo_bf = keep.tile([P, 2, N * PACK], BF16, name="wo_bf", tag="wo_bf", align_bytes=64)
             for g in range(2):
                 nc.vector.tensor_copy(
-                    out=wo_bf[:, g, :].rearrange("p (c i j) -> p c j i", i=2, j=PACK),
-                    in_=wo_raw[g][:].rearrange("p j (c i) -> p c j i", i=2),
+                    out=wo_bf[:, g, :].rearrange("p (w z t) -> p w t z", z=2, t=PACK),
+                    in_=wo_raw[g][:].rearrange("p t (w z) -> p w t z", z=2),
                 )
             nc.vector.tensor_copy(out=sel_c[:], in_=sel_t[:, :, 0:7:2])
-            nc.vector.quantize_mx(out=wo_q[:].bitcast(E4M3), scales=wo_s[:], in_=wo_bf[:].rearrange("p g c -> p (g c)"))
+            nc.vector.quantize_mx(out=wo_q[:].bitcast(E4M3), scales=wo_s[:], in_=wo_bf[:].rearrange("p g w -> p (g w)"))
 
-        out_rows = out.rearrange("(h p) j -> p h j", h=2)
+        out_rows = out.rearrange("(y p) j -> p y j", y=2)
         logs, h_bf, h_q, h_s, acc = {}, {}, {}, {}, {}
 
-        def log_unit(g, j0, width):
-            h, lo = divmod(j0, HALF)
-            whole = late.tile([P, 2, width, 2], F32, name="logs", tag="late", align_bytes=64)
-            logs[g, j0] = whole[:]
+        def take_log(g, j0, width):
+            half, lo = divmod(j0, HALF)
+            logs[g, j0] = late.tile([P, 2, width, 2], F32, name="logs", tag="late", align_bytes=64)
             nc.scalar.activation(
-                whole[:],
-                expd[g, h][:, :, lo : lo + width].rearrange("p (u e) j -> p u j e", u=2),
+                logs[g, j0][:],
+                expd[g, half][:, :, lo : lo + width].rearrange("p (u s) j -> p u j s", u=2),
                 ACT.Ln,
                 bias=1.0,
             )
 
-        def scale_unit(g, j0, width, lo, hi):
+        def times_sel(g, j0, width, lo, hi):
             if g == 0 and lo == 0:
-                h_bf[j0] = ring.tile([P, 2, width, PACK], BF16, name="h_bf", tag="bf", align_bytes=64, bufs=4)
+                h_bf[j0] = ring.tile([P, 2, width, PACK], BF16, name="h_bf", tag="bf", align_bytes=64, bufs=WOVEN_BUFS)
             nc.vector.tensor_tensor(
-                h_bf[j0][:, g, lo:hi].rearrange("p j (u e) -> p j u e", u=2),
-                logs[g, j0 + lo].rearrange("p u j e -> p j u e"),
-                sel_c[:, g, :].rearrange("p (u e) -> p u e", u=2).unsqueeze(1).to_broadcast([P, hi - lo, 2, 2]),
+                h_bf[j0][:, g, lo:hi].rearrange("p j (u s) -> p j u s", u=2),
+                logs[g, j0 + lo][:].rearrange("p u j s -> p j u s"),
+                sel_c[:, g, :].rearrange("p (u s) -> p u s", u=2).unsqueeze(1).to_broadcast([P, hi - lo, 2, 2]),
                 MULT,
-            )
-
-        def quant_unit(g0, g1, j0, width):
-            if g0 == 0:
-                h_q[j0] = ring.tile([P, 2, width], U32, name="h_q", align_bytes=64, bufs=3)
-                h_s[j0] = ring.tile([P, 2, width], U8, name="h_s", align_bytes=64, bufs=3)
-            nc.vector.quantize_mx(
-                out=h_q[j0][:, g0:g1].rearrange("p g j -> p (g j)").bitcast(E4M3),
-                scales=h_s[j0][:, g0:g1].rearrange("p g j -> p (g j)"),
-                in_=h_bf[j0][:, g0:g1].rearrange("p g j t -> p (g j t)"),
             )
 
         def mm_out(g, j0, width):
             apart = j0 + width == S
             if g == 0:
                 if apart:
-                    acc[j0] = [psum.tile([P, width], F32, name="acc", tag="bank%d" % (6 + h))[:] for h in range(2)]
+                    acc[j0] = [psum.tile([P, width], F32, name="acc", tag="bank%d" % (6 + y))[:] for y in range(2)]
                 else:
                     both = psum.tile([P, 2, width], F32, name="acc", tag="bank%d" % len(acc))
-                    acc[j0] = [both[:, h, :] for h in range(2)]
-            for h in range(2):
-                m = slice(g * N + h * P, g * N + (h + 1) * P)
+                    acc[j0] = [both[:, y, :] for y in range(2)]
+            for y in range(2):
+                cols = slice(g * N + y * P, g * N + (y + 1) * P)
                 nc.tensor.matmul_mx(
-                    out=acc[j0][h],
-                    lhsT=wo_q[:, m].bitcast(E4M3),
-                    lhsT_scale=wo_s[:, m],
+                    out=acc[j0][y],
+                    lhsT=wo_q[:, cols].bitcast(E4M3),
+                    lhsT_scale=wo_s[:, cols],
                     rhs=h_q[j0][:, g].bitcast(E4M3),
                     rhs_scale=h_s[j0][:, g],
-                    start=g == 0 and (h == 0 or apart),
-                    stop=g == 1 and (h == 1 or apart),
+                    start=g == 0 and (y == 0 or apart),
+                    stop=g == 1 and (y == 1 or apart),
                 )
 
+        def quant_and_multiply(g0, g1, j0, width):
+            if g0 == 0:
+                h_q[j0] = ring.tile([P, 2, width], U32, name="h_q", align_bytes=64, bufs=CODE_BUFS)
+                h_s[j0] = ring.tile([P, 2, width], U8, name="h_s", align_bytes=64, bufs=CODE_BUFS)
+            nc.vector.quantize_mx(
+                out=h_q[j0][:, g0:g1].rearrange("p g j -> p (g j)").bitcast(E4M3),
+                scales=h_s[j0][:, g0:g1].rearrange("p g j -> p (g j)"),
+                in_=h_bf[j0][:, g0:g1].rearrange("p g j t -> p (g j t)"),
+            )
+            for g in range(g0, g1):
+                mm_out(g, j0, width)
+
         def store(j0, width):
-            res = ring.tile([P, 2, width], F32, name="res", tag="wbf", align_bytes=64, bufs=4)
-            for h in range(2):
-                if j0 + width == S and h == 1:
-                    nc.vector.tensor_scalar_add(res[:, h, :], acc[j0][h], bo_t[:, h : h + 1])
+            res = ring.tile([P, 2, width], F32, name="res", tag="wbf", align_bytes=64, bufs=WOVEN_BUFS)
+            for y in range(2):
+                if j0 + width == S and y == 1:
+                    nc.vector.tensor_scalar_add(res[:, y, :], acc[j0][y], bo_t[:, y : y + 1])
                 else:
-                    nc.scalar.activation(res[:, h, :], acc[j0][h], ACT.Identity, bias=bo_t[:, h : h + 1])
+                    nc.scalar.activation(res[:, y, :], acc[j0][y], ACT.Identity, bias=bo_t[:, y : y + 1])
             nc.sync.dma_start(out=out_rows[:, :, j0 : j0 + width], in_=res[:])
 
         nc.vector.tensor_copy(t_s[:], tabs[:].indirect(offs_t[:]))
         nc.vector.tensor_copy(t_q[:], tabw[:].indirect(offs_t[:]))
-        gather_x(0, 0, 0, S)
-        for i in range(1, PACK):
+        for i in range(PACK):
             gather_x(0, i, 0, S)
-        gather_x(1, 0, 0, HALF)
-        gather_x(1, 0, HALF, S)
         weave_wx(0, 0, 0, PACK, "scalar")
-        for h in range(2):
-            weave_x(0, h * HALF, (h + 1) * HALF, "scalar")
+        for lo in (0, HALF):
+            weave_x(0, lo, lo + HALF, "scalar")
         weave_wx(0, 1, 0, PACK, "scalar")
-        quant_wx(0, 0, 0, PACK)
-        quant_x(0, 0, HALF)
         order_wk()
-        quant_x(0, HALF, S)
-        gather_x(1, 1, 0, HALF)
-        gather_x(1, 1, HALF, S)
-        gather_x(1, 2, 0, HALF)
-        gather_x(1, 2, HALF, S)
+        quant_wx(0, 0, 0, PACK)
+        for lo in (0, HALF):
+            gather_x(1, 0, lo, lo + HALF)
+        for lo in (0, HALF):
+            quant_x(0, lo, lo + HALF)
+        for i in (1, 2):
+            for lo in (0, HALF):
+                gather_x(1, i, lo, lo + HALF)
         quant_wx(0, 1, 0, PACK)
         for q in range(4):
             for u in range(2):
@@ -358,62 +372,57 @@ def tile_list_predicate_join_cardinality_kernel(
         for q in range(4):
             for u in range(2):
                 quarter_x(q, u, 0)
+
+        def close_quarter(q):
+            quant_x(1, q * QUART, (q + 1) * QUART)
+            for u in range(2):
+                quarter_x(q, u, 1)
+                quarter_exp(q, u)
+
         for q, engine in enumerate(("scalar", "vector")):
-            gather_x(1, 3, q * QUART, (q + 1) * QUART)
+            gather_x(1, PACK - 1, q * QUART, (q + 1) * QUART)
             weave_x(1, q * QUART, (q + 1) * QUART, engine)
-        weave_wx(1, 0, 0, 2, "scalar")
+        weave_wx(1, 0, *LATE_RUNS[0], "scalar")
         for q in range(2):
-            quant_x(1, q * QUART, (q + 1) * QUART)
-            for u in range(2):
-                quarter_x(q, u, 1)
-                quarter_exp(q, u)
+            close_quarter(q)
         for q in (2, 3):
-            gather_x(1, 3, q * QUART, (q + 1) * QUART)
+            gather_x(1, PACK - 1, q * QUART, (q + 1) * QUART)
             weave_x(1, q * QUART, (q + 1) * QUART, "vector")
-            quant_x(1, q * QUART, (q + 1) * QUART)
-            for u in range(2):
-                quarter_x(q, u, 1)
-                quarter_exp(q, u)
+            close_quarter(q)
+
         for t in range(PACK):
-            mm_tab(1, 0, t, True, False)
-        for t0, t1 in ((0, 2), (2, 3), (3, 4)):
+            half_tab(0, t)
+        for t0, t1 in LATE_RUNS:
             if t0 > 0:
                 weave_wx(1, 0, t0, t1, "vector")
             weave_wx(1, 1, t0, t1, "vector")
             for a in range(2):
                 quant_wx(1, a, t0, t1)
-            for h in range(2):
+            for half in range(2):
                 for t in range(t0, t1):
-                    if h == 1:
-                        mm_tab(1, h, t, True, False)
-                    mm_x(1, h, t, 0, False, False)
-                    mm_x(1, h, t, 1, False, True)
-                    exp_bank(1, h, t)
+                    if half == 1:
+                        half_tab(half, t)
+                    for a in range(2):
+                        half_x(half, t, a)
+                    half_exp(half, t)
         quant_wo()
-        widths = [128, 128, 256, 256, 128, 128]
-        steps = [(sum(widths[:n]), width) for n, width in enumerate(widths)]
 
-        def finish(g0, g1, j0, width):
-            quant_unit(g0, g1, j0, width)
-            for g in range(g0, g1):
-                mm_out(g, j0, width)
-
-        lead = widths[0] // 2
-        log_unit(0, 0, lead)
-        log_unit(0, lead, lead)
-        log_unit(1, *steps[0])
-        for n, step in enumerate(steps):
-            if n == 0:
-                scale_unit(0, *step, 0, lead)
-            if n + 1 < len(steps):
-                log_unit(0, *steps[n + 1])
-            scale_unit(0, *step, lead if n == 0 else 0, step[1])
+        steps = [(sum(STEP_WIDTHS[:n]), width) for n, width in enumerate(STEP_WIDTHS)]
+        take_log(0, 0, LEAD)
+        take_log(0, LEAD, LEAD)
+        take_log(1, *steps[0])
+        times_sel(0, *steps[0], 0, LEAD)
+        for n, (j0, width) in enumerate(steps):
+            ahead = steps[n + 1 : n + 2]
+            for step in ahead:
+                take_log(0, *step)
+            times_sel(0, j0, width, LEAD if n == 0 else 0, width)
             if n > 0:
-                finish(0, 2, *steps[n - 1])
-            if n + 1 < len(steps):
-                log_unit(1, *steps[n + 1])
-            scale_unit(1, *step, 0, step[1])
-        finish(0, 1, *steps[-1])
-        finish(1, 2, *steps[-1])
+                quant_and_multiply(0, 2, *steps[n - 1])
+            for step in ahead:
+                take_log(1, *step)
+            times_sel(1, j0, width, 0, width)
+        for g in range(2):
+            quant_and_multiply(g, g + 1, *steps[-1])
         for step in steps:
             store(*step)

@@ -1,6 +1,7 @@
 from contextlib import ExitStack
 
 import concourse.mybir as mybir
+from concourse.masks import make_identity
 
 K, C, H, N, T, D, S = 512, 1024, 1024, 256, 2048, 2048, 1024
 FLOPS = 2 * S * (C * H + K * H + H * N)
@@ -21,15 +22,16 @@ PACK = 4
 KP = P * PACK
 HALF = S // 2
 QUART = S // 4
+SCALE_ROWS = 16
 PER_COLUMN = 16
 
-PLANE_BUFS = 7
+PLANE_BUFS = 6
 LOG_BUFS = 4
 WOVEN_BUFS = 4
 CODE_BUFS = 3
 STEP_WIDTHS = [128, 128, 256, 256, 128, 128]
 LEAD = STEP_WIDTHS[0] // 2
-LATE_RUNS = ((0, 2), (2, 3), (3, 4))
+LATE_RUNS = ((0, 1), (1, 2), (2, 3), (3, 4))
 
 
 def tile_list_predicate_join_cardinality_kernel(
@@ -52,16 +54,22 @@ def tile_list_predicate_join_cardinality_kernel(
         wks_raw = held([P, H], U8, "wks_raw")
         tabs = held([P, T], U8, "tabs")
         tabw = keep.tile([P, T], U32, name="tabw", tag="tabw", align_bytes=64)
-        wgt_t = held([P, S], F32, "wgt_t")
+        wgt_all = held([P, S], F32, "wgt_all")
         sel_t = held([P, 2, 8], F32, "sel_t")
         bo_t = held([P, 2], F32, "bo_t")
 
         nc.vector.memset(tabs[:].bitcast(I32), 0)
+        ident = held([P, P], F32, "ident")
+        nc.vector.memset(ident[:].bitcast(I32), 0)
+        make_identity(nc, ident[:], nomemset=True)
         nc.vector.memset(wks_raw[:].bitcast(I32), 0)
+        t_s = held([P, S], U8, "t_s")
+        nc.vector.memset(t_s[:].bitcast(I32), 0)
+        wgt_part = held([P, QUART], F32, "wgt_part")
 
-        def load_scales(engine, tile, rows):
+        def load_scales(engines, tile, rows):
             for quad in range(4):
-                engine.dma_start(
+                engines[quad % 2].dma_start(
                     out=tile[32 * quad : 32 * quad + 4, :].bitcast(I32),
                     in_=rows[0, 4 * quad : 4 * quad + 4, :].bitcast(I32),
                 )
@@ -79,21 +87,31 @@ def tile_list_predicate_join_cardinality_kernel(
             wx_raw[g, a] = keep.tile([P, PACK, KP], F32, name="wx_raw", tag="wx%d%d" % (g, a), align_bytes=64)
             nc.sync.dma_start(out=wx_raw[g, a][:], in_=wx_rows[g, a])
 
-        load_scales(nc.scalar, tabs, tab_scales)
+        wgt_by_quarter = wgt.rearrange("(k q) (c j) -> q c k j", q=4, c=4)
+        for q in range(4):
+            nc.scalar.dma_start(out=wgt_part[q::4, :], in_=wgt_by_quarter[q, q])
         nc.sync.dma_start(offs_t[:], offs)
-        nc.sync.dma_start(out=tabw[:].bitcast(I32), in_=tab_words[0].rearrange("p t i -> p (t i)").bitcast(I32))
         nc.sync.dma_start(offs2_t[:], offs2)
-        nc.sync.dma_start(out=wgt_t[:], in_=wgt)
-        for i in range(PACK):
-            load_plane(0, i)
-        load_wx(0, 0)
-        nc.sync.dma_start(out=wk_raw[:].bitcast(I32), in_=wk_words[0].bitcast(I32))
-        load_scales(nc.sync, wks_raw, wk_scales)
+        nc.sync.dma_start(out=tabs[0:SCALE_ROWS, :].bitcast(I32), in_=tab_scales[0].bitcast(I32))
+        nc.sync.dma_start(out=tabw[:].bitcast(I32), in_=tab_words[0].rearrange("p t i -> p (t i)").bitcast(I32))
+        load_plane(0, 0)
+        load_plane(0, 1)
+        load_plane(0, 2)
+        t_s_rows = held([P, S], U8, "t_s_rows")
+        nc.vector.tensor_copy(t_s_rows[:], tabs[:].indirect(offs_t[:]))
+        for quad in range(4):
+            nc.sync.dma_start(
+                out=t_s[32 * quad : 32 * quad + 4, :].bitcast(I32), in_=t_s_rows[4 * quad : 4 * quad + 4, :].bitcast(I32)
+            )
+        load_plane(0, 3)
         load_plane(1, 0)
+        nc.sync.dma_start(out=wk_raw[:].bitcast(I32), in_=wk_words[0].bitcast(I32))
+        load_scales((nc.sync, nc.sync), wks_raw, wk_scales)
         load_plane(1, 1)
-        load_wx(0, 1)
+        load_wx(0, 0)
         load_plane(1, 2)
         load_plane(1, 3)
+        load_wx(0, 1)
         load_wx(1, 0)
         load_wx(1, 1)
         wo_raw = [held([P, PACK, N], F32, "wo_raw%d" % g) for g in range(2)]
@@ -126,41 +144,46 @@ def tile_list_predicate_join_cardinality_kernel(
                 nc.scalar.copy(out=dst, in_=src)
 
         picked0 = keep.tile([P, PACK, S], F32, name="picked0", tag="picked0", align_bytes=64)
-        picked1 = [held([P, PACK, HALF], F32, "picked1%d" % half) for half in range(2)]
+        picked_early = held([P, 2, S], F32, "picked_early")
+        picked_late = [held([P, 2, HALF], F32, "picked_late%d" % half) for half in range(2)]
 
-        def picks(a, lo, hi):
+        def picks(a, i, lo, hi):
             if a == 0:
-                return picked0[:, :, lo:hi]
+                return picked0[:, i, lo:hi]
+            if i < 2:
+                return picked_early[:, i, lo:hi]
             half = lo // HALF
-            return picked1[half][:, :, lo - half * HALF : hi - half * HALF]
+            return picked_late[half][:, i - 2, lo - half * HALF : hi - half * HALF]
 
-        x_bf, x_bf_pass0 = {}, []
+        x_bf = {}
         x_q = [held([P, S], U32, "x_q0"), late.tile([P, S], U32, name="x_q1", tag="late", align_bytes=64)]
         x_s = [held([P, S], U8, "x_s0"), late.tile([P, S], U8, name="x_s1", tag="late", align_bytes=64)]
 
         def gather_x(a, i, lo, hi):
             window = planes[a, i][:].indirect(offs2_t[:, lo // PER_COLUMN : hi // PER_COLUMN])
-            nc.vector.tensor_tensor(picks(a, lo, hi)[:, i, :], window, wgt_t[:, lo:hi], MULT)
+            nc.vector.tensor_tensor(picks(a, i, lo, hi), window, wgt_all[:, lo:hi], MULT)
 
-        def weave_x(a, lo, hi, engine):
-            if (a, lo) == (1, 0):
-                x_bf[a, lo] = picked1[1][:, PACK - 1, :].bitcast(BF16)
-            elif a == 0:
-                if lo == 0:
-                    x_bf_pass0.append(keep.tile([P, S * PACK], BF16, name="x_bf0", tag="wx00", align_bytes=64))
-                x_bf[a, lo] = x_bf_pass0[0][:, lo * PACK : hi * PACK]
+        def woven(a):
+            if a not in x_bf:
+                x_bf[a] = keep.tile([P, S * PACK], BF16, name="x_bf", tag=("x_bf0", "wx00")[a], align_bytes=64)
+            return x_bf[a]
+
+        def weave_x(a, lo, hi, i0, i1, engine):
+            if a == 0:
+                rows = picked0[:, :, lo:hi]
+            elif i0 == 0:
+                rows = picked_early[:, :, lo:hi]
             else:
-                x_bf[a, lo] = ring.tile(
-                    [P, (hi - lo) * PACK], BF16, name="x_bf", tag="bf", align_bytes=64, bufs=WOVEN_BUFS
-                )[:]
+                half = lo // HALF
+                rows = picked_late[half][:, :, lo - half * HALF : hi - half * HALF]
             copy_on(
                 engine,
-                x_bf[a, lo].rearrange("p (w z i) -> p w i z", z=2, i=PACK),
-                picks(a, lo, hi).rearrange("p i (w z) -> p w i z", z=2),
+                woven(a)[:, lo * PACK : hi * PACK].rearrange("p (w z i) -> p w i z", z=2, i=PACK)[:, :, i0:i1],
+                rows.rearrange("p i (w z) -> p w i z", z=2),
             )
 
         def quant_x(a, lo, hi):
-            nc.vector.quantize_mx(out=x_q[a][:, lo:hi].bitcast(E4M3), scales=x_s[a][:, lo:hi], in_=x_bf[a, lo])
+            nc.vector.quantize_mx(out=x_q[a][:, lo:hi].bitcast(E4M3), scales=x_s[a][:, lo:hi], in_=x_bf[a][:, lo * PACK : hi * PACK])
 
         w_bf, w_q, w_s = {}, {}, {}
 
@@ -168,6 +191,8 @@ def tile_list_predicate_join_cardinality_kernel(
             width = (t1 - t0) * P * PACK
             if (g, a, t1) == (1, 1, PACK):
                 w_bf[g, a, t0] = keep.tile([P, width], BF16, name="w_bf_last", tag="wo_bf", align_bytes=64)
+            elif (g, a, t0) == (0, 1, 0):
+                w_bf[g, a, t0] = picked_late[1][:, 1, :].bitcast(BF16)
             else:
                 w_bf[g, a, t0] = ring.tile([P, width], BF16, name="w_bf", tag="wbf", align_bytes=64, bufs=WOVEN_BUFS)
             copy_on(
@@ -190,13 +215,12 @@ def tile_list_predicate_join_cardinality_kernel(
             nc.vector.quantize_mx(out=codes[:].bitcast(E4M3), scales=scales[:], in_=w_bf[g, a, t0][:])
 
         t_q = held([P, S], U32, "t_q")
-        t_s = held([P, S], U8, "t_s")
 
         banks, expd = {}, {}
 
         def exp_tile(g, half):
             if (g, half) not in expd:
-                tag = (("wx00", "wx01"), ("picked0", "tabw"))[g][half]
+                tag = (("x_bf0", "wx01"), ("picked0", "tabw"))[g][half]
                 expd[g, half] = keep.tile([P, PACK, HALF], F32, name="expd", tag=tag, align_bytes=64)
             return expd[g, half]
 
@@ -348,24 +372,43 @@ def tile_list_predicate_join_cardinality_kernel(
                     nc.scalar.activation(res[:, y, :], acc[j0][y], ACT.Identity, bias=bo_t[:, y : y + 1])
             nc.sync.dma_start(out=out_rows[:, :, j0 : j0 + width], in_=res[:])
 
-        nc.vector.tensor_copy(t_s[:], tabs[:].indirect(offs_t[:]))
+        def spread_wgt():
+            turned = keep.tile([P, 4, 2, P // 4, 4], F32, name="wgt_turned", tag="picked0", align_bytes=64)
+            by_query = psum.tile([P, 2, P], F32, name="by_query", tag="bank0")
+            for b in range(2):
+                nc.tensor.transpose(by_query[:, b, :], wgt_part[:, b * P : (b + 1) * P], ident[:])
+            for half in range(2):
+                pieces = by_query[:].rearrange("p b (k q) -> p q b k", q=4)[:, 2 * half : 2 * half + 2]
+                nc.scalar.copy(
+                    out=turned[:, 2 * half : 2 * half + 2], in_=pieces.unsqueeze(4).to_broadcast([P, 2, 2, P // 4, 4])
+                )
+            for half in range(2):
+                spread = psum.tile([P, PACK, P], F32, name="spread", tag="bank%d" % (2 + half))
+                for b in range(PACK):
+                    nc.tensor.transpose(
+                        spread[:, b, :], turned[:, 2 * half + b // 2, b % 2].rearrange("p k r -> p (k r)"), ident[:]
+                    )
+                nc.scalar.copy(
+                    out=wgt_all[:, half * HALF : (half + 1) * HALF], in_=spread[:].rearrange("p b j -> p (b j)")
+                )
+
+        spread_wgt()
         nc.vector.tensor_copy(t_q[:], tabw[:].indirect(offs_t[:]))
         for i in range(PACK):
             gather_x(0, i, 0, S)
+        for lo in (0, HALF):
+            weave_x(0, lo, lo + HALF, 0, PACK, "scalar")
+        gather_x(1, 0, 0, S)
+        order_wk()
+        quant_x(0, 0, HALF)
+        gather_x(1, 1, 0, S)
+        quant_x(0, HALF, S)
         weave_wx(0, 0, 0, PACK, "scalar")
         for lo in (0, HALF):
-            weave_x(0, lo, lo + HALF, "scalar")
-        weave_wx(0, 1, 0, PACK, "scalar")
-        order_wk()
+            weave_x(1, lo, lo + HALF, 0, 2, "scalar")
         quant_wx(0, 0, 0, PACK)
         for lo in (0, HALF):
-            gather_x(1, 0, lo, lo + HALF)
-        for lo in (0, HALF):
-            quant_x(0, lo, lo + HALF)
-        for i in (1, 2):
-            for lo in (0, HALF):
-                gather_x(1, i, lo, lo + HALF)
-        quant_wx(0, 1, 0, PACK)
+            gather_x(1, 2, lo, lo + HALF)
         for q in range(4):
             for u in range(2):
                 quarter_tab(q, u)
@@ -373,28 +416,32 @@ def tile_list_predicate_join_cardinality_kernel(
             for u in range(2):
                 quarter_x(q, u, 0)
 
-        def close_quarter(q):
+        def finish_x(q):
+            gather_x(1, PACK - 1, q * QUART, (q + 1) * QUART)
+            weave_x(1, q * QUART, (q + 1) * QUART, 2, PACK, "scalar" if q == 0 else "vector")
             quant_x(1, q * QUART, (q + 1) * QUART)
-            for u in range(2):
-                quarter_x(q, u, 1)
-                quarter_exp(q, u)
 
-        for q, engine in enumerate(("scalar", "vector")):
-            gather_x(1, PACK - 1, q * QUART, (q + 1) * QUART)
-            weave_x(1, q * QUART, (q + 1) * QUART, engine)
-        weave_wx(1, 0, *LATE_RUNS[0], "scalar")
+        def close(q, u):
+            quarter_x(q, u, 1)
+            quarter_exp(q, u)
+
         for q in range(2):
-            close_quarter(q)
+            finish_x(q)
+        for u in range(2):
+            weave_wx(0, 1, 2 * u, 2 * u + 2, "scalar")
+        for u in range(2):
+            quant_wx(0, 1, 2 * u, 2 * u + 2)
+            for q in range(2):
+                close(q, u)
         for q in (2, 3):
-            gather_x(1, PACK - 1, q * QUART, (q + 1) * QUART)
-            weave_x(1, q * QUART, (q + 1) * QUART, "vector")
-            close_quarter(q)
+            finish_x(q)
+            for u in range(2):
+                close(q, u)
 
         for t in range(PACK):
             half_tab(0, t)
         for t0, t1 in LATE_RUNS:
-            if t0 > 0:
-                weave_wx(1, 0, t0, t1, "vector")
+            weave_wx(1, 0, t0, t1, "vector")
             weave_wx(1, 1, t0, t1, "vector")
             for a in range(2):
                 quant_wx(1, a, t0, t1)

@@ -29,9 +29,8 @@ PLANE_BUFS = 6
 LOG_BUFS = 4
 WOVEN_BUFS = 4
 CODE_BUFS = 3
-STEP_WIDTHS = [128, 128, 256, 256, 128, 128]
+STEP_WIDTHS = [128, 128, 128, 128, 256, 128, 128]
 LEAD = STEP_WIDTHS[0] // 2
-LATE_RUNS = ((0, 1), (1, 2), (2, 3), (3, 4))
 
 
 def tile_list_predicate_join_cardinality_kernel(
@@ -366,11 +365,14 @@ def tile_list_predicate_join_cardinality_kernel(
         def store(j0, width):
             res = ring.tile([P, 2, width], F32, name="res", tag="wbf", align_bytes=64, bufs=WOVEN_BUFS)
             for y in range(2):
-                if j0 + width == S and y == 1:
+                if j0 + width == S and y == 0:
                     nc.vector.tensor_scalar_add(res[:, y, :], acc[j0][y], bo_t[:, y : y + 1])
                 else:
                     nc.scalar.activation(res[:, y, :], acc[j0][y], ACT.Identity, bias=bo_t[:, y : y + 1])
-            nc.sync.dma_start(out=out_rows[:, :, j0 : j0 + width], in_=res[:])
+                if j0 + width == S:
+                    (nc.sync, nc.scalar)[y].dma_start(out=out_rows[:, y, j0 : j0 + width], in_=res[:, y, :])
+            if j0 + width < S:
+                nc.sync.dma_start(out=out_rows[:, :, j0 : j0 + width], in_=res[:])
 
         def spread_wgt():
             turned = keep.tile([P, 4, 2, P // 4, 4], F32, name="wgt_turned", tag="picked0", align_bytes=64)
@@ -433,6 +435,8 @@ def tile_list_predicate_join_cardinality_kernel(
             quant_wx(0, 1, 2 * u, 2 * u + 2)
             for q in range(2):
                 close(q, u)
+            if u == 0:
+                weave_wx(1, 0, 0, 2, "scalar")
         for q in (2, 3):
             finish_x(q)
             for u in range(2):
@@ -440,18 +444,19 @@ def tile_list_predicate_join_cardinality_kernel(
 
         for t in range(PACK):
             half_tab(0, t)
-        for t0, t1 in LATE_RUNS:
-            weave_wx(1, 0, t0, t1, "vector")
-            weave_wx(1, 1, t0, t1, "vector")
-            for a in range(2):
-                quant_wx(1, a, t0, t1)
+        for t in range(PACK):
+            if t == 2:
+                weave_wx(1, 0, 2, PACK, "vector")
+            weave_wx(1, 1, t, t + 1, "vector")
+            if t % 2 == 0:
+                quant_wx(1, 0, t, t + 2)
+            quant_wx(1, 1, t, t + 1)
             for half in range(2):
-                for t in range(t0, t1):
-                    if half == 1:
-                        half_tab(half, t)
-                    for a in range(2):
-                        half_x(half, t, a)
-                    half_exp(half, t)
+                if half == 1:
+                    half_tab(half, t)
+                for a in range(2):
+                    half_x(half, t, a)
+                half_exp(half, t)
         quant_wo()
 
         steps = [(sum(STEP_WIDTHS[:n]), width) for n, width in enumerate(STEP_WIDTHS)]

@@ -25,11 +25,12 @@ QUART = S // 4
 SCALE_ROWS = 16
 PER_COLUMN = 16
 
-PLANE_BUFS = 6
+PLANE_BUFS = 5
 LOG_BUFS = 4
 WOVEN_BUFS = 4
 CODE_BUFS = 3
 STEP_WIDTHS = [128, 128, 128, 128, 256, 128, 128]
+STORE_WIDTHS = [256, 256, 256, 128, 128]
 LEAD = STEP_WIDTHS[0] // 2
 
 
@@ -77,10 +78,15 @@ def tile_list_predicate_join_cardinality_kernel(
         wx_rows = wx.rearrange("(a p j) (g r) -> g a p j r", a=2, j=PACK, g=2)
         planes = {}
         wx_raw = {}
+        wx01_raw = []
 
         def load_plane(a, i):
             planes[a, i] = plane_pool.tile([P, D], F32, name="plane", tag="plane", align_bytes=64)
             nc.sync.dma_start(out=planes[a, i][:], in_=x_rows[a, i])
+
+        def load_wx01(part):
+            wx01_raw.append(held([P, PACK, KP // 2], F32, "wx01_raw%d" % part))
+            nc.sync.dma_start(out=wx01_raw[part][:], in_=wx_rows[0, 1][:, :, part * (KP // 2) : (part + 1) * (KP // 2)])
 
         def load_wx(g, a):
             wx_raw[g, a] = keep.tile([P, PACK, KP], F32, name="wx_raw", tag="wx%d%d" % (g, a), align_bytes=64)
@@ -104,13 +110,14 @@ def tile_list_predicate_join_cardinality_kernel(
             )
         load_plane(0, 3)
         load_plane(1, 0)
+        load_plane(1, 1)
         nc.sync.dma_start(out=wk_raw[:].bitcast(I32), in_=wk_words[0].bitcast(I32))
         load_scales((nc.sync, nc.sync), wks_raw, wk_scales)
-        load_plane(1, 1)
         load_wx(0, 0)
         load_plane(1, 2)
+        load_wx01(0)
         load_plane(1, 3)
-        load_wx(0, 1)
+        load_wx01(1)
         load_wx(1, 0)
         load_wx(1, 1)
         wo_raw = [held([P, PACK, N], F32, "wo_raw%d" % g) for g in range(2)]
@@ -143,16 +150,8 @@ def tile_list_predicate_join_cardinality_kernel(
                 nc.scalar.copy(out=dst, in_=src)
 
         picked0 = keep.tile([P, PACK, S], F32, name="picked0", tag="picked0", align_bytes=64)
-        picked_early = held([P, 2, S], F32, "picked_early")
-        picked_late = [held([P, 2, HALF], F32, "picked_late%d" % half) for half in range(2)]
-
-        def picks(a, i, lo, hi):
-            if a == 0:
-                return picked0[:, i, lo:hi]
-            if i < 2:
-                return picked_early[:, i, lo:hi]
-            half = lo // HALF
-            return picked_late[half][:, i - 2, lo - half * HALF : hi - half * HALF]
+        picked1_flat = held([P, PACK * S + HALF], F32, "picked1")
+        picked = [picked0[:], picked1_flat[:, 0 : PACK * S].rearrange("p (i j) -> p i j", i=PACK)]
 
         x_bf = {}
         x_q = [held([P, S], U32, "x_q0"), late.tile([P, S], U32, name="x_q1", tag="late", align_bytes=64)]
@@ -160,7 +159,7 @@ def tile_list_predicate_join_cardinality_kernel(
 
         def gather_x(a, i, lo, hi):
             window = planes[a, i][:].indirect(offs2_t[:, lo // PER_COLUMN : hi // PER_COLUMN])
-            nc.vector.tensor_tensor(picks(a, i, lo, hi), window, wgt_all[:, lo:hi], MULT)
+            nc.vector.tensor_tensor(picked[a][:, i, lo:hi], window, wgt_all[:, lo:hi], MULT)
 
         def woven(a):
             if a not in x_bf:
@@ -168,17 +167,10 @@ def tile_list_predicate_join_cardinality_kernel(
             return x_bf[a]
 
         def weave_x(a, lo, hi, i0, i1, engine):
-            if a == 0:
-                rows = picked0[:, :, lo:hi]
-            elif i0 == 0:
-                rows = picked_early[:, :, lo:hi]
-            else:
-                half = lo // HALF
-                rows = picked_late[half][:, :, lo - half * HALF : hi - half * HALF]
             copy_on(
                 engine,
                 woven(a)[:, lo * PACK : hi * PACK].rearrange("p (w z i) -> p w i z", z=2, i=PACK)[:, :, i0:i1],
-                rows.rearrange("p i (w z) -> p w i z", z=2),
+                picked[a][:, i0:i1, lo:hi].rearrange("p i (w z) -> p w i z", z=2),
             )
 
         def quant_x(a, lo, hi):
@@ -190,14 +182,23 @@ def tile_list_predicate_join_cardinality_kernel(
             width = (t1 - t0) * P * PACK
             if (g, a, t1) == (1, 1, PACK):
                 w_bf[g, a, t0] = keep.tile([P, width], BF16, name="w_bf_last", tag="wo_bf", align_bytes=64)
-            elif (g, a, t0) == (0, 1, 0):
-                w_bf[g, a, t0] = picked_late[1][:, 1, :].bitcast(BF16)
             else:
                 w_bf[g, a, t0] = ring.tile([P, width], BF16, name="w_bf", tag="wbf", align_bytes=64, bufs=WOVEN_BUFS)
             copy_on(
                 engine,
                 w_bf[g, a, t0][:].rearrange("p (t m e i) -> p m t i e", t=t1 - t0, e=2, i=PACK),
                 wx_raw[g, a][:].rearrange("p i (m t e) -> p m t i e", t=PACK, e=2)[:, :, t0:t1],
+            )
+
+        wx01_bf = picked1_flat[:, PACK * S - HALF :].bitcast(BF16)
+        for t0 in (0, 2):
+            w_bf[0, 1, t0] = wx01_bf[:, t0 * P * PACK : (t0 + 2) * P * PACK]
+
+        def weave_wx01(part, t0, t1):
+            m = P // 4
+            nc.scalar.copy(
+                out=wx01_bf.rearrange("p (t m e i) -> p m t i e", t=PACK, e=2, i=PACK)[:, part * m : (part + 1) * m, t0:t1],
+                in_=wx01_raw[part][:].rearrange("p i (m t e) -> p m t i e", t=PACK, e=2)[:, :, t0:t1],
             )
 
         def quant_wx(g, a, t0, t1):
@@ -219,7 +220,7 @@ def tile_list_predicate_join_cardinality_kernel(
 
         def exp_tile(g, half):
             if (g, half) not in expd:
-                tag = (("x_bf0", "wx01"), ("picked0", "tabw"))[g][half]
+                tag = (("x_bf0", "expd01"), ("picked0", "tabw"))[g][half]
                 expd[g, half] = keep.tile([P, PACK, HALF], F32, name="expd", tag=tag, align_bytes=64)
             return expd[g, half]
 
@@ -309,6 +310,7 @@ def tile_list_predicate_join_cardinality_kernel(
 
         out_rows = out.rearrange("(y p) j -> p y j", y=2)
         logs, h_bf, h_q, h_s, acc = {}, {}, {}, {}, {}
+        stores = [(sum(STORE_WIDTHS[:n]), width) for n, width in enumerate(STORE_WIDTHS)]
 
         def take_log(g, j0, width):
             half, lo = divmod(j0, HALF)
@@ -331,23 +333,24 @@ def tile_list_predicate_join_cardinality_kernel(
             )
 
         def mm_out(g, j0, width):
-            apart = j0 + width == S
-            if g == 0:
+            n, (s0, span) = [(n, store) for n, store in enumerate(stores) if store[0] <= j0][-1]
+            apart = s0 + span == S
+            if s0 not in acc:
                 if apart:
-                    acc[j0] = [psum.tile([P, width], F32, name="acc", tag="bank%d" % (6 + y))[:] for y in range(2)]
+                    acc[s0] = [psum.tile([P, span], F32, name="acc", tag="bank%d" % (6 + y))[:] for y in range(2)]
                 else:
-                    both = psum.tile([P, 2, width], F32, name="acc", tag="bank%d" % len(acc))
-                    acc[j0] = [both[:, y, :] for y in range(2)]
+                    both = psum.tile([P, 2, span], F32, name="acc", tag="bank%d" % n)
+                    acc[s0] = [both[:, y, :] for y in range(2)]
             for y in range(2):
                 cols = slice(g * N + y * P, g * N + (y + 1) * P)
                 nc.tensor.matmul_mx(
-                    out=acc[j0][y],
+                    out=acc[s0][y][:, j0 - s0 : j0 - s0 + width],
                     lhsT=wo_q[:, cols].bitcast(E4M3),
                     lhsT_scale=wo_s[:, cols],
                     rhs=h_q[j0][:, g].bitcast(E4M3),
                     rhs_scale=h_s[j0][:, g],
-                    start=g == 0 and (y == 0 or apart),
-                    stop=g == 1 and (y == 1 or apart),
+                    start=j0 == s0 and g == 0 and (y == 0 or apart),
+                    stop=j0 + width == s0 + span and g == 1 and (y == 1 or apart),
                 )
 
         def quant_and_multiply(g0, g1, j0, width):
@@ -398,19 +401,19 @@ def tile_list_predicate_join_cardinality_kernel(
         nc.vector.tensor_copy(t_q[:], tabw[:].indirect(offs_t[:]))
         for i in range(PACK):
             gather_x(0, i, 0, S)
+            if i == 1:
+                weave_x(0, 0, S, 0, 2, "scalar")
         for lo in (0, HALF):
-            weave_x(0, lo, lo + HALF, 0, PACK, "scalar")
+            weave_x(0, lo, lo + HALF, 2, PACK, "scalar")
         gather_x(1, 0, 0, S)
-        order_wk()
         quant_x(0, 0, HALF)
         gather_x(1, 1, 0, S)
+        order_wk()
         quant_x(0, HALF, S)
         weave_wx(0, 0, 0, PACK, "scalar")
-        for lo in (0, HALF):
-            weave_x(1, lo, lo + HALF, 0, 2, "scalar")
+        weave_x(1, 0, S - QUART, 0, 2, "scalar")
         quant_wx(0, 0, 0, PACK)
-        for lo in (0, HALF):
-            gather_x(1, 2, lo, lo + HALF)
+        gather_x(1, 2, 0, S)
         for q in range(4):
             for u in range(2):
                 quarter_tab(q, u)
@@ -420,23 +423,22 @@ def tile_list_predicate_join_cardinality_kernel(
 
         def finish_x(q):
             gather_x(1, PACK - 1, q * QUART, (q + 1) * QUART)
-            weave_x(1, q * QUART, (q + 1) * QUART, 2, PACK, "scalar" if q == 0 else "vector")
+            weave_x(1, q * QUART, (q + 1) * QUART, 2 if q < 3 else 0, PACK, "scalar" if q == 0 else "vector")
             quant_x(1, q * QUART, (q + 1) * QUART)
 
         def close(q, u):
             quarter_x(q, u, 1)
             quarter_exp(q, u)
 
+        weave_wx01(0, 0, PACK)
         for q in range(2):
             finish_x(q)
         for u in range(2):
-            weave_wx(0, 1, 2 * u, 2 * u + 2, "scalar")
+            weave_wx01(1, 2 * u, 2 * u + 2)
         for u in range(2):
             quant_wx(0, 1, 2 * u, 2 * u + 2)
             for q in range(2):
                 close(q, u)
-            if u == 0:
-                weave_wx(1, 0, 0, 2, "scalar")
         for q in (2, 3):
             finish_x(q)
             for u in range(2):
@@ -445,12 +447,10 @@ def tile_list_predicate_join_cardinality_kernel(
         for t in range(PACK):
             half_tab(0, t)
         for t in range(PACK):
-            if t == 2:
-                weave_wx(1, 0, 2, PACK, "vector")
-            weave_wx(1, 1, t, t + 1, "vector")
-            if t % 2 == 0:
-                quant_wx(1, 0, t, t + 2)
-            quant_wx(1, 1, t, t + 1)
+            for a in range(2):
+                weave_wx(1, a, t, t + 1, "vector")
+            for a in range(2):
+                quant_wx(1, a, t, t + 1)
             for half in range(2):
                 if half == 1:
                     half_tab(half, t)
@@ -476,5 +476,5 @@ def tile_list_predicate_join_cardinality_kernel(
             times_sel(1, j0, width, 0, width)
         for g in range(2):
             quant_and_multiply(g, g + 1, *steps[-1])
-        for step in steps:
-            store(*step)
+        for span in stores:
+            store(*span)

@@ -24,6 +24,7 @@ HALF = S // 2
 QUART = S // 4
 SCALE_ROWS = 16
 PER_COLUMN = 16
+GROUPS = 8
 
 PLANE_BUFS = 5
 LOG_BUFS = 4
@@ -45,8 +46,8 @@ def tile_list_predicate_join_cardinality_kernel(
         ring = ctx.enter_context(tc.tile_pool(name="ring", bufs=2))
         psum = ctx.enter_context(tc.psum_pool(name="psum", bufs=1))
 
-        def held(shape, dtype, name):
-            return keep.tile(shape, dtype, name=name, align_bytes=64)
+        def held(shape, dtype, name, tag=None):
+            return keep.tile(shape, dtype, name=name, tag=tag or name, align_bytes=64)
 
         offs2_t = keep.tile([P, S // PER_COLUMN], U16, name="offs2_t")
         offs_t = keep.tile([P, S // PER_COLUMN], U16, name="offs_t")
@@ -58,21 +59,15 @@ def tile_list_predicate_join_cardinality_kernel(
         sel_t = held([P, 2, 8], F32, "sel_t")
         bo_t = held([P, 2], F32, "bo_t")
 
-        nc.vector.memset(tabs[:].bitcast(I32), 0)
+        nc.vector.memset(tabs[32:64, :].bitcast(I32), 0)
+        nc.vector.memset(tabs[64:P, :].bitcast(I32), 0)
         ident = held([P, P], F32, "ident")
         nc.vector.memset(ident[:].bitcast(I32), 0)
         make_identity(nc, ident[:], nomemset=True)
         nc.vector.memset(wks_raw[:].bitcast(I32), 0)
         t_s = held([P, S], U8, "t_s")
         nc.vector.memset(t_s[:].bitcast(I32), 0)
-        wgt_part = held([P, QUART], F32, "wgt_part")
-
-        def load_scales(engines, tile, rows):
-            for quad in range(4):
-                engines[quad % 2].dma_start(
-                    out=tile[32 * quad : 32 * quad + 4, :].bitcast(I32),
-                    in_=rows[0, 4 * quad : 4 * quad + 4, :].bitcast(I32),
-                )
+        wgt_part = held([P, P], F32, "wgt_part")
 
         x_rows = xT.rearrange("(a p i) d -> a i p d", a=2, i=PACK)
         wx_rows = wx.rearrange("(a p j) (g r) -> g a p j r", a=2, j=PACK, g=2)
@@ -92,27 +87,36 @@ def tile_list_predicate_join_cardinality_kernel(
             wx_raw[g, a] = keep.tile([P, PACK, KP], F32, name="wx_raw", tag="wx%d%d" % (g, a), align_bytes=64)
             nc.sync.dma_start(out=wx_raw[g, a][:], in_=wx_rows[g, a])
 
-        wgt_by_quarter = wgt.rearrange("(k q) (c j) -> q c k j", q=4, c=4)
-        for q in range(4):
-            nc.scalar.dma_start(out=wgt_part[q::4, :], in_=wgt_by_quarter[q, q])
+        nc.scalar.dma_start(out=wgt_part[:], in_=wgt.rearrange("(g x) (c j) -> g (x c) j", g=GROUPS, j=P)[:, 0:16, :])
         nc.sync.dma_start(offs_t[:], offs)
-        nc.sync.dma_start(offs2_t[:], offs2)
-        nc.sync.dma_start(out=tabs[0:SCALE_ROWS, :].bitcast(I32), in_=tab_scales[0].bitcast(I32))
+        nc.sync.dma_start(out=tabs[0:32, :].bitcast(I32), in_=tab_scales.bitcast(I32).to_broadcast([2, SCALE_ROWS, T // 4]))
         nc.sync.dma_start(out=tabw[:].bitcast(I32), in_=tab_words[0].rearrange("p t i -> p (t i)").bitcast(I32))
-        load_plane(0, 0)
-        load_plane(0, 1)
-        load_plane(0, 2)
         t_s_rows = held([P, S], U8, "t_s_rows")
         nc.vector.tensor_copy(t_s_rows[:], tabs[:].indirect(offs_t[:]))
-        for quad in range(4):
+
+        def carry(quad):
             nc.sync.dma_start(
-                out=t_s[32 * quad : 32 * quad + 4, :].bitcast(I32), in_=t_s_rows[4 * quad : 4 * quad + 4, :].bitcast(I32)
+                out=t_s[32 * quad : 32 * quad + 4, :].bitcast(I32), in_=t_s_rows[8 * (quad // 2 * 3) + 4 * (quad % 2) :][0:4, :].bitcast(I32)
             )
-        load_plane(0, 3)
-        load_plane(1, 0)
-        load_plane(1, 1)
+
+        def load_wks(quad):
+            nc.sync.dma_start(
+                out=wks_raw[32 * quad : 32 * quad + 4, :].bitcast(I32), in_=wk_scales[0, 4 * quad : 4 * quad + 4, :].bitcast(I32)
+            )
+
+        nc.sync.dma_start(offs2_t[:], offs2)
+        load_plane(0, 0)
         nc.sync.dma_start(out=wk_raw[:].bitcast(I32), in_=wk_words[0].bitcast(I32))
-        load_scales((nc.sync, nc.sync), wks_raw, wk_scales)
+        load_wks(0)
+        for i in range(1, PACK):
+            load_wks(i)
+            load_plane(0, i)
+        load_plane(1, 0)
+        carry(0)
+        carry(1)
+        carry(2)
+        load_plane(1, 1)
+        carry(3)
         load_wx(0, 0)
         load_plane(1, 2)
         load_wx01(0)
@@ -134,11 +138,11 @@ def tile_list_predicate_join_cardinality_kernel(
         wk_s = held([P, H], U8, "wk_s")
 
         def order_wk():
-            nc.vector.tensor_copy(
-                out=wk_q[:].bitcast(I32).rearrange("p (g t w m) -> p g w t m", g=2, t=PACK, m=4),
-                in_=wk_raw[:].bitcast(I32).rearrange("p (g w m t) -> p g w t m", g=2, t=PACK, m=4),
+            nc.scalar.copy(
+                out=wk_q[:].bitcast(U32).rearrange("p (g t w m) -> p g w t m", g=2, t=PACK, m=4),
+                in_=wk_raw[:].bitcast(U32).rearrange("p (g w m t) -> p g w t m", g=2, t=PACK, m=4),
             )
-            nc.vector.tensor_copy(
+            nc.scalar.copy(
                 out=wk_s[:].bitcast(U16).rearrange("p (g t w m) -> p g w t m", g=2, t=PACK, m=8),
                 in_=wks_raw[:].bitcast(U16).rearrange("p (g w m t) -> p g w t m", g=2, t=PACK, m=8),
             )
@@ -155,7 +159,14 @@ def tile_list_predicate_join_cardinality_kernel(
 
         x_bf = {}
         x_q = [held([P, S], U32, "x_q0"), late.tile([P, S], U32, name="x_q1", tag="late", align_bytes=64)]
-        x_s = [held([P, S], U8, "x_s0"), late.tile([P, S], U8, name="x_s1", tag="late", align_bytes=64)]
+        after_carry = held([P, 2, HALF], U8, "after_carry", "t_s_rows")
+        x_s_first = held([P, HALF], U8, "x_s0")
+        x_s_last = late.tile([P, S], U8, name="x_s1", tag="late", align_bytes=64)
+
+        def x_s(a, lo, hi):
+            if a == 1:
+                return x_s_last[:, lo:hi]
+            return x_s_first[:, lo:hi] if lo < HALF else after_carry[:, 0, lo - HALF : hi - HALF]
 
         def gather_x(a, i, lo, hi):
             window = planes[a, i][:].indirect(offs2_t[:, lo // PER_COLUMN : hi // PER_COLUMN])
@@ -174,7 +185,7 @@ def tile_list_predicate_join_cardinality_kernel(
             )
 
         def quant_x(a, lo, hi):
-            nc.vector.quantize_mx(out=x_q[a][:, lo:hi].bitcast(E4M3), scales=x_s[a][:, lo:hi], in_=x_bf[a][:, lo * PACK : hi * PACK])
+            nc.vector.quantize_mx(out=x_q[a][:, lo:hi].bitcast(E4M3), scales=x_s(a, lo, hi), in_=x_bf[a][:, lo * PACK : hi * PACK])
 
         w_bf, w_q, w_s = {}, {}, {}
 
@@ -205,14 +216,14 @@ def tile_list_predicate_join_cardinality_kernel(
             width = (t1 - t0) * P
             if (g, a, t1) == (1, 1, PACK):
                 codes = late.tile([P, width], U32, name="w_q_late", tag="late", align_bytes=64)
-                scales = late.tile([P, width], U8, name="w_s_late", tag="late", align_bytes=64)
+                scales = late.tile([P, width], U8, name="w_s_late", tag="late", align_bytes=64)[:]
             else:
                 codes = held([P, width], U32, "w_q%d%d%d" % (g, a, t0))
-                scales = held([P, width], U8, "w_s%d%d%d" % (g, a, t0))
+                scales = after_carry[:, 1] if (g, a) == (0, 0) else held([P, width], U8, "w_s%d%d%d" % (g, a, t0))[:]
             for t in range(t0, t1):
                 w_q[g, a, t] = codes[:, (t - t0) * P : (t - t0 + 1) * P]
                 w_s[g, a, t] = scales[:, (t - t0) * P : (t - t0 + 1) * P]
-            nc.vector.quantize_mx(out=codes[:].bitcast(E4M3), scales=scales[:], in_=w_bf[g, a, t0][:])
+            nc.vector.quantize_mx(out=codes[:].bitcast(E4M3), scales=scales, in_=w_bf[g, a, t0][:])
 
         t_q = held([P, S], U32, "t_q")
 
@@ -230,19 +241,18 @@ def tile_list_predicate_join_cardinality_kernel(
             return banks["quarter", q, u]
 
         def quarter_tab(q, u):
+            cols = slice(q * QUART, (q + 1) * QUART)
             for s in range(2):
                 c0 = (2 * u + s) * P
-                for part in range(QUART // P):
-                    cols = slice(q * QUART + part * P, q * QUART + (part + 1) * P)
-                    nc.tensor.matmul_mx(
-                        out=quarter_bank(q, u)[:, s, part * P : (part + 1) * P],
-                        lhsT=wk_q[:, 2 * c0 : 2 * (c0 + P)].bitcast(E2M1),
-                        lhsT_scale=wk_s[:, c0 : c0 + P],
-                        rhs=t_q[:, cols].bitcast(E4M3),
-                        rhs_scale=t_s[:, cols],
-                        start=s == 0 and part == 0,
-                        stop=False,
-                    )
+                nc.tensor.matmul_mx(
+                    out=quarter_bank(q, u)[:, s, :],
+                    lhsT=wk_q[:, 2 * c0 : 2 * (c0 + P)].bitcast(E2M1),
+                    lhsT_scale=wk_s[:, c0 : c0 + P],
+                    rhs=t_q[:, cols].bitcast(E4M3),
+                    rhs_scale=t_s[:, cols],
+                    start=s == 0,
+                    stop=False,
+                )
 
         def quarter_x(q, u, a):
             cols = slice(q * QUART, (q + 1) * QUART)
@@ -252,7 +262,7 @@ def tile_list_predicate_join_cardinality_kernel(
                     lhsT=w_q[0, a, 2 * u + s].bitcast(E4M3),
                     lhsT_scale=w_s[0, a, 2 * u + s],
                     rhs=x_q[a][:, cols].bitcast(E4M3),
-                    rhs_scale=x_s[a][:, cols],
+                    rhs_scale=x_s(a, cols.start, cols.stop),
                     start=False,
                     stop=a == 1 and s == 1,
                 )
@@ -286,7 +296,7 @@ def tile_list_predicate_join_cardinality_kernel(
                 lhsT=w_q[1, a, t].bitcast(E4M3),
                 lhsT_scale=w_s[1, a, t],
                 rhs=x_q[a][:, cols].bitcast(E4M3),
-                rhs_scale=x_s[a][:, cols],
+                rhs_scale=x_s(a, cols.start, cols.stop),
                 start=False,
                 stop=a == 1,
             )
@@ -378,21 +388,19 @@ def tile_list_predicate_join_cardinality_kernel(
                 nc.sync.dma_start(out=out_rows[:, :, j0 : j0 + width], in_=res[:])
 
         def spread_wgt():
-            turned = keep.tile([P, 4, 2, P // 4, 4], F32, name="wgt_turned", tag="picked0", align_bytes=64)
-            by_query = psum.tile([P, 2, P], F32, name="by_query", tag="bank0")
-            for b in range(2):
-                nc.tensor.transpose(by_query[:, b, :], wgt_part[:, b * P : (b + 1) * P], ident[:])
+            turned = [held([P, PACK, 16, 8], F32, "wgt_turned", tag) for tag in ("picked0", "wk_q")]
+            by_query = psum.tile([P, P], F32, name="by_query", tag="bank0")
+            nc.tensor.transpose(by_query[:], wgt_part[:], ident[:])
+            runs = by_query[:].rearrange("p (r c) -> p c r", c=GROUPS)
             for half in range(2):
-                pieces = by_query[:].rearrange("p b (k q) -> p q b k", q=4)[:, 2 * half : 2 * half + 2]
                 nc.scalar.copy(
-                    out=turned[:, 2 * half : 2 * half + 2], in_=pieces.unsqueeze(4).to_broadcast([P, 2, 2, P // 4, 4])
+                    out=turned[half][:],
+                    in_=runs[:, 4 * half : 4 * half + 4].unsqueeze(3).to_broadcast([P, 4, 16, 8]),
                 )
             for half in range(2):
                 spread = psum.tile([P, PACK, P], F32, name="spread", tag="bank%d" % (2 + half))
                 for b in range(PACK):
-                    nc.tensor.transpose(
-                        spread[:, b, :], turned[:, 2 * half + b // 2, b % 2].rearrange("p k r -> p (k r)"), ident[:]
-                    )
+                    nc.tensor.transpose(spread[:, b, :], turned[half][:, b].rearrange("p r k -> p (r k)"), ident[:])
                 nc.scalar.copy(
                     out=wgt_all[:, half * HALF : (half + 1) * HALF], in_=spread[:].rearrange("p b j -> p (b j)")
                 )
@@ -403,12 +411,12 @@ def tile_list_predicate_join_cardinality_kernel(
             gather_x(0, i, 0, S)
             if i == 1:
                 weave_x(0, 0, S, 0, 2, "scalar")
-        for lo in (0, HALF):
-            weave_x(0, lo, lo + HALF, 2, PACK, "scalar")
+        weave_x(0, 0, HALF + P, 2, PACK, "scalar")
+        weave_x(0, HALF + P, S, 2, PACK, "scalar")
         gather_x(1, 0, 0, S)
         quant_x(0, 0, HALF)
-        gather_x(1, 1, 0, S)
         order_wk()
+        gather_x(1, 1, 0, S)
         quant_x(0, HALF, S)
         weave_wx(0, 0, 0, PACK, "scalar")
         weave_x(1, 0, S - QUART, 0, 2, "scalar")

@@ -87,16 +87,16 @@ def tile_list_predicate_join_cardinality_kernel(
             wx_raw[g, a] = keep.tile([P, PACK, KP], F32, name="wx_raw", tag="wx%d%d" % (g, a), align_bytes=64)
             nc.sync.dma_start(out=wx_raw[g, a][:], in_=wx_rows[g, a])
 
-        nc.scalar.dma_start(out=wgt_part[:], in_=wgt.rearrange("(g x) (c j) -> g (x c) j", g=GROUPS, j=P)[:, 0:16, :])
+        nc.scalar.dma_start(out=wgt_part[:], in_=wgt.rearrange("(g x) (c j) -> (x c) g j", g=GROUPS, j=P)[0:16])
         nc.sync.dma_start(offs_t[:], offs)
-        nc.sync.dma_start(out=tabs[0:32, :].bitcast(I32), in_=tab_scales.bitcast(I32).to_broadcast([2, SCALE_ROWS, T // 4]))
+        nc.sync.dma_start(out=tabs[0:32, :].bitcast(I32), in_=tab_scales[0].bitcast(I32).unsqueeze(1).to_broadcast([SCALE_ROWS, 2, T // 4]))
         nc.sync.dma_start(out=tabw[:].bitcast(I32), in_=tab_words[0].rearrange("p t i -> p (t i)").bitcast(I32))
         t_s_rows = held([P, S], U8, "t_s_rows")
         nc.vector.tensor_copy(t_s_rows[:], tabs[:].indirect(offs_t[:]))
 
         def carry(quad):
             nc.sync.dma_start(
-                out=t_s[32 * quad : 32 * quad + 4, :].bitcast(I32), in_=t_s_rows[8 * (quad // 2 * 3) + 4 * (quad % 2) :][0:4, :].bitcast(I32)
+                out=t_s[32 * quad : 32 * quad + 4, :].bitcast(I32), in_=t_s_rows[8 * quad + quad % 2 : 8 * quad + 8 : 2, :].bitcast(I32)
             )
 
         def load_wks(quad):
@@ -119,8 +119,8 @@ def tile_list_predicate_join_cardinality_kernel(
         carry(3)
         load_wx(0, 0)
         load_plane(1, 2)
-        load_wx01(0)
         load_plane(1, 3)
+        load_wx01(0)
         load_wx01(1)
         load_wx(1, 0)
         load_wx(1, 1)
@@ -391,11 +391,11 @@ def tile_list_predicate_join_cardinality_kernel(
             turned = [held([P, PACK, 16, 8], F32, "wgt_turned", tag) for tag in ("picked0", "wk_q")]
             by_query = psum.tile([P, P], F32, name="by_query", tag="bank0")
             nc.tensor.transpose(by_query[:], wgt_part[:], ident[:])
-            runs = by_query[:].rearrange("p (r c) -> p c r", c=GROUPS)
+            runs = by_query[:].rearrange("p (x c g) -> p c g x", x=2, g=GROUPS)
             for half in range(2):
                 nc.scalar.copy(
-                    out=turned[half][:],
-                    in_=runs[:, 4 * half : 4 * half + 4].unsqueeze(3).to_broadcast([P, 4, 16, 8]),
+                    out=turned[half][:].rearrange("p c (g x) k -> p c g x k", x=2),
+                    in_=runs[:, 4 * half : 4 * half + 4].unsqueeze(4).to_broadcast([P, 4, GROUPS, 2, 8]),
                 )
             for half in range(2):
                 spread = psum.tile([P, PACK, P], F32, name="spread", tag="bank%d" % (2 + half))
@@ -431,7 +431,7 @@ def tile_list_predicate_join_cardinality_kernel(
 
         def finish_x(q):
             gather_x(1, PACK - 1, q * QUART, (q + 1) * QUART)
-            weave_x(1, q * QUART, (q + 1) * QUART, 2 if q < 3 else 0, PACK, "scalar" if q == 0 else "vector")
+            weave_x(1, q * QUART, (q + 1) * QUART, 2 if q < 3 else 0, PACK, "vector")
             quant_x(1, q * QUART, (q + 1) * QUART)
 
         def close(q, u):

@@ -156,6 +156,12 @@ def tile_list_predicate_join_cardinality_kernel(
         picked0 = keep.tile([P, PACK, S], F32, name="picked0", tag="picked0", align_bytes=64)
         picked1_flat = held([P, PACK * S + HALF], F32, "picked1")
         picked = [picked0[:], picked1_flat[:, 0 : PACK * S].rearrange("p (i j) -> p i j", i=PACK)]
+        last_pair = picked1_flat[:, 2 * S :].rearrange("p (i j) -> p i j", i=2)
+
+        def picks(a, i0, i1, lo, hi):
+            if a == 1 and i1 == PACK and lo >= HALF:
+                return last_pair[:, i0 - 2 : i1 - 2, lo:hi]
+            return picked[a][:, i0:i1, lo:hi]
 
         x_bf = {}
         x_q = [held([P, S], U32, "x_q0"), late.tile([P, S], U32, name="x_q1", tag="late", align_bytes=64)]
@@ -170,7 +176,7 @@ def tile_list_predicate_join_cardinality_kernel(
 
         def gather_x(a, i, lo, hi):
             window = planes[a, i][:].indirect(offs2_t[:, lo // PER_COLUMN : hi // PER_COLUMN])
-            nc.vector.tensor_tensor(picked[a][:, i, lo:hi], window, wgt_all[:, lo:hi], MULT)
+            nc.vector.tensor_tensor(picks(a, i, i + 1, lo, hi)[:, 0], window, wgt_all[:, lo:hi], MULT)
 
         def woven(a):
             if a not in x_bf:
@@ -181,7 +187,7 @@ def tile_list_predicate_join_cardinality_kernel(
             copy_on(
                 engine,
                 woven(a)[:, lo * PACK : hi * PACK].rearrange("p (w z i) -> p w i z", z=2, i=PACK)[:, :, i0:i1],
-                picked[a][:, i0:i1, lo:hi].rearrange("p i (w z) -> p w i z", z=2),
+                picks(a, i0, i1, lo, hi).rearrange("p i (w z) -> p w i z", z=2),
             )
 
         def quant_x(a, lo, hi):
@@ -419,7 +425,7 @@ def tile_list_predicate_join_cardinality_kernel(
         gather_x(1, 1, 0, S)
         quant_x(0, HALF, S)
         weave_wx(0, 0, 0, PACK, "scalar")
-        weave_x(1, 0, S - QUART, 0, 2, "scalar")
+        weave_x(1, 0, S, 0, 2, "scalar")
         quant_wx(0, 0, 0, PACK)
         gather_x(1, 2, 0, S)
         for q in range(4):
@@ -431,7 +437,7 @@ def tile_list_predicate_join_cardinality_kernel(
 
         def finish_x(q):
             gather_x(1, PACK - 1, q * QUART, (q + 1) * QUART)
-            weave_x(1, q * QUART, (q + 1) * QUART, 2 if q < 3 else 0, PACK, "vector")
+            weave_x(1, q * QUART, (q + 1) * QUART, 2, PACK, "vector")
             quant_x(1, q * QUART, (q + 1) * QUART)
 
         def close(q, u):

@@ -225,7 +225,7 @@ def tile_list_predicate_join_cardinality_kernel(
                 scales = late.tile([P, width], U8, name="w_s_late", tag="late", align_bytes=64)[:]
             else:
                 codes = held([P, width], U32, "w_q%d%d%d" % (g, a, t0))
-                scales = after_carry[:, 1] if (g, a) == (0, 0) else held([P, width], U8, "w_s%d%d%d" % (g, a, t0))[:]
+                scales = after_carry[:, 1, t0 * P : t1 * P] if (g, a) == (0, 0) else held([P, width], U8, "w_s%d%d%d" % (g, a, t0))[:]
             for t in range(t0, t1):
                 w_q[g, a, t] = codes[:, (t - t0) * P : (t - t0 + 1) * P]
                 w_s[g, a, t] = scales[:, (t - t0) * P : (t - t0 + 1) * P]
@@ -256,7 +256,7 @@ def tile_list_predicate_join_cardinality_kernel(
                     lhsT_scale=wk_s[:, c0 : c0 + P],
                     rhs=t_q[:, cols].bitcast(E4M3),
                     rhs_scale=t_s[:, cols],
-                    start=s == 0,
+                    start=u == 0 and s == 0,
                     stop=False,
                 )
 
@@ -269,7 +269,7 @@ def tile_list_predicate_join_cardinality_kernel(
                     lhsT_scale=w_s[0, a, 2 * u + s],
                     rhs=x_q[a][:, cols].bitcast(E4M3),
                     rhs_scale=x_s(a, cols.start, cols.stop),
-                    start=False,
+                    start=u == 1 and a == 0 and s == 0,
                     stop=a == 1 and s == 1,
                 )
 
@@ -424,16 +424,19 @@ def tile_list_predicate_join_cardinality_kernel(
         order_wk()
         gather_x(1, 1, 0, S)
         quant_x(0, HALF, S)
-        weave_wx(0, 0, 0, PACK, "scalar")
+        for u in range(2):
+            weave_wx(0, 0, 2 * u, 2 * u + 2, "scalar")
         weave_x(1, 0, S, 0, 2, "scalar")
-        quant_wx(0, 0, 0, PACK)
+        quant_wx(0, 0, 0, 2)
         gather_x(1, 2, 0, S)
+        quant_wx(0, 0, 2, PACK)
         for q in range(4):
-            for u in range(2):
-                quarter_tab(q, u)
-        for q in range(4):
-            for u in range(2):
+            quarter_tab(q, 0)
+        for u in range(2):
+            for q in range(4):
                 quarter_x(q, u, 0)
+        for q in range(4):
+            quarter_tab(q, 1)
 
         def finish_x(q):
             gather_x(1, PACK - 1, q * QUART, (q + 1) * QUART)

@@ -208,8 +208,8 @@ def tile_list_predicate_join_cardinality_kernel(
             )
 
         wx01_bf = picked1_flat[:, PACK * S - HALF :].bitcast(BF16)
-        for t0 in (0, 2):
-            w_bf[0, 1, t0] = wx01_bf[:, t0 * P * PACK : (t0 + 2) * P * PACK]
+        for t in range(PACK):
+            w_bf[0, 1, t] = wx01_bf[:, t * P * PACK : (t + 1) * P * PACK]
 
         def weave_wx01(part, t0, t1):
             m = P // 4
@@ -277,38 +277,38 @@ def tile_list_predicate_join_cardinality_kernel(
             half, lo = divmod(q * QUART, HALF)
             nc.scalar.activation(exp_tile(0, half)[:, 2 * u : 2 * u + 2, lo : lo + QUART], quarter_bank(q, u)[:], ACT.Exp)
 
-        def half_bank(half, t):
-            if ("half", half, t) not in banks:
-                banks["half", half, t] = psum.tile([P, HALF], F32, name="bank", tag="bank%d" % (PACK * half + t))
-            return banks["half", half, t][:]
+        def half_bank(g, half, t):
+            if ("half", g, half, t) not in banks:
+                banks["half", g, half, t] = psum.tile([P, HALF], F32, name="bank", tag="bank%d" % (PACK * half + t))
+            return banks["half", g, half, t][:]
 
-        def half_tab(half, t):
-            c0 = KP + t * P
+        def half_tab(g, half, t, first):
+            c0 = g * KP + t * P
             cols = slice(half * HALF, (half + 1) * HALF)
             nc.tensor.matmul_mx(
-                out=half_bank(half, t),
+                out=half_bank(g, half, t),
                 lhsT=wk_q[:, 2 * c0 : 2 * (c0 + P)].bitcast(E2M1),
                 lhsT_scale=wk_s[:, c0 : c0 + P],
                 rhs=t_q[:, cols].bitcast(E4M3),
                 rhs_scale=t_s[:, cols],
-                start=True,
+                start=first,
                 stop=False,
             )
 
-        def half_x(half, t, a):
+        def half_x(g, half, t, a, first):
             cols = slice(half * HALF, (half + 1) * HALF)
             nc.tensor.matmul_mx(
-                out=half_bank(half, t),
-                lhsT=w_q[1, a, t].bitcast(E4M3),
-                lhsT_scale=w_s[1, a, t],
+                out=half_bank(g, half, t),
+                lhsT=w_q[g, a, t].bitcast(E4M3),
+                lhsT_scale=w_s[g, a, t],
                 rhs=x_q[a][:, cols].bitcast(E4M3),
                 rhs_scale=x_s(a, cols.start, cols.stop),
-                start=False,
+                start=first,
                 stop=a == 1,
             )
 
-        def half_exp(half, t):
-            nc.scalar.activation(exp_tile(1, half)[:, t, :], half_bank(half, t), ACT.Exp)
+        def half_exp(g, half, t):
+            nc.scalar.activation(exp_tile(g, half)[:, t, :], half_bank(g, half, t), ACT.Exp)
 
         wo_q = held([P, 2 * N], U32, "wo_q")
         wo_s = held([P, 2 * N], U8, "wo_s")
@@ -430,12 +430,18 @@ def tile_list_predicate_join_cardinality_kernel(
         quant_wx(0, 0, 0, 2)
         gather_x(1, 2, 0, S)
         quant_wx(0, 0, 2, PACK)
-        for q in range(4):
+        for t in range(2):
+            half_tab(0, 0, t, True)
+        for q in (2, 3):
             quarter_tab(q, 0)
         for u in range(2):
-            for q in range(4):
+            for t in (2 * u, 2 * u + 1):
+                half_x(0, 0, t, 0, u == 1)
+            for q in (2, 3):
                 quarter_x(q, u, 0)
-        for q in range(4):
+        for t in (2, 3):
+            half_tab(0, 0, t, False)
+        for q in (2, 3):
             quarter_tab(q, 1)
 
         def finish_x(q):
@@ -450,19 +456,19 @@ def tile_list_predicate_join_cardinality_kernel(
         weave_wx01(0, 0, PACK)
         for q in range(2):
             finish_x(q)
-        for u in range(2):
-            weave_wx01(1, 2 * u, 2 * u + 2)
-        for u in range(2):
-            quant_wx(0, 1, 2 * u, 2 * u + 2)
-            for q in range(2):
-                close(q, u)
+        for t in range(PACK):
+            weave_wx01(1, t, t + 1)
+        for t in range(PACK):
+            quant_wx(0, 1, t, t + 1)
+            half_x(0, 0, t, 1, False)
+            half_exp(0, 0, t)
         for q in (2, 3):
             finish_x(q)
             for u in range(2):
                 close(q, u)
 
         for t in range(PACK):
-            half_tab(0, t)
+            half_tab(1, 0, t, True)
         for t in range(PACK):
             for a in range(2):
                 weave_wx(1, a, t, t + 1, "vector")
@@ -470,10 +476,10 @@ def tile_list_predicate_join_cardinality_kernel(
                 quant_wx(1, a, t, t + 1)
             for half in range(2):
                 if half == 1:
-                    half_tab(half, t)
+                    half_tab(1, half, t, True)
                 for a in range(2):
-                    half_x(half, t, a)
-                half_exp(half, t)
+                    half_x(1, half, t, a, False)
+                half_exp(1, half, t)
         quant_wo()
 
         steps = [(sum(STEP_WIDTHS[:n]), width) for n, width in enumerate(STEP_WIDTHS)]

@@ -32,6 +32,7 @@ WOVEN_BUFS = 4
 CODE_BUFS = 3
 STEP_WIDTHS = [128, 128, 128, 128, 256, 128, 128]
 STORE_WIDTHS = [256, 256, 256, 128, 128]
+POOL_SHARES = [0, 32, 32, 64, 80, 32, 0]
 LEAD = STEP_WIDTHS[0] // 2
 
 
@@ -56,7 +57,6 @@ def tile_list_predicate_join_cardinality_kernel(
         tabs = held([P, T], U8, "tabs")
         tabw = keep.tile([P, T], U32, name="tabw", tag="tabw", align_bytes=64)
         wgt_all = held([P, S], F32, "wgt_all")
-        sel_t = held([P, 2, 8], F32, "sel_t")
         bo_t = held([P, 2], F32, "bo_t")
 
         nc.vector.memset(tabs[32:64, :].bitcast(I32), 0)
@@ -68,6 +68,8 @@ def tile_list_predicate_join_cardinality_kernel(
         t_s = held([P, S], U8, "t_s")
         nc.vector.memset(t_s[:].bitcast(I32), 0)
         wgt_part = held([P, P], F32, "wgt_part")
+        sel_part = held([P, P], F32, "sel_part")
+        nc.gpsimd.memset(sel_part[:], 0.0)
 
         x_rows = xT.rearrange("(a p i) d -> a i p d", a=2, i=PACK)
         wx_rows = wx.rearrange("(a p j) (g r) -> g a p j r", a=2, j=PACK, g=2)
@@ -129,9 +131,11 @@ def tile_list_predicate_join_cardinality_kernel(
         for g in range(2):
             for e in range(2):
                 nc.sync.dma_start(out=wo_raw[g][e::2, :, :], in_=wo_rows[g, e])
-        sel_runs = sel.rearrange("(g m k) -> m g k", g=2, k=8)
-        for e in range(2):
-            nc.sync.dma_start(out=sel_t[e::2, :, 0:7], in_=sel_runs[:, :, e : e + 7])
+        sel_rows = sel.rearrange("(g m t e) -> g t m e", g=2, t=PACK, e=2)
+        for g in range(2):
+            nc.sync.dma_start(
+                out=sel_part[PACK * g : PACK * (g + 1), :].rearrange("t (m e) -> t m e", e=2), in_=sel_rows[g]
+            )
         nc.sync.dma_start(out=bo_t[:], in_=bo.rearrange("(y p) -> p y", y=2))
 
         wk_q = held([P, 2 * H], U8, "wk_q")
@@ -321,11 +325,18 @@ def tile_list_predicate_join_cardinality_kernel(
                     out=wo_bf[:, g, :].rearrange("p (w z t) -> p w t z", z=2, t=PACK),
                     in_=wo_raw[g][:].rearrange("p t (w z) -> p w t z", z=2),
                 )
-            nc.vector.tensor_copy(out=sel_c[:], in_=sel_t[:, :, 0:7:2])
             nc.vector.quantize_mx(out=wo_q[:].bitcast(E4M3), scales=wo_s[:], in_=wo_bf[:].rearrange("p g w -> p (g w)"))
+
+        def turn_sel():
+            turned = psum.tile([P, P], F32, name="sel_p", tag="bank7")
+            nc.tensor.transpose(turned[:], sel_part[:], ident[:])
+            factors = turned[:, 0 : 2 * PACK].rearrange("p (g t) -> p g t", g=2)
+            nc.vector.tensor_copy(out=sel_c[:], in_=factors)
+            return factors
 
         out_rows = out.rearrange("(y p) j -> p y j", y=2)
         logs, h_bf, h_q, h_s, acc = {}, {}, {}, {}, {}
+        h_all = held([P, (S + STEP_WIDTHS[0]) * PACK], BF16, "h_all")
         stores = [(sum(STORE_WIDTHS[:n]), width) for n, width in enumerate(STORE_WIDTHS)]
 
         def take_log(g, j0, width):
@@ -339,21 +350,24 @@ def tile_list_predicate_join_cardinality_kernel(
             )
 
         def times_sel(g, j0, width, lo, hi):
-            if g == 0 and lo == 0:
-                h_bf[j0] = ring.tile([P, 2, width, PACK], BF16, name="h_bf", tag="bf", align_bytes=64, bufs=WOVEN_BUFS)
-            nc.vector.tensor_tensor(
-                h_bf[j0][:, g, lo:hi].rearrange("p j (u s) -> p j u s", u=2),
-                logs[g, j0 + lo][:].rearrange("p u j s -> p j u s"),
-                sel_c[:, g, :].rearrange("p (u s) -> p u s", u=2).unsqueeze(1).to_broadcast([P, hi - lo, 2, 2]),
-                MULT,
-            )
+            start = (S - j0 - width) * PACK
+            h_bf[j0] = h_all[:, start : start + 2 * width * PACK].rearrange("p (g j t) -> p g j t", g=2, t=PACK)
+            share = POOL_SHARES[[step[0] for step in steps].index(j0)] if g == 1 else 0
+            for engine, factors, q0, q1 in ((nc.gpsimd, sel_c, 0, share), (nc.vector, sel_p, share, hi - lo)):
+                if q1 > q0:
+                    engine.tensor_tensor(
+                        h_bf[j0][:, g, lo + q0 : lo + q1].rearrange("p j (u s) -> p j u s", u=2),
+                        logs[g, j0 + lo][:, :, q0:q1].rearrange("p u j s -> p j u s"),
+                        factors[:, g, :].rearrange("p (u s) -> p u s", u=2).unsqueeze(1).to_broadcast([P, q1 - q0, 2, 2]),
+                        MULT,
+                    )
 
         def mm_out(g, j0, width):
             n, (s0, span) = [(n, store) for n, store in enumerate(stores) if store[0] <= j0][-1]
             apart = s0 + span == S
             if s0 not in acc:
                 if apart:
-                    acc[s0] = [psum.tile([P, span], F32, name="acc", tag="bank%d" % (6 + y))[:] for y in range(2)]
+                    acc[s0] = [psum.tile([P, span], F32, name="acc", tag="bank%d" % (4 + y))[:] for y in range(2)]
                 else:
                     both = psum.tile([P, 2, span], F32, name="acc", tag="bank%d" % n)
                     acc[s0] = [both[:, y, :] for y in range(2)]
@@ -481,6 +495,7 @@ def tile_list_predicate_join_cardinality_kernel(
                     half_x(1, half, t, a, False)
                 half_exp(1, half, t)
         quant_wo()
+        sel_p = turn_sel()
 
         steps = [(sum(STEP_WIDTHS[:n]), width) for n, width in enumerate(STEP_WIDTHS)]
         take_log(0, 0, LEAD)

@@ -336,7 +336,7 @@ def tile_list_predicate_join_cardinality_kernel(
 
         out_rows = out.rearrange("(y p) j -> p y j", y=2)
         logs, h_bf, h_q, h_s, acc = {}, {}, {}, {}, {}
-        h_all = held([P, (S + STEP_WIDTHS[0]) * PACK], BF16, "h_all")
+        h_all = held([P, (2 * S - sum(POOL_SHARES[1:])) * PACK], BF16, "h_all")
         stores = [(sum(STORE_WIDTHS[:n]), width) for n, width in enumerate(STORE_WIDTHS)]
 
         def take_log(g, j0, width):
@@ -350,10 +350,11 @@ def tile_list_predicate_join_cardinality_kernel(
             )
 
         def times_sel(g, j0, width, lo, hi):
-            start = (S - j0 - width) * PACK
+            n = [step[0] for step in steps].index(j0)
+            start = (sum(2 * w for w in STEP_WIDTHS[n + 1 :]) - sum(POOL_SHARES[n + 1 :])) * PACK
             h_bf[j0] = h_all[:, start : start + 2 * width * PACK].rearrange("p (g j t) -> p g j t", g=2, t=PACK)
-            share = POOL_SHARES[[step[0] for step in steps].index(j0)] if g == 1 else 0
-            for engine, factors, q0, q1 in ((nc.gpsimd, sel_c, 0, share), (nc.vector, sel_p, share, hi - lo)):
+            split = hi - lo - (POOL_SHARES[n] if g == 1 else 0)
+            for engine, factors, q0, q1 in ((nc.gpsimd, sel_c, split, hi - lo), (nc.vector, sel_p, 0, split)):
                 if q1 > q0:
                     engine.tensor_tensor(
                         h_bf[j0][:, g, lo + q0 : lo + q1].rearrange("p j (u s) -> p j u s", u=2),

@@ -27,13 +27,16 @@ PER_COLUMN = 16
 GROUPS = 8
 
 PLANE_BUFS = 5
-LOG_BUFS = 4
+LOG_BUFS = 6
 WOVEN_BUFS = 4
 CODE_BUFS = 3
-STEP_WIDTHS = [128, 128, 128, 128, 256, 128, 128]
-STORE_WIDTHS = [256, 256, 256, 128, 128]
-POOL_SHARES = [0, 32, 32, 64, 80, 32, 0]
-LEAD = STEP_WIDTHS[0] // 2
+UNIT = 128
+STEP_WIDTHS = [128, 128, 256, 256, 128, 128]
+POOL_SHARES = [0, 32, 112, 112, 32, 0]
+VECTOR_BIASES = [(5, 0)]
+EARLY_STORES = 0
+REPEAT = P // (2 * PACK)
+LEAD = UNIT // 2
 
 
 def tile_list_predicate_join_cardinality_kernel(
@@ -61,15 +64,15 @@ def tile_list_predicate_join_cardinality_kernel(
 
         nc.vector.memset(tabs[32:64, :].bitcast(I32), 0)
         nc.vector.memset(tabs[64:P, :].bitcast(I32), 0)
-        ident = held([P, P], F32, "ident")
+        ident = late.tile([P, P], F32, name="ident", tag="late", align_bytes=64)
         nc.vector.memset(ident[:].bitcast(I32), 0)
         make_identity(nc, ident[:], nomemset=True)
         nc.vector.memset(wks_raw[:].bitcast(I32), 0)
         t_s = held([P, S], U8, "t_s")
         nc.vector.memset(t_s[:].bitcast(I32), 0)
         wgt_part = held([P, P], F32, "wgt_part")
-        sel_part = held([P, P], F32, "sel_part")
-        nc.gpsimd.memset(sel_part[:], 0.0)
+        sel_part = late.tile([P, P], F32, name="sel_part", tag="late", align_bytes=64)
+        sel_t = held([P, 2, 8], F32, "sel_t")
 
         x_rows = xT.rearrange("(a p i) d -> a i p d", a=2, i=PACK)
         wx_rows = wx.rearrange("(a p j) (g r) -> g a p j r", a=2, j=PACK, g=2)
@@ -131,11 +134,9 @@ def tile_list_predicate_join_cardinality_kernel(
         for g in range(2):
             for e in range(2):
                 nc.sync.dma_start(out=wo_raw[g][e::2, :, :], in_=wo_rows[g, e])
-        sel_rows = sel.rearrange("(g m t e) -> g t m e", g=2, t=PACK, e=2)
-        for g in range(2):
-            nc.sync.dma_start(
-                out=sel_part[PACK * g : PACK * (g + 1), :].rearrange("t (m e) -> t m e", e=2), in_=sel_rows[g]
-            )
+        sel_runs = sel.rearrange("(g m k) -> m g k", g=2, k=8)
+        for e in range(2):
+            nc.sync.dma_start(out=sel_t[e::2, :, 0:7], in_=sel_runs[:, :, e : e + 7])
         nc.sync.dma_start(out=bo_t[:], in_=bo.rearrange("(y p) -> p y", y=2))
 
         wk_q = held([P, 2 * H], U8, "wk_q")
@@ -316,7 +317,7 @@ def tile_list_predicate_join_cardinality_kernel(
 
         wo_q = held([P, 2 * N], U32, "wo_q")
         wo_s = held([P, 2 * N], U8, "wo_s")
-        sel_c = held([P, 2, PACK], F32, "sel_c")
+        sel_c = held([P, 2, REPEAT, PACK], F32, "sel_c")
 
         def quant_wo():
             wo_bf = keep.tile([P, 2, N * PACK], BF16, name="wo_bf", tag="wo_bf", align_bytes=64)
@@ -328,84 +329,88 @@ def tile_list_predicate_join_cardinality_kernel(
             nc.vector.quantize_mx(out=wo_q[:].bitcast(E4M3), scales=wo_s[:], in_=wo_bf[:].rearrange("p g w -> p (g w)"))
 
         def turn_sel():
-            turned = psum.tile([P, P], F32, name="sel_p", tag="bank7")
-            nc.tensor.transpose(turned[:], sel_part[:], ident[:])
-            factors = turned[:, 0 : 2 * PACK].rearrange("p (g t) -> p g t", g=2)
-            nc.vector.tensor_copy(out=sel_c[:], in_=factors)
-            return factors
+            nc.vector.tensor_copy(out=sel_c[:], in_=sel_t[:, :, 0:7:2].unsqueeze(2).to_broadcast([P, 2, REPEAT, PACK]))
+            once = psum.tile([P, P], F32, name="sel_once", tag="bank3")
+            nc.tensor.transpose(once[:], sel_c[:].rearrange("p g j t -> p (g j t)"), ident[:])
+            nc.vector.tensor_copy(out=sel_part[:], in_=once[:])
+            twice = psum.tile([P, P], F32, name="sel_p", tag="bank7")
+            nc.tensor.transpose(twice[:], sel_part[:], ident[:])
+            return twice[:].rearrange("p (g j t) -> p g j t", g=2, t=PACK)
 
         out_rows = out.rearrange("(y p) j -> p y j", y=2)
-        logs, h_bf, h_q, h_s, acc = {}, {}, {}, {}, {}
+        steps = [(sum(STEP_WIDTHS[:n]), width) for n, width in enumerate(STEP_WIDTHS)]
+        last = len(steps) - 1
         h_all = held([P, (2 * S - sum(POOL_SHARES[1:])) * PACK], BF16, "h_all")
-        stores = [(sum(STORE_WIDTHS[:n]), width) for n, width in enumerate(STORE_WIDTHS)]
+        logs, h_q, h_s, acc = {}, {}, {}, {}
 
-        def take_log(g, j0, width):
-            half, lo = divmod(j0, HALF)
-            logs[g, j0] = late.tile([P, 2, width, 2], F32, name="logs", tag="late", align_bytes=64)
+        def h_bf(n):
+            start = (sum(2 * w for w in STEP_WIDTHS[n + 1 :]) - sum(POOL_SHARES[n + 1 :])) * PACK
+            return h_all[:, start : start + 2 * STEP_WIDTHS[n] * PACK].rearrange("p (g j t) -> p g j t", g=2, t=PACK)
+
+        def take_log(n, g, lo, hi):
+            half, j = divmod(steps[n][0] + lo, HALF)
+            logs[n, g, lo] = late.tile([P, 2, hi - lo, 2], F32, name="logs", tag="late", align_bytes=64)
             nc.scalar.activation(
-                logs[g, j0][:],
-                expd[g, half][:, :, lo : lo + width].rearrange("p (u s) j -> p u j s", u=2),
+                logs[n, g, lo][:],
+                expd[g, half][:, :, j : j + hi - lo].rearrange("p (u s) j -> p u j s", u=2),
                 ACT.Ln,
                 bias=1.0,
             )
 
-        def times_sel(g, j0, width, lo, hi):
-            n = [step[0] for step in steps].index(j0)
-            start = (sum(2 * w for w in STEP_WIDTHS[n + 1 :]) - sum(POOL_SHARES[n + 1 :])) * PACK
-            h_bf[j0] = h_all[:, start : start + 2 * width * PACK].rearrange("p (g j t) -> p g j t", g=2, t=PACK)
-            split = hi - lo - (POOL_SHARES[n] if g == 1 else 0)
-            for engine, factors, q0, q1 in ((nc.gpsimd, sel_c, split, hi - lo), (nc.vector, sel_p, 0, split)):
+        def times_sel(n, g, lo, hi):
+            split = min(hi, max(lo, STEP_WIDTHS[n] - POOL_SHARES[n])) if g == 1 else hi
+            for engine, factors, q0, q1 in ((nc.gpsimd, sel_c, split, hi), (nc.vector, sel_p, lo, split)):
                 if q1 > q0:
                     engine.tensor_tensor(
-                        h_bf[j0][:, g, lo + q0 : lo + q1].rearrange("p j (u s) -> p j u s", u=2),
-                        logs[g, j0 + lo][:, :, q0:q1].rearrange("p u j s -> p j u s"),
-                        factors[:, g, :].rearrange("p (u s) -> p u s", u=2).unsqueeze(1).to_broadcast([P, q1 - q0, 2, 2]),
+                        h_bf(n)[:, g, q0:q1].rearrange("p (b j) (u s) -> p b j u s", j=REPEAT, u=2),
+                        logs[n, g, lo][:, :, q0 - lo : q1 - lo].rearrange("p u (b j) s -> p b j u s", j=REPEAT),
+                        factors[:, g].rearrange("p j (u s) -> p j u s", u=2).unsqueeze(1).to_broadcast([P, (q1 - q0) // REPEAT, REPEAT, 2, 2]),
                         MULT,
                     )
 
-        def mm_out(g, j0, width):
-            n, (s0, span) = [(n, store) for n, store in enumerate(stores) if store[0] <= j0][-1]
-            apart = s0 + span == S
-            if s0 not in acc:
-                if apart:
-                    acc[s0] = [psum.tile([P, span], F32, name="acc", tag="bank%d" % (4 + y))[:] for y in range(2)]
+        def mm_out(n, g):
+            width = STEP_WIDTHS[n]
+            if n not in acc:
+                if n == last:
+                    acc[n] = [psum.tile([P, width], F32, name="acc", tag="bank%d" % (5 + y))[:] for y in range(2)]
                 else:
-                    both = psum.tile([P, 2, span], F32, name="acc", tag="bank%d" % n)
-                    acc[s0] = [both[:, y, :] for y in range(2)]
+                    both = psum.tile([P, 2, width], F32, name="acc", tag="bank%d" % n)
+                    acc[n] = [both[:, y, :] for y in range(2)]
             for y in range(2):
                 cols = slice(g * N + y * P, g * N + (y + 1) * P)
                 nc.tensor.matmul_mx(
-                    out=acc[s0][y][:, j0 - s0 : j0 - s0 + width],
+                    out=acc[n][y],
                     lhsT=wo_q[:, cols].bitcast(E4M3),
                     lhsT_scale=wo_s[:, cols],
-                    rhs=h_q[j0][:, g].bitcast(E4M3),
-                    rhs_scale=h_s[j0][:, g],
-                    start=j0 == s0 and g == 0 and (y == 0 or apart),
-                    stop=j0 + width == s0 + span and g == 1 and (y == 1 or apart),
+                    rhs=h_q[n][:, g].bitcast(E4M3),
+                    rhs_scale=h_s[n][:, g],
+                    start=g == 0 and (y == 0 or n == last),
+                    stop=g == 1 and (y == 1 or n == last),
                 )
 
-        def quant_and_multiply(g0, g1, j0, width):
+        def quant_and_multiply(n, g0, g1):
             if g0 == 0:
-                h_q[j0] = ring.tile([P, 2, width], U32, name="h_q", align_bytes=64, bufs=CODE_BUFS)
-                h_s[j0] = ring.tile([P, 2, width], U8, name="h_s", align_bytes=64, bufs=CODE_BUFS)
+                h_q[n] = ring.tile([P, 2, STEP_WIDTHS[n]], U32, name="h_q", align_bytes=64, bufs=CODE_BUFS)
+                h_s[n] = ring.tile([P, 2, STEP_WIDTHS[n]], U8, name="h_s", align_bytes=64, bufs=CODE_BUFS)
             nc.vector.quantize_mx(
-                out=h_q[j0][:, g0:g1].rearrange("p g j -> p (g j)").bitcast(E4M3),
-                scales=h_s[j0][:, g0:g1].rearrange("p g j -> p (g j)"),
-                in_=h_bf[j0][:, g0:g1].rearrange("p g j t -> p (g j t)"),
+                out=h_q[n][:, g0:g1].rearrange("p g j -> p (g j)").bitcast(E4M3),
+                scales=h_s[n][:, g0:g1].rearrange("p g j -> p (g j)"),
+                in_=h_bf(n)[:, g0:g1].rearrange("p g j t -> p (g j t)"),
             )
             for g in range(g0, g1):
-                mm_out(g, j0, width)
+                mm_out(n, g)
 
-        def store(j0, width):
+        def store(n):
+            j0, width = steps[n]
             res = ring.tile([P, 2, width], F32, name="res", tag="wbf", align_bytes=64, bufs=WOVEN_BUFS)
             for y in range(2):
-                if j0 + width == S and y == 0:
-                    nc.vector.tensor_scalar_add(res[:, y, :], acc[j0][y], bo_t[:, y : y + 1])
+                if (n, y) in VECTOR_BIASES:
+                    nc.vector.tensor_scalar_add(res[:, y, :], acc[n][y], bo_t[:, y : y + 1])
                 else:
-                    nc.scalar.activation(res[:, y, :], acc[j0][y], ACT.Identity, bias=bo_t[:, y : y + 1])
-                if j0 + width == S:
+                    nc.scalar.activation(res[:, y, :], acc[n][y], ACT.Identity, bias=bo_t[:, y : y + 1])
+                if n == last:
                     (nc.sync, nc.scalar)[y].dma_start(out=out_rows[:, y, j0 : j0 + width], in_=res[:, y, :])
-            if j0 + width < S:
+            if n < last:
                 nc.sync.dma_start(out=out_rows[:, :, j0 : j0 + width], in_=res[:])
 
         def spread_wgt():
@@ -498,22 +503,27 @@ def tile_list_predicate_join_cardinality_kernel(
         quant_wo()
         sel_p = turn_sel()
 
-        steps = [(sum(STEP_WIDTHS[:n]), width) for n, width in enumerate(STEP_WIDTHS)]
-        take_log(0, 0, LEAD)
-        take_log(0, LEAD, LEAD)
-        take_log(1, *steps[0])
-        times_sel(0, *steps[0], 0, LEAD)
-        for n, (j0, width) in enumerate(steps):
-            ahead = steps[n + 1 : n + 2]
-            for step in ahead:
-                take_log(0, *step)
-            times_sel(0, j0, width, LEAD if n == 0 else 0, width)
-            if n > 0:
-                quant_and_multiply(0, 2, *steps[n - 1])
-            for step in ahead:
-                take_log(1, *step)
-            times_sel(1, j0, width, 0, width)
+        units = [(0, 0, 0, LEAD), (0, 0, LEAD, UNIT), (0, 1, 0, UNIT)]
+        for n in range(1, last + 1):
+            width = STEP_WIDTHS[n]
+            if width == UNIT:
+                units += [(n, 0, 0, width), (n, 1, 0, width)]
+            else:
+                rest = width - POOL_SHARES[n]
+                units += [(n, 0, 0, UNIT), (n, 1, rest, width), (n, 0, UNIT, width), (n, 1, 0, rest)]
+        ahead = 2
+        for unit in units[:ahead]:
+            take_log(*unit)
+        for k, unit in enumerate(units):
+            for later in units[k + ahead : k + ahead + 1]:
+                take_log(*later)
+            n, g, lo, hi = unit
+            times_sel(*unit)
+            if n > 0 and g == 0 and lo == 0:
+                quant_and_multiply(n - 1, 0, 2)
+            if g == 0 and lo == UNIT and n - 1 < EARLY_STORES and n > 0:
+                store(n - 1)
         for g in range(2):
-            quant_and_multiply(g, g + 1, *steps[-1])
-        for span in stores:
-            store(*span)
+            quant_and_multiply(last, g, g + 1)
+        for n in range(EARLY_STORES, last + 1):
+            store(n)

@@ -28,12 +28,13 @@ GROUPS = 8
 
 PLANE_BUFS = 5
 LOG_BUFS = 6
-WOVEN_BUFS = 4
+WOVEN_BUFS = 5
 CODE_BUFS = 3
 UNIT = 128
 STEP_WIDTHS = [128, 128, 256, 256, 128, 128]
-POOL_SHARES = [0, 32, 112, 112, 32, 0]
-VECTOR_BIASES = [(5, 0)]
+POOL_SHARES = [0, 32, 112, 112, 64, 0]
+VECTOR_BIASES = [(3, 0), (3, 1), (4, 0)]
+STORE_WIDTHS = [256, 256, 256, 128, 128]
 EARLY_STORES = 0
 REPEAT = P // (2 * PACK)
 LEAD = UNIT // 2
@@ -340,6 +341,7 @@ def tile_list_predicate_join_cardinality_kernel(
         out_rows = out.rearrange("(y p) j -> p y j", y=2)
         steps = [(sum(STEP_WIDTHS[:n]), width) for n, width in enumerate(STEP_WIDTHS)]
         last = len(steps) - 1
+        stores = [(sum(STORE_WIDTHS[:k]), width) for k, width in enumerate(STORE_WIDTHS)]
         h_all = held([P, (2 * S - sum(POOL_SHARES[1:])) * PACK], BF16, "h_all")
         logs, h_q, h_s, acc = {}, {}, {}, {}
 
@@ -359,7 +361,9 @@ def tile_list_predicate_join_cardinality_kernel(
 
         def times_sel(n, g, lo, hi):
             split = min(hi, max(lo, STEP_WIDTHS[n] - POOL_SHARES[n])) if g == 1 else hi
-            for engine, factors, q0, q1 in ((nc.gpsimd, sel_c, split, hi), (nc.vector, sel_p, lo, split)):
+            first = g == 0 and lo == 0
+            own = sel_p if POOL_SHARES[n - 1 if (first or n == last) and n > 0 else n] > 0 else sel_c
+            for engine, factors, q0, q1 in ((nc.gpsimd, sel_c, split, hi), (nc.vector, own, lo, split)):
                 if q1 > q0:
                     engine.tensor_tensor(
                         h_bf(n)[:, g, q0:q1].rearrange("p (b j) (u s) -> p b j u s", j=REPEAT, u=2),
@@ -369,23 +373,24 @@ def tile_list_predicate_join_cardinality_kernel(
                     )
 
         def mm_out(n, g):
-            width = STEP_WIDTHS[n]
-            if n not in acc:
+            j0, width = steps[n]
+            k, (s0, span) = [(k, store) for k, store in enumerate(stores) if store[0] <= j0][-1]
+            if k not in acc:
                 if n == last:
-                    acc[n] = [psum.tile([P, width], F32, name="acc", tag="bank%d" % (5 + y))[:] for y in range(2)]
+                    acc[k] = [psum.tile([P, span], F32, name="acc", tag="bank%d" % (5 + y))[:] for y in range(2)]
                 else:
-                    both = psum.tile([P, 2, width], F32, name="acc", tag="bank%d" % n)
-                    acc[n] = [both[:, y, :] for y in range(2)]
+                    both = psum.tile([P, 2, span], F32, name="acc", tag="bank%d" % k)
+                    acc[k] = [both[:, y, :] for y in range(2)]
             for y in range(2):
                 cols = slice(g * N + y * P, g * N + (y + 1) * P)
                 nc.tensor.matmul_mx(
-                    out=acc[n][y],
+                    out=acc[k][y][:, j0 - s0 : j0 - s0 + width],
                     lhsT=wo_q[:, cols].bitcast(E4M3),
                     lhsT_scale=wo_s[:, cols],
                     rhs=h_q[n][:, g].bitcast(E4M3),
                     rhs_scale=h_s[n][:, g],
-                    start=g == 0 and (y == 0 or n == last),
-                    stop=g == 1 and (y == 1 or n == last),
+                    start=j0 == s0 and g == 0 and (y == 0 or n == last),
+                    stop=j0 + width == s0 + span and g == 1 and (y == 1 or n == last),
                 )
 
         def quant_and_multiply(n, g0, g1):
@@ -401,16 +406,16 @@ def tile_list_predicate_join_cardinality_kernel(
                 mm_out(n, g)
 
         def store(n):
-            j0, width = steps[n]
+            j0, width = stores[n]
             res = ring.tile([P, 2, width], F32, name="res", tag="wbf", align_bytes=64, bufs=WOVEN_BUFS)
             for y in range(2):
                 if (n, y) in VECTOR_BIASES:
                     nc.vector.tensor_scalar_add(res[:, y, :], acc[n][y], bo_t[:, y : y + 1])
                 else:
                     nc.scalar.activation(res[:, y, :], acc[n][y], ACT.Identity, bias=bo_t[:, y : y + 1])
-                if n == last:
+                if j0 + width == S:
                     (nc.sync, nc.scalar)[y].dma_start(out=out_rows[:, y, j0 : j0 + width], in_=res[:, y, :])
-            if n < last:
+            if j0 + width < S:
                 nc.sync.dma_start(out=out_rows[:, :, j0 : j0 + width], in_=res[:])
 
         def spread_wgt():
@@ -519,11 +524,11 @@ def tile_list_predicate_join_cardinality_kernel(
                 take_log(*later)
             n, g, lo, hi = unit
             times_sel(*unit)
-            if n > 0 and g == 0 and lo == 0:
+            if n > 0 and lo == 0 and g == (1 if n == last else 0):
                 quant_and_multiply(n - 1, 0, 2)
             if g == 0 and lo == UNIT and n - 1 < EARLY_STORES and n > 0:
                 store(n - 1)
         for g in range(2):
             quant_and_multiply(last, g, g + 1)
-        for n in range(EARLY_STORES, last + 1):
+        for n in range(EARLY_STORES, len(stores)):
             store(n)

@@ -32,7 +32,7 @@ WOVEN_BUFS = 5
 CODE_BUFS = 3
 UNIT = 128
 STEP_WIDTHS = [128, 128, 256, 256, 128, 128]
-POOL_SHARES = [0, 32, 112, 112, 64, 0]
+POOL_SHARES = [0, 0, 128, 128, 80, 0]
 VECTOR_BIASES = [(3, 0), (3, 1), (4, 0)]
 STORE_WIDTHS = [256, 256, 256, 128, 128]
 EARLY_STORES = 0

@@ -32,7 +32,7 @@ WOVEN_BUFS = 5
 CODE_BUFS = 3
 UNIT = 128
 STEP_WIDTHS = [128, 128, 256, 256, 128, 128]
-POOL_SHARES = [0, 0, 128, 128, 80, 0]
+POOL_SHARES = [0, 0, 112, 128, 80, 0]
 VECTOR_BIASES = [(3, 0), (3, 1), (4, 0)]
 STORE_WIDTHS = [256, 256, 256, 128, 128]
 EARLY_STORES = 0
@@ -342,12 +342,12 @@ def tile_list_predicate_join_cardinality_kernel(
         steps = [(sum(STEP_WIDTHS[:n]), width) for n, width in enumerate(STEP_WIDTHS)]
         last = len(steps) - 1
         stores = [(sum(STORE_WIDTHS[:k]), width) for k, width in enumerate(STORE_WIDTHS)]
-        h_all = held([P, (2 * S - sum(POOL_SHARES[1:])) * PACK], BF16, "h_all")
+        h_all = [held([P, (S - g * sum(POOL_SHARES)) * PACK], BF16, "h_all%d" % g) for g in range(2)]
         logs, h_q, h_s, acc = {}, {}, {}, {}
 
-        def h_bf(n):
-            start = (sum(2 * w for w in STEP_WIDTHS[n + 1 :]) - sum(POOL_SHARES[n + 1 :])) * PACK
-            return h_all[:, start : start + 2 * STEP_WIDTHS[n] * PACK].rearrange("p (g j t) -> p g j t", g=2, t=PACK)
+        def h_bf(n, g):
+            start = (sum(STEP_WIDTHS[n + 1 :]) - g * sum(POOL_SHARES[n + 1 :])) * PACK
+            return h_all[g][:, start : start + STEP_WIDTHS[n] * PACK]
 
         def take_log(n, g, lo, hi):
             half, j = divmod(steps[n][0] + lo, HALF)
@@ -366,13 +366,13 @@ def tile_list_predicate_join_cardinality_kernel(
             for engine, factors, q0, q1 in ((nc.gpsimd, sel_c, split, hi), (nc.vector, own, lo, split)):
                 if q1 > q0:
                     engine.tensor_tensor(
-                        h_bf(n)[:, g, q0:q1].rearrange("p (b j) (u s) -> p b j u s", j=REPEAT, u=2),
+                        h_bf(n, g)[:, q0 * PACK : q1 * PACK].rearrange("p (b j u s) -> p b j u s", j=REPEAT, u=2, s=2),
                         logs[n, g, lo][:, :, q0 - lo : q1 - lo].rearrange("p u (b j) s -> p b j u s", j=REPEAT),
                         factors[:, g].rearrange("p j (u s) -> p j u s", u=2).unsqueeze(1).to_broadcast([P, (q1 - q0) // REPEAT, REPEAT, 2, 2]),
                         MULT,
                     )
 
-        def mm_out(n, g):
+        def mm_out(n, g, first):
             j0, width = steps[n]
             k, (s0, span) = [(k, store) for k, store in enumerate(stores) if store[0] <= j0][-1]
             if k not in acc:
@@ -389,21 +389,17 @@ def tile_list_predicate_join_cardinality_kernel(
                     lhsT_scale=wo_s[:, cols],
                     rhs=h_q[n][:, g].bitcast(E4M3),
                     rhs_scale=h_s[n][:, g],
-                    start=j0 == s0 and g == 0 and (y == 0 or n == last),
-                    stop=j0 + width == s0 + span and g == 1 and (y == 1 or n == last),
+                    start=j0 == s0 and first and (y == 0 or n == last),
+                    stop=j0 + width == s0 + span and not first and (y == 1 or n == last),
                 )
 
-        def quant_and_multiply(n, g0, g1):
-            if g0 == 0:
-                h_q[n] = ring.tile([P, 2, STEP_WIDTHS[n]], U32, name="h_q", align_bytes=64, bufs=CODE_BUFS)
-                h_s[n] = ring.tile([P, 2, STEP_WIDTHS[n]], U8, name="h_s", align_bytes=64, bufs=CODE_BUFS)
-            nc.vector.quantize_mx(
-                out=h_q[n][:, g0:g1].rearrange("p g j -> p (g j)").bitcast(E4M3),
-                scales=h_s[n][:, g0:g1].rearrange("p g j -> p (g j)"),
-                in_=h_bf(n)[:, g0:g1].rearrange("p g j t -> p (g j t)"),
-            )
-            for g in range(g0, g1):
-                mm_out(n, g)
+        def quant_and_multiply(n, order):
+            h_q[n] = ring.tile([P, 2, STEP_WIDTHS[n]], U32, name="h_q", align_bytes=64, bufs=CODE_BUFS)
+            h_s[n] = ring.tile([P, 2, STEP_WIDTHS[n]], U8, name="h_s", align_bytes=64, bufs=CODE_BUFS)
+            for g in order:
+                nc.vector.quantize_mx(out=h_q[n][:, g].bitcast(E4M3), scales=h_s[n][:, g], in_=h_bf(n, g))
+            for g in order:
+                mm_out(n, g, g == order[0])
 
         def store(n):
             j0, width = stores[n]
@@ -525,10 +521,9 @@ def tile_list_predicate_join_cardinality_kernel(
             n, g, lo, hi = unit
             times_sel(*unit)
             if n > 0 and lo == 0 and g == (1 if n == last else 0):
-                quant_and_multiply(n - 1, 0, 2)
+                quant_and_multiply(n - 1, (1, 0))
             if g == 0 and lo == UNIT and n - 1 < EARLY_STORES and n > 0:
                 store(n - 1)
-        for g in range(2):
-            quant_and_multiply(last, g, g + 1)
+        quant_and_multiply(last, (0, 1))
         for n in range(EARLY_STORES, len(stores)):
             store(n)

from contextlib import ExitStack

import concourse.mybir as mybir
from concourse.masks import make_identity

K, C, H, N, T, D, S = 512, 1024, 1024, 256, 2048, 2048, 1024
FLOPS = 2 * S * (C * H + K * H + H * N)

F32 = mybir.dt.float32
BF16 = mybir.dt.bfloat16
I32 = mybir.dt.int32
U32 = mybir.dt.uint32
U16 = mybir.dt.uint16
U8 = mybir.dt.uint8
E4M3 = mybir.dt.float8_e4m3fn_x4
E2M1 = mybir.dt.float4_e2m1fn_x4
MULT = mybir.AluOpType.mult
ACT = mybir.ActivationFunctionType

P = 128
PACK = 4
KP = P * PACK
HALF = S // 2
QUART = S // 4
SCALE_ROWS = 16
PER_COLUMN = 16
GROUPS = 8

PLANE_BUFS = 5
LOG_BUFS = 6
WOVEN_BUFS = 5
CODE_BUFS = 3
UNIT = 128
STEP_WIDTHS = [128, 128, 256, 256, 128, 128]
POOL_SHARES = [0, 0, 112, 128, 80, 0]
VECTOR_BIASES = [(3, 0), (3, 1), (4, 0)]
STORE_WIDTHS = [256, 256, 256, 128, 128]
EARLY_STORES = 0
REPEAT = P // (2 * PACK)
LEAD = UNIT // 2


def tile_list_predicate_join_cardinality_kernel(
    tc, tab_words, tab_scales, offs, xT, wgt, offs2, wx, wk_words, wk_scales, sel, wo, bo, out
):
    nc = tc.nc
    with ExitStack() as ctx:
        keep = ctx.enter_context(tc.tile_pool(name="keep", bufs=1))
        plane_pool = ctx.enter_context(tc.tile_pool(name="planes", bufs=PLANE_BUFS))
        late = ctx.enter_context(tc.tile_pool(name="late", bufs=LOG_BUFS))
        ring = ctx.enter_context(tc.tile_pool(name="ring", bufs=2))
        psum = ctx.enter_context(tc.psum_pool(name="psum", bufs=1))

        def held(shape, dtype, name, tag=None):
            return keep.tile(shape, dtype, name=name, tag=tag or name, align_bytes=64)

        offs2_t = keep.tile([P, S // PER_COLUMN], U16, name="offs2_t")
        offs_t = keep.tile([P, S // PER_COLUMN], U16, name="offs_t")
        wk_raw = held([P, 2 * H], U8, "wk_raw")
        wks_raw = held([P, H], U8, "wks_raw")
        tabs = held([P, T], U8, "tabs")
        tabw = keep.tile([P, T], U32, name="tabw", tag="tabw", align_bytes=64)
        wgt_all = held([P, S], F32, "wgt_all")
        bo_t = held([P, 2], F32, "bo_t")

        nc.vector.memset(tabs[32:64, :].bitcast(I32), 0)
        nc.vector.memset(tabs[64:P, :].bitcast(I32), 0)
        ident = late.tile([P, P], F32, name="ident", tag="late", align_bytes=64)
        nc.vector.memset(ident[:].bitcast(I32), 0)
        make_identity(nc, ident[:], nomemset=True)
        nc.vector.memset(wks_raw[:].bitcast(I32), 0)
        t_s = held([P, S], U8, "t_s")
        nc.vector.memset(t_s[:].bitcast(I32), 0)
        wgt_part = held([P, P], F32, "wgt_part")
        sel_part = late.tile([P, P], F32, name="sel_part", tag="late", align_bytes=64)
        sel_t = held([P, 2, 8], F32, "sel_t")

        x_rows = xT.rearrange("(a p i) d -> a i p d", a=2, i=PACK)
        wx_rows = wx.rearrange("(a p j) (g r) -> g a p j r", a=2, j=PACK, g=2)
        planes = {}
        wx_raw = {}
        wx01_raw = []

        def load_plane(a, i):
            planes[a, i] = plane_pool.tile([P, D], F32, name="plane", tag="plane", align_bytes=64)
            nc.sync.dma_start(out=planes[a, i][:], in_=x_rows[a, i])

        def load_wx01(part):
            wx01_raw.append(held([P, PACK, KP // 2], F32, "wx01_raw%d" % part))
            nc.sync.dma_start(out=wx01_raw[part][:], in_=wx_rows[0, 1][:, :, part * (KP // 2) : (part + 1) * (KP // 2)])

        def load_wx(g, a):
            wx_raw[g, a] = keep.tile([P, PACK, KP], F32, name="wx_raw", tag="wx%d%d" % (g, a), align_bytes=64)
            nc.sync.dma_start(out=wx_raw[g, a][:], in_=wx_rows[g, a])

        nc.scalar.dma_start(out=wgt_part[:], in_=wgt.rearrange("(g x) (c j) -> (x c) g j", g=GROUPS, j=P)[0:16])
        nc.sync.dma_start(offs_t[:], offs)
        nc.sync.dma_start(out=tabs[0:32, :].bitcast(I32), in_=tab_scales[0].bitcast(I32).unsqueeze(1).to_broadcast([SCALE_ROWS, 2, T // 4]))
        nc.sync.dma_start(out=tabw[:].bitcast(I32), in_=tab_words[0].rearrange("p t i -> p (t i)").bitcast(I32))
        t_s_rows = held([P, S], U8, "t_s_rows")
        nc.vector.tensor_copy(t_s_rows[:], tabs[:].indirect(offs_t[:]))

        def carry(quad):
            nc.sync.dma_start(
                out=t_s[32 * quad : 32 * quad + 4, :].bitcast(I32), in_=t_s_rows[8 * quad + quad % 2 : 8 * quad + 8 : 2, :].bitcast(I32)
            )

        def load_wks(quad):
            nc.sync.dma_start(
                out=wks_raw[32 * quad : 32 * quad + 4, :].bitcast(I32), in_=wk_scales[0, 4 * quad : 4 * quad + 4, :].bitcast(I32)
            )

        nc.sync.dma_start(offs2_t[:], offs2)
        load_plane(0, 0)
        nc.sync.dma_start(out=wk_raw[:].bitcast(I32), in_=wk_words[0].bitcast(I32))
        load_wks(0)
        for i in range(1, PACK):
            load_wks(i)
            load_plane(0, i)
        load_plane(1, 0)
        carry(0)
        carry(1)
        carry(2)
        load_plane(1, 1)
        carry(3)
        load_wx(0, 0)
        load_plane(1, 2)
        load_plane(1, 3)
        load_wx01(0)
        load_wx01(1)
        load_wx(1, 0)
        load_wx(1, 1)
        wo_raw = [held([P, PACK, N], F32, "wo_raw%d" % g) for g in range(2)]
        wo_rows = wo.rearrange("(g m t e) n -> g e m t n", g=2, t=PACK, e=2)
        for g in range(2):
            for e in range(2):
                nc.sync.dma_start(out=wo_raw[g][e::2, :, :], in_=wo_rows[g, e])
        sel_runs = sel.rearrange("(g m k) -> m g k", g=2, k=8)
        for e in range(2):
            nc.sync.dma_start(out=sel_t[e::2, :, 0:7], in_=sel_runs[:, :, e : e + 7])
        nc.sync.dma_start(out=bo_t[:], in_=bo.rearrange("(y p) -> p y", y=2))

        wk_q = held([P, 2 * H], U8, "wk_q")
        wk_s = held([P, H], U8, "wk_s")

        def order_wk():
            nc.scalar.copy(
                out=wk_q[:].bitcast(U32).rearrange("p (g t w m) -> p g w t m", g=2, t=PACK, m=4),
                in_=wk_raw[:].bitcast(U32).rearrange("p (g w m t) -> p g w t m", g=2, t=PACK, m=4),
            )
            nc.scalar.copy(
                out=wk_s[:].bitcast(U16).rearrange("p (g t w m) -> p g w t m", g=2, t=PACK, m=8),
                in_=wks_raw[:].bitcast(U16).rearrange("p (g w m t) -> p g w t m", g=2, t=PACK, m=8),
            )

        def copy_on(engine, dst, src):
            if engine == "vector":
                nc.vector.tensor_copy(out=dst, in_=src)
            else:
                nc.scalar.copy(out=dst, in_=src)

        picked0 = keep.tile([P, PACK, S], F32, name="picked0", tag="picked0", align_bytes=64)
        picked1_flat = held([P, PACK * S + HALF], F32, "picked1")
        picked = [picked0[:], picked1_flat[:, 0 : PACK * S].rearrange("p (i j) -> p i j", i=PACK)]
        last_pair = picked1_flat[:, 2 * S :].rearrange("p (i j) -> p i j", i=2)

        def picks(a, i0, i1, lo, hi):
            if a == 1 and i1 == PACK and lo >= HALF:
                return last_pair[:, i0 - 2 : i1 - 2, lo:hi]
            return picked[a][:, i0:i1, lo:hi]

        x_bf = {}
        x_q = [held([P, S], U32, "x_q0"), late.tile([P, S], U32, name="x_q1", tag="late", align_bytes=64)]
        after_carry = held([P, 2, HALF], U8, "after_carry", "t_s_rows")
        x_s_first = held([P, HALF], U8, "x_s0")
        x_s_last = late.tile([P, S], U8, name="x_s1", tag="late", align_bytes=64)

        def x_s(a, lo, hi):
            if a == 1:
                return x_s_last[:, lo:hi]
            return x_s_first[:, lo:hi] if lo < HALF else after_carry[:, 0, lo - HALF : hi - HALF]

        def gather_x(a, i, lo, hi):
            window = planes[a, i][:].indirect(offs2_t[:, lo // PER_COLUMN : hi // PER_COLUMN])
            nc.vector.tensor_tensor(picks(a, i, i + 1, lo, hi)[:, 0], window, wgt_all[:, lo:hi], MULT)

        def woven(a):
            if a not in x_bf:
                x_bf[a] = keep.tile([P, S * PACK], BF16, name="x_bf", tag=("x_bf0", "wx00")[a], align_bytes=64)
            return x_bf[a]

        def weave_x(a, lo, hi, i0, i1, engine):
            copy_on(
                engine,
                woven(a)[:, lo * PACK : hi * PACK].rearrange("p (w z i) -> p w i z", z=2, i=PACK)[:, :, i0:i1],
                picks(a, i0, i1, lo, hi).rearrange("p i (w z) -> p w i z", z=2),
            )

        def quant_x(a, lo, hi):
            nc.vector.quantize_mx(out=x_q[a][:, lo:hi].bitcast(E4M3), scales=x_s(a, lo, hi), in_=x_bf[a][:, lo * PACK : hi * PACK])

        w_bf, w_q, w_s = {}, {}, {}

        def weave_wx(g, a, t0, t1, engine):
            width = (t1 - t0) * P * PACK
            if (g, a, t1) == (1, 1, PACK):
                w_bf[g, a, t0] = keep.tile([P, width], BF16, name="w_bf_last", tag="wo_bf", align_bytes=64)
            else:
                w_bf[g, a, t0] = ring.tile([P, width], BF16, name="w_bf", tag="wbf", align_bytes=64, bufs=WOVEN_BUFS)
            copy_on(
                engine,
                w_bf[g, a, t0][:].rearrange("p (t m e i) -> p m t i e", t=t1 - t0, e=2, i=PACK),
                wx_raw[g, a][:].rearrange("p i (m t e) -> p m t i e", t=PACK, e=2)[:, :, t0:t1],
            )

        wx01_bf = picked1_flat[:, PACK * S - HALF :].bitcast(BF16)
        for t in range(PACK):
            w_bf[0, 1, t] = wx01_bf[:, t * P * PACK : (t + 1) * P * PACK]

        def weave_wx01(part, t0, t1):
            m = P // 4
            nc.scalar.copy(
                out=wx01_bf.rearrange("p (t m e i) -> p m t i e", t=PACK, e=2, i=PACK)[:, part * m : (part + 1) * m, t0:t1],
                in_=wx01_raw[part][:].rearrange("p i (m t e) -> p m t i e", t=PACK, e=2)[:, :, t0:t1],
            )

        def quant_wx(g, a, t0, t1):
            width = (t1 - t0) * P
            if (g, a, t1) == (1, 1, PACK):
                codes = late.tile([P, width], U32, name="w_q_late", tag="late", align_bytes=64)
                scales = late.tile([P, width], U8, name="w_s_late", tag="late", align_bytes=64)[:]
            else:
                codes = held([P, width], U32, "w_q%d%d%d" % (g, a, t0))
                scales = after_carry[:, 1, t0 * P : t1 * P] if (g, a) == (0, 0) else held([P, width], U8, "w_s%d%d%d" % (g, a, t0))[:]
            for t in range(t0, t1):
                w_q[g, a, t] = codes[:, (t - t0) * P : (t - t0 + 1) * P]
                w_s[g, a, t] = scales[:, (t - t0) * P : (t - t0 + 1) * P]
            nc.vector.quantize_mx(out=codes[:].bitcast(E4M3), scales=scales, in_=w_bf[g, a, t0][:])

        t_q = held([P, S], U32, "t_q")

        banks, expd = {}, {}

        def exp_tile(g, half):
            if (g, half) not in expd:
                tag = (("x_bf0", "expd01"), ("picked0", "tabw"))[g][half]
                expd[g, half] = keep.tile([P, PACK, HALF], F32, name="expd", tag=tag, align_bytes=64)
            return expd[g, half]

        def quarter_bank(q, u):
            if ("quarter", q, u) not in banks:
                banks["quarter", q, u] = psum.tile([P, 2, QUART], F32, name="bank", tag="bank%d" % (2 * q + u))
            return banks["quarter", q, u]

        def quarter_tab(q, u):
            cols = slice(q * QUART, (q + 1) * QUART)
            for s in range(2):
                c0 = (2 * u + s) * P
                nc.tensor.matmul_mx(
                    out=quarter_bank(q, u)[:, s, :],
                    lhsT=wk_q[:, 2 * c0 : 2 * (c0 + P)].bitcast(E2M1),
                    lhsT_scale=wk_s[:, c0 : c0 + P],
                    rhs=t_q[:, cols].bitcast(E4M3),
                    rhs_scale=t_s[:, cols],
                    start=u == 0 and s == 0,
                    stop=False,
                )

        def quarter_x(q, u, a):
            cols = slice(q * QUART, (q + 1) * QUART)
            for s in range(2):
                nc.tensor.matmul_mx(
                    out=quarter_bank(q, u)[:, s, :],
                    lhsT=w_q[0, a, 2 * u + s].bitcast(E4M3),
                    lhsT_scale=w_s[0, a, 2 * u + s],
                    rhs=x_q[a][:, cols].bitcast(E4M3),
                    rhs_scale=x_s(a, cols.start, cols.stop),
                    start=u == 1 and a == 0 and s == 0,
                    stop=a == 1 and s == 1,
                )

        def quarter_exp(q, u):
            half, lo = divmod(q * QUART, HALF)
            nc.scalar.activation(exp_tile(0, half)[:, 2 * u : 2 * u + 2, lo : lo + QUART], quarter_bank(q, u)[:], ACT.Exp)

        def half_bank(g, half, t):
            if ("half", g, half, t) not in banks:
                banks["half", g, half, t] = psum.tile([P, HALF], F32, name="bank", tag="bank%d" % (PACK * half + t))
            return banks["half", g, half, t][:]

        def half_tab(g, half, t, first):
            c0 = g * KP + t * P
            cols = slice(half * HALF, (half + 1) * HALF)
            nc.tensor.matmul_mx(
                out=half_bank(g, half, t),
                lhsT=wk_q[:, 2 * c0 : 2 * (c0 + P)].bitcast(E2M1),
                lhsT_scale=wk_s[:, c0 : c0 + P],
                rhs=t_q[:, cols].bitcast(E4M3),
                rhs_scale=t_s[:, cols],
                start=first,
                stop=False,
            )

        def half_x(g, half, t, a, first):
            cols = slice(half * HALF, (half + 1) * HALF)
            nc.tensor.matmul_mx(
                out=half_bank(g, half, t),
                lhsT=w_q[g, a, t].bitcast(E4M3),
                lhsT_scale=w_s[g, a, t],
                rhs=x_q[a][:, cols].bitcast(E4M3),
                rhs_scale=x_s(a, cols.start, cols.stop),
                start=first,
                stop=a == 1,
            )

        def half_exp(g, half, t):
            nc.scalar.activation(exp_tile(g, half)[:, t, :], half_bank(g, half, t), ACT.Exp)

        wo_q = held([P, 2 * N], U32, "wo_q")
        wo_s = held([P, 2 * N], U8, "wo_s")
        sel_c = held([P, 2, REPEAT, PACK], F32, "sel_c")

        def quant_wo():
            wo_bf = keep.tile([P, 2, N * PACK], BF16, name="wo_bf", tag="wo_bf", align_bytes=64)
            for g in range(2):
                nc.vector.tensor_copy(
                    out=wo_bf[:, g, :].rearrange("p (w z t) -> p w t z", z=2, t=PACK),
                    in_=wo_raw[g][:].rearrange("p t (w z) -> p w t z", z=2),
                )
            nc.vector.quantize_mx(out=wo_q[:].bitcast(E4M3), scales=wo_s[:], in_=wo_bf[:].rearrange("p g w -> p (g w)"))

        def turn_sel():
            nc.vector.tensor_copy(out=sel_c[:], in_=sel_t[:, :, 0:7:2].unsqueeze(2).to_broadcast([P, 2, REPEAT, PACK]))
            once = psum.tile([P, P], F32, name="sel_once", tag="bank3")
            nc.tensor.transpose(once[:], sel_c[:].rearrange("p g j t -> p (g j t)"), ident[:])
            nc.vector.tensor_copy(out=sel_part[:], in_=once[:])
            twice = psum.tile([P, P], F32, name="sel_p", tag="bank7")
            nc.tensor.transpose(twice[:], sel_part[:], ident[:])
            return twice[:].rearrange("p (g j t) -> p g j t", g=2, t=PACK)

        out_rows = out.rearrange("(y p) j -> p y j", y=2)
        steps = [(sum(STEP_WIDTHS[:n]), width) for n, width in enumerate(STEP_WIDTHS)]
        last = len(steps) - 1
        stores = [(sum(STORE_WIDTHS[:k]), width) for k, width in enumerate(STORE_WIDTHS)]
        h_all = [held([P, (S - g * sum(POOL_SHARES)) * PACK], BF16, "h_all%d" % g) for g in range(2)]
        logs, h_q, h_s, acc = {}, {}, {}, {}

        def h_bf(n, g):
            start = (sum(STEP_WIDTHS[n + 1 :]) - g * sum(POOL_SHARES[n + 1 :])) * PACK
            return h_all[g][:, start : start + STEP_WIDTHS[n] * PACK]

        def take_log(n, g, lo, hi):
            half, j = divmod(steps[n][0] + lo, HALF)
            logs[n, g, lo] = late.tile([P, 2, hi - lo, 2], F32, name="logs", tag="late", align_bytes=64)
            nc.scalar.activation(
                logs[n, g, lo][:],
                expd[g, half][:, :, j : j + hi - lo].rearrange("p (u s) j -> p u j s", u=2),
                ACT.Ln,
                bias=1.0,
            )

        def times_sel(n, g, lo, hi):
            split = min(hi, max(lo, STEP_WIDTHS[n] - POOL_SHARES[n])) if g == 1 else hi
            first = g == 0 and lo == 0
            own = sel_p if POOL_SHARES[n - 1 if (first or n == last) and n > 0 else n] > 0 else sel_c
            for engine, factors, q0, q1 in ((nc.gpsimd, sel_c, split, hi), (nc.vector, own, lo, split)):
                if q1 > q0:
                    engine.tensor_tensor(
                        h_bf(n, g)[:, q0 * PACK : q1 * PACK].rearrange("p (b j u s) -> p b j u s", j=REPEAT, u=2, s=2),
                        logs[n, g, lo][:, :, q0 - lo : q1 - lo].rearrange("p u (b j) s -> p b j u s", j=REPEAT),
                        factors[:, g].rearrange("p j (u s) -> p j u s", u=2).unsqueeze(1).to_broadcast([P, (q1 - q0) // REPEAT, REPEAT, 2, 2]),
                        MULT,
                    )

        def mm_out(n, g, first):
            j0, width = steps[n]
            k, (s0, span) = [(k, store) for k, store in enumerate(stores) if store[0] <= j0][-1]
            if k not in acc:
                if n == last:
                    acc[k] = [psum.tile([P, span], F32, name="acc", tag="bank%d" % (5 + y))[:] for y in range(2)]
                else:
                    both = psum.tile([P, 2, span], F32, name="acc", tag="bank%d" % k)
                    acc[k] = [both[:, y, :] for y in range(2)]
            for y in range(2):
                cols = slice(g * N + y * P, g * N + (y + 1) * P)
                nc.tensor.matmul_mx(
                    out=acc[k][y][:, j0 - s0 : j0 - s0 + width],
                    lhsT=wo_q[:, cols].bitcast(E4M3),
                    lhsT_scale=wo_s[:, cols],
                    rhs=h_q[n][:, g].bitcast(E4M3),
                    rhs_scale=h_s[n][:, g],
                    start=j0 == s0 and first and (y == 0 or n == last),
                    stop=j0 + width == s0 + span and not first and (y == 1 or n == last),
                )

        def quant_and_multiply(n, order):
            h_q[n] = ring.tile([P, 2, STEP_WIDTHS[n]], U32, name="h_q", align_bytes=64, bufs=CODE_BUFS)
            h_s[n] = ring.tile([P, 2, STEP_WIDTHS[n]], U8, name="h_s", align_bytes=64, bufs=CODE_BUFS)
            for g in order:
                nc.vector.quantize_mx(out=h_q[n][:, g].bitcast(E4M3), scales=h_s[n][:, g], in_=h_bf(n, g))
            for g in order:
                mm_out(n, g, g == order[0])

        def store(n):
            j0, width = stores[n]
            res = ring.tile([P, 2, width], F32, name="res", tag="wbf", align_bytes=64, bufs=WOVEN_BUFS)
            for y in range(2):
                if (n, y) in VECTOR_BIASES:
                    nc.vector.tensor_scalar_add(res[:, y, :], acc[n][y], bo_t[:, y : y + 1])
                else:
                    nc.scalar.activation(res[:, y, :], acc[n][y], ACT.Identity, bias=bo_t[:, y : y + 1])
                if j0 + width == S:
                    (nc.sync, nc.scalar)[y].dma_start(out=out_rows[:, y, j0 : j0 + width], in_=res[:, y, :])
            if j0 + width < S:
                nc.sync.dma_start(out=out_rows[:, :, j0 : j0 + width], in_=res[:])

        def spread_wgt():
            turned = [held([P, PACK, 16, 8], F32, "wgt_turned", tag) for tag in ("picked0", "wk_q")]
            by_query = psum.tile([P, P], F32, name="by_query", tag="bank0")
            nc.tensor.transpose(by_query[:], wgt_part[:], ident[:])
            runs = by_query[:].rearrange("p (x c g) -> p c g x", x=2, g=GROUPS)
            for half in range(2):
                nc.scalar.copy(
                    out=turned[half][:].rearrange("p c (g x) k -> p c g x k", x=2),
                    in_=runs[:, 4 * half : 4 * half + 4].unsqueeze(4).to_broadcast([P, 4, GROUPS, 2, 8]),
                )
            for half in range(2):
                spread = psum.tile([P, PACK, P], F32, name="spread", tag="bank%d" % (2 + half))
                for b in range(PACK):
                    nc.tensor.transpose(spread[:, b, :], turned[half][:, b].rearrange("p r k -> p (r k)"), ident[:])
                nc.scalar.copy(
                    out=wgt_all[:, half * HALF : (half + 1) * HALF], in_=spread[:].rearrange("p b j -> p (b j)")
                )

        spread_wgt()
        nc.vector.tensor_copy(t_q[:], tabw[:].indirect(offs_t[:]))
        for i in range(PACK):
            gather_x(0, i, 0, S)
            if i == 1:
                weave_x(0, 0, S, 0, 2, "scalar")
        weave_x(0, 0, HALF + P, 2, PACK, "scalar")
        weave_x(0, HALF + P, S, 2, PACK, "scalar")
        gather_x(1, 0, 0, S)
        quant_x(0, 0, HALF)
        order_wk()
        gather_x(1, 1, 0, S)
        quant_x(0, HALF, S)
        for u in range(2):
            weave_wx(0, 0, 2 * u, 2 * u + 2, "scalar")
        weave_x(1, 0, S, 0, 2, "scalar")
        quant_wx(0, 0, 0, 2)
        gather_x(1, 2, 0, S)
        quant_wx(0, 0, 2, PACK)
        for t in range(2):
            half_tab(0, 0, t, True)
        for q in (2, 3):
            quarter_tab(q, 0)
        for u in range(2):
            for t in (2 * u, 2 * u + 1):
                half_x(0, 0, t, 0, u == 1)
            for q in (2, 3):
                quarter_x(q, u, 0)
        for t in (2, 3):
            half_tab(0, 0, t, False)
        for q in (2, 3):
            quarter_tab(q, 1)

        def finish_x(q):
            gather_x(1, PACK - 1, q * QUART, (q + 1) * QUART)
            weave_x(1, q * QUART, (q + 1) * QUART, 2, PACK, "vector")
            quant_x(1, q * QUART, (q + 1) * QUART)

        def close(q, u):
            quarter_x(q, u, 1)
            quarter_exp(q, u)

        weave_wx01(0, 0, PACK)
        for q in range(2):
            finish_x(q)
        for t in range(PACK):
            weave_wx01(1, t, t + 1)
        for t in range(PACK):
            quant_wx(0, 1, t, t + 1)
            half_x(0, 0, t, 1, False)
            half_exp(0, 0, t)
        for q in (2, 3):
            finish_x(q)
            for u in range(2):
                close(q, u)

        for t in range(PACK):
            half_tab(1, 0, t, True)
        for t in range(PACK):
            for a in range(2):
                weave_wx(1, a, t, t + 1, "vector")
            for a in range(2):
                quant_wx(1, a, t, t + 1)
            for half in range(2):
                if half == 1:
                    half_tab(1, half, t, True)
                for a in range(2):
                    half_x(1, half, t, a, False)
                half_exp(1, half, t)
        quant_wo()
        sel_p = turn_sel()

        units = [(0, 0, 0, LEAD), (0, 0, LEAD, UNIT), (0, 1, 0, UNIT)]
        for n in range(1, last + 1):
            width = STEP_WIDTHS[n]
            if width == UNIT:
                units += [(n, 0, 0, width), (n, 1, 0, width)]
            else:
                rest = width - POOL_SHARES[n]
                units += [(n, 0, 0, UNIT), (n, 1, rest, width), (n, 0, UNIT, width), (n, 1, 0, rest)]
        ahead = 2
        for unit in units[:ahead]:
            take_log(*unit)
        for k, unit in enumerate(units):
            for later in units[k + ahead : k + ahead + 1]:
                take_log(*later)
            n, g, lo, hi = unit
            times_sel(*unit)
            if n > 0 and lo == 0 and g == (1 if n == last else 0):
                quant_and_multiply(n - 1, (1, 0))
            if g == 0 and lo == UNIT and n - 1 < EARLY_STORES and n > 0:
                store(n - 1)
        quant_and_multiply(last, (0, 1))
        for n in range(EARLY_STORES, len(stores)):
            store(n)
